import numpy as np
import ml_dtypes


def mxq(x, axis, fmt="e4m3"):
    dtype, down = {"e4m3": (ml_dtypes.float8_e4m3fn, 7), "e5m2": (ml_dtypes.float8_e5m2, 14)}[fmt]
    v = np.moveaxis(np.asarray(x, np.float32).astype(ml_dtypes.bfloat16).astype(np.float64), axis, -1)
    blocks = v.reshape(v.shape[:-1] + (-1, 32))
    amax = np.abs(blocks).max(-1, keepdims=True)
    byte = np.maximum(np.where(amax > 0, np.frexp(amax)[1] - 1 + 127, 0) - down, 1)
    scale = np.exp2(byte - 127.0)
    codes = (blocks / scale).astype(np.float32).astype(dtype).astype(np.float64)
    return np.moveaxis((codes * scale).reshape(v.shape), -1, axis)


WIDE = False


def mx_kscale(k):
    if not WIDE:
        return np.ones(k)
    levels = np.array([10, -10, 5, -5, 0])
    if k % 512:
        return np.exp2(np.random.permutation(np.resize(levels, k // 32))).repeat(32)
    a = np.empty((k // 512, 16))
    for p in range(k // 512):
        a[p, :8] = np.random.permutation(np.resize(levels, 8))
        for g in range(8):
            far = levels[np.abs(levels - a[p, g]) >= 10]
            a[p, g + 8] = far[np.random.randint(len(far))]
    return np.exp2(a.ravel()).repeat(32)


def f64(x):
    return np.asarray(x).astype(np.float64)


def striped(idx):
    return np.tile(idx.reshape(-1, 16).T, (8, 1)).astype(np.uint16)


def unstriped(offs):
    return offs[:16].T.reshape(-1).astype(np.int64)


E2M1 = np.array([0.0, 0.5, 1.0, 1.5, 2.0, 3.0, 4.0, 6.0, -0.0, -0.5, -1.0, -1.5, -2.0, -3.0, -4.0, -6.0])


def pack_weight(w, fmt):
    k, n = w.shape
    w = f64(np.asarray(w, np.float32).astype(ml_dtypes.bfloat16)).reshape(k // 32, 32, n)
    amax = np.abs(w).max(1)
    if fmt == "e4m3":
        byte = np.frexp(amax)[1] - 1 + 127 - 7
    else:
        mant, ex = np.frexp(amax / 6.0)
        byte = np.where(mant > 0.5, ex, ex - 1) + 127
    byte = np.clip(np.where(amax > 0, byte, 1), 1, 254)
    scaled = (w * np.exp2(127.0 - byte)[:, None, :]).reshape(k, n).astype(np.float32)
    by_word = np.ascontiguousarray(scaled.reshape(k // 512, 128, 4, n).transpose(0, 1, 3, 2))
    if fmt == "e4m3":
        words = by_word.astype(ml_dtypes.float8_e4m3fn).view(np.uint8)
    else:
        c = by_word.astype(ml_dtypes.float4_e2m1fn).view(np.uint8) & 0xF
        words = (c[..., 0::2] | (c[..., 1::2] << 4)).reshape(k // 512, 128, 2 * n)
    return np.ascontiguousarray(words), np.ascontiguousarray(byte.astype(np.uint8).reshape(k // 512, 16, n))


def unpack_weight(words, scales, fmt):
    g, _, n = scales.shape
    words = np.ascontiguousarray(words).reshape(g, 128, n, -1)
    if fmt == "e4m3":
        vals = words.view(ml_dtypes.float8_e4m3fn).astype(np.float64)
    else:
        nib = np.empty((g, 128, n, 4), np.uint8)
        nib[..., 0::2] = words & 0xF
        nib[..., 1::2] = words >> 4
        vals = E2M1[nib]
    vals = vals * np.repeat(np.exp2(scales.astype(np.float64) - 127.0), 8, axis=1)[..., None]
    return vals.transpose(0, 1, 3, 2).reshape(g * 512, n)


def gelu(v):
    return 0.5 * v * (1.0 + np.tanh(np.sqrt(2.0 / np.pi) * (v + 0.044715 * v**3)))


K, T, S, H, T2, P, N = 1536, 2048, 1024, 512, 2048, 1024, 1536

def setup_inputs():
    n = np.random.standard_normal
    s = mx_kscale(K)[:, None]
    u = mx_kscale(H)[:, None]
    tab_words, tab_scales = pack_weight(n((K, T)) * s, "e4m3")
    w1_words, w1_scales = pack_weight(1.5 * n((K, H)) / np.sqrt(K) / s, "e2m1")
    w3_words, w3_scales = pack_weight(n((H, N)) / np.sqrt(H) / u, "e4m3")
    return {
        "tab_words": tab_words, "tab_scales": tab_scales,
        "offs": striped(np.random.permutation(T)[:S]),
        "w1_words": w1_words, "w1_scales": w1_scales,
        "w2": (1.5 * n((K, H)) / np.sqrt(K) / s).astype(np.float32),
        "b2": (0.5 * n(H)).astype(np.float32),
        "wgs": np.exp(0.3 * n((128, S))).astype(np.float32),
        "offs2": striped(np.random.permutation(T2)[:S]),
        "offs3": striped(np.random.permutation(T2)[:P]),
        "skip": (n((H, P)) * u).astype(np.float32),
        "w3_words": w3_words, "w3_scales": w3_scales,
    }

def reference(tab_words, tab_scales, offs, w1_words, w1_scales, w2, b2, wgs, offs2, offs3, skip, w3_words, w3_scales):
    v = unpack_weight(tab_words, tab_scales, "e4m3")[:, unstriped(offs)]
    w1 = unpack_weight(w1_words, w1_scales, "e2m1")
    a = w1.T @ v
    b = (mxq(f64(w2), 0, "e4m3").T @ v) + f64(b2)[:, None]
    h = a + 0.5 * b * (1 + np.tanh(np.sqrt(2 / np.pi) * (b + 0.044715 * b ** 3)))
    page = np.zeros((H, T2))
    page[:, unstriped(offs2)] = np.tile(f64(wgs), (H // 128, 1)) * h
    x = page[:, unstriped(offs3)]
    z = f64(skip) / (1 + np.exp(-x))
    w3 = unpack_weight(w3_words, w3_scales, "e4m3")
    return w3.T @ mxq(z, 0, "e4m3")

@@ -1,0 +1,259 @@
+from contextlib import ExitStack
+
+import concourse.mybir as mybir
+
+K, T, S, H, T2, M_OUT, N_OUT = 1536, 2048, 1024, 512, 2048, 1024, 1536
+FLOPS = 2 * (2 * K * H * S + H * N_OUT * M_OUT)
+
+F32 = mybir.dt.float32
+BF16 = mybir.dt.bfloat16
+I32 = mybir.dt.int32
+U32 = mybir.dt.uint32
+U16 = mybir.dt.uint16
+U8 = mybir.dt.uint8
+FP8X4 = mybir.dt.float8_e4m3fn_x4
+FP4X4 = mybir.dt.float4_e2m1fn_x4
+ACT = mybir.ActivationFunctionType
+ALU = mybir.AluOpType
+
+P = 128
+PACK = 4
+PASSES = K // (P * PACK)
+QUADS = 4
+BANK = 512
+HALVES = S // BANK
+CHUNK = 256
+CHUNKS = M_OUT // CHUNK
+BLOCKS = N_OUT // P
+PER_BANK = BANK // CHUNK
+PER_STORE = 4
+
+
+def tile_list_pipeline_stage_transfer_kernel(
+    tc, tab_words, tab_scales, offs, w1_words, w1_scales, w2, b2, wgs, offs2, offs3, skip, w3_words, w3_scales, out
+):
+    nc = tc.nc
+    with ExitStack() as ctx:
+        lists = ctx.enter_context(tc.tile_pool(name="lists", bufs=1))
+        keep = ctx.enter_context(tc.tile_pool(name="keep", bufs=1))
+        ring = ctx.enter_context(tc.tile_pool(name="ring", bufs=3))
+        stage = ctx.enter_context(tc.tile_pool(name="stage", bufs=6))
+        psum = ctx.enter_context(tc.psum_pool(name="psum", bufs=1))
+
+        idx = lists.tile([P, S // 16], U16, name="idx")
+        idx2 = lists.tile([P, S // 16], U16, name="idx2")
+        idx3 = lists.tile([P, M_OUT // 16], U16, name="idx3")
+
+        tab = [keep.tile([P, T], U32, name="tab%d" % a, align_bytes=64) for a in range(PASSES)]
+        tab_s = keep.tile([P, T], U8, name="tab_s", align_bytes=64)
+        v = [keep.tile([P, S], U32, name="v%d" % a, align_bytes=64) for a in range(PASSES)]
+        v_s = [keep.tile([P, S], U8, name="v_s%d" % a, align_bytes=64) for a in range(PASSES)]
+        w1_raw = keep.tile([P, PASSES, 2 * H], U8, name="w1_raw", align_bytes=64)
+        w1_raw_s = keep.tile([P, PASSES, H], U8, name="w1_raw_s", align_bytes=64)
+        w1c = keep.tile([P, PASSES, 2 * H], U8, name="w1c", align_bytes=64)
+        w1s = keep.tile([P, PASSES, H], U8, name="w1s", align_bytes=64)
+        w2_raw = [keep.tile([P, PACK, H], F32, name="w2_raw%d" % a, align_bytes=64) for a in range(PASSES)]
+        w2_bf_first = keep.tile([P, H * PACK], BF16, name="w2_bf_first", align_bytes=64)
+        w2_bf_rest = keep.tile([P, PASSES - 1, H * PACK], BF16, name="w2_bf_rest", align_bytes=64)
+        w2_bf = [w2_bf_first[:]] + [w2_bf_rest[:, a - 1, :] for a in range(1, PASSES)]
+        w2c = [keep.tile([P, H], U32, name="w2c%d" % a, align_bytes=64) for a in range(PASSES)]
+        w2s = [keep.tile([P, H], U8, name="w2s%d" % a, align_bytes=64) for a in range(PASSES)]
+        bias = keep.tile([P, PACK], F32, name="bias", align_bytes=64)
+        wg_first = keep.tile([P, S], F32, name="wg_first", align_bytes=64)
+        wg_rest = keep.tile([P, PACK - 1, S], F32, name="wg_rest", tag="late", align_bytes=64)
+        pages = [keep.tile([P, T2], F32, name="page%d" % t, align_bytes=64) for t in range(2)]
+        skip_sb = keep.tile([P, PACK, M_OUT], F32, name="skip_sb", align_bytes=64)
+        w3c = keep.tile([P, N_OUT], U32, name="w3c", align_bytes=64)
+        w3s = keep.tile([P, N_OUT], U8, name="w3s", align_bytes=64)
+
+        nc.vector.memset(tab_s[:].bitcast(I32), 0)
+        nc.vector.memset(w1_raw_s[:].bitcast(I32), 0)
+        for a in range(1, PASSES):
+            nc.vector.memset(v_s[a][:].bitcast(I32), 0)
+
+        def load_tab(a):
+            nc.sync.dma_start(out=tab[a][:].bitcast(I32), in_=tab_words[a].rearrange("p t i -> p (t i)").bitcast(I32))
+
+        def load_w2(a):
+            rows = w2[a * P * PACK : (a + 1) * P * PACK, :]
+            nc.sync.dma_start(out=w2_raw[a][:], in_=rows.rearrange("(p j) c -> p j c", j=PACK))
+
+        wgs_rows = wgs.rearrange("(m t) j -> m t j", t=PACK)
+
+        nc.sync.dma_start(idx[:], offs)
+        load_tab(0)
+        nc.sync.dma_start(out=w1_raw[:].bitcast(I32), in_=w1_words.rearrange("a p c -> p a c").bitcast(I32))
+        for q in range(QUADS):
+            nc.sync.dma_start(
+                out=tab_s[32 * q : 32 * q + 4 * PASSES, :].bitcast(I32),
+                in_=tab_scales[:, 4 * q : 4 * q + 4, :].bitcast(I32),
+            )
+        load_w2(0)
+        load_w2(1)
+        for q in range(QUADS):
+            nc.sync.dma_start(
+                out=w1_raw_s[32 * q : 32 * q + 4, :, :].bitcast(I32),
+                in_=w1_scales[:, 4 * q : 4 * q + 4, :].rearrange("a r c -> r a c").bitcast(I32),
+            )
+        load_tab(1)
+        load_w2(2)
+        load_tab(2)
+        nc.sync.dma_start(out=bias[:], in_=b2.rearrange("(p t) -> p t", t=PACK))
+        for q in range(QUADS):
+            nc.sync.dma_start(out=wg_first[32 * q : 32 * q + 32, :], in_=wgs_rows[:, 0, :])
+        nc.sync.dma_start(idx2[:], offs2)
+        for q in range(QUADS):
+            nc.sync.dma_start(out=wg_rest[32 * q : 32 * q + 32, :, :], in_=wgs_rows[:, 1:PACK, :])
+        nc.sync.dma_start(idx3[:], offs3)
+        nc.sync.dma_start(out=skip_sb[:], in_=skip.rearrange("(p t) m -> p t m", t=PACK))
+        nc.vector.memset(w3s[:].bitcast(I32), 0)
+        nc.sync.dma_start(out=w3c[:].bitcast(I32), in_=w3_words[0].rearrange("p c i -> p (c i)").bitcast(I32))
+        for q in range(QUADS):
+            nc.sync.dma_start(
+                out=w3s[32 * q : 32 * q + 4, :].bitcast(I32), in_=w3_scales[0, 4 * q : 4 * q + 4, :].bitcast(I32)
+            )
+
+        def cast_w2(a):
+            nc.scalar.copy(
+                out=w2_bf[a].rearrange("p (t m j) -> p m t j", t=PACK, j=PACK),
+                in_=w2_raw[a][:].rearrange("p j (m t) -> p m t j", t=PACK),
+            )
+
+        def quantize_w2(a):
+            nc.vector.quantize_mx(out=w2c[a][:].bitcast(FP8X4), scales=w2s[a][:], in_=w2_bf[a])
+
+        def gather_words(a, lo, hi):
+            nc.vector.tensor_copy(out=v[a][:, lo:hi], in_=tab[a][:].indirect(idx[:, lo // 16 : hi // 16]))
+
+        for a in range(PASSES):
+            cast_w2(a)
+
+        nc.vector.tensor_copy(out=v_s[0][:], in_=tab_s[:].indirect(idx[:]))
+        for a in range(1, PASSES):
+            nc.gpsimd.dma_start(out=v_s[a][0:112, :].bitcast(I32), in_=v_s[0][4 * a : 4 * a + 112, :].bitcast(I32))
+        gather_words(0, 0, S)
+        nc.vector.tensor_copy(
+            out=w1c[:].bitcast(U16).rearrange("p a (t m) -> p a t m", t=PACK),
+            in_=w1_raw[:].bitcast(U16).rearrange("p a (m t) -> p a t m", t=PACK),
+        )
+        nc.vector.tensor_copy(
+            out=w1s[:].rearrange("p a (t m) -> p a t m", t=PACK),
+            in_=w1_raw_s[:].rearrange("p a (m t) -> p a t m", t=PACK),
+        )
+        quantize_w2(0)
+        gather_words(1, 0, S)
+        quantize_w2(1)
+        gather_words(2, 0, BANK)
+        quantize_w2(2)
+        gather_words(2, BANK, S)
+
+        for t in range(2):
+            nc.vector.memset(pages[t][:], 0.0)
+        for t, tenant in ((2, "w2_bf_rest"), (3, "tab2")):
+            page = keep.tile([P, T2], F32, name="page%d" % t, tag=tenant, align_bytes=64)
+            nc.gpsimd.memset(page[:], 0.0)
+            pages.append(page)
+
+        units = [(t, half) for t in range(PACK) for half in range(HALVES)]
+        h_of = {}
+
+        def make_h(t, half):
+            cols = slice(half * BANK, (half + 1) * BANK)
+            rows = slice(t * P, (t + 1) * P)
+            acc_b = psum.tile([P, BANK], F32, name="acc_b", tag="bank%d" % (2 * half))
+            acc_a = psum.tile([P, BANK], F32, name="acc_a", tag="bank%d" % (2 * half + 1))
+            for a in range(PASSES):
+                nc.tensor.matmul_mx(
+                    out=acc_b[:],
+                    lhsT=w2c[a][:, rows].bitcast(FP8X4),
+                    lhsT_scale=w2s[a][:, rows],
+                    rhs=v[a][:, cols].bitcast(FP8X4),
+                    rhs_scale=v_s[a][:, cols],
+                    start=(a == 0),
+                    stop=(a == PASSES - 1),
+                )
+                nc.tensor.matmul_mx(
+                    out=acc_a[:],
+                    lhsT=w1c[:, a, 2 * t * P : 2 * (t + 1) * P].bitcast(FP4X4),
+                    lhsT_scale=w1s[:, a, rows],
+                    rhs=v[a][:, cols].bitcast(FP8X4),
+                    rhs_scale=v_s[a][:, cols],
+                    start=(a == 0),
+                    stop=(a == PASSES - 1),
+                )
+            gel = ring.tile([P, BANK], F32, name="gel")
+            nc.scalar.activation(out=gel[:], in_=acc_b[:], func=ACT.Gelu_apprx_tanh, bias=bias[:, t : t + 1])
+            h = ring.tile([P, BANK], F32, name="h")
+            nc.vector.tensor_tensor(out=h[:], in0=acc_a[:], in1=gel[:], op=ALU.add)
+            h_of[(t, half)] = h
+
+        def place_h(t, half):
+            cols = slice(half * BANK, (half + 1) * BANK)
+            weight = wg_first[:, cols] if t == 0 else wg_rest[:, t - 1, cols]
+            slots = idx2[:, half * BANK // 16 : (half + 1) * BANK // 16]
+            nc.vector.tensor_tensor(out=pages[t][:].indirect(slots), in0=h_of[(t, half)][:], in1=weight, op=ALU.mult)
+
+        make_h(*units[0])
+        for u in range(len(units)):
+            if u + 1 < len(units):
+                make_h(*units[u + 1])
+            place_h(*units[u])
+
+        span = PACK * CHUNK
+        work = keep.tile([P, CHUNKS * span + CHUNK + span], F32, name="work", tag="late", align_bytes=64)
+        out_rows = out.rearrange("(b p) m -> p b m", p=P)
+
+        def x_of(c):
+            return work[:, c * span : (c + 1) * span]
+
+        def gate_of(c):
+            return work[:, (c + 1) * span + CHUNK : (c + 2) * span + CHUNK]
+
+        def pick(c, t):
+            slots = idx3[:, c * CHUNK // 16 : (c + 1) * CHUNK // 16]
+            nc.vector.tensor_copy(out=x_of(c)[:, t * CHUNK : (t + 1) * CHUNK], in_=pages[t][:].indirect(slots))
+            if t % 2 == 1:
+                pair = slice((t - 1) * CHUNK, (t + 1) * CHUNK)
+                nc.scalar.activation(out=gate_of(c)[:, pair], in_=x_of(c)[:, pair], func=ACT.Sigmoid)
+
+        for t in range(PACK):
+            pick(0, t)
+        for c in range(CHUNKS):
+            cols = slice(c * CHUNK, (c + 1) * CHUNK)
+            if c + 1 < CHUNKS:
+                pick(c + 1, 0)
+            z = ring.tile([P, span], BF16, name="z", align_bytes=64)
+            nc.vector.tensor_tensor(
+                out=z[:].rearrange("p (n i t) -> p n t i", i=2, t=PACK),
+                in0=gate_of(c).rearrange("p (t n i) -> p n t i", t=PACK, i=2),
+                in1=skip_sb[:, :, cols].rearrange("p t (n i) -> p n t i", i=2),
+                op=ALU.mult,
+            )
+            zc = ring.tile([P, CHUNK], U32, name="zc", align_bytes=64)
+            zs = ring.tile([P, CHUNK], U8, name="zs", align_bytes=64)
+            nc.vector.quantize_mx(out=zc[:].bitcast(FP8X4), scales=zs[:], in_=z[:])
+            if c + 1 < CHUNKS:
+                for t in range(1, PACK):
+                    pick(c + 1, t)
+            for s in range(BLOCKS // PER_STORE):
+                staged = stage.tile([P, PER_STORE, CHUNK], F32, name="staged")
+                for k in range(PER_STORE // PER_BANK):
+                    acc = psum.tile([P, PER_BANK, CHUNK], F32, name="acc", tag="bank%d" % ((4 + (c * BLOCKS + s * PER_STORE) // PER_BANK + k) % 8))
+                    for e in range(PER_BANK):
+                        b = s * PER_STORE + k * PER_BANK + e
+                        nc.tensor.matmul_mx(
+                            out=acc[:, e, :],
+                            lhsT=w3c[:, b * P : (b + 1) * P].bitcast(FP8X4),
+                            lhsT_scale=w3s[:, b * P : (b + 1) * P],
+                            rhs=zc[:].bitcast(FP8X4),
+                            rhs_scale=zs[:],
+                            start=True,
+                            stop=True,
+                        )
+                    target = staged[:, k * PER_BANK : (k + 1) * PER_BANK, :]
+                    on_vector = k == 1 and (c == CHUNKS - 1 or s == BLOCKS // PER_STORE - 1)
+                    if on_vector:
+                        nc.vector.tensor_copy(out=target, in_=acc[:])
+                    else:
+                        nc.scalar.copy(out=target, in_=acc[:])
+                nc.sync.dma_start(out=out_rows[:, s * PER_STORE : (s + 1) * PER_STORE, cols], in_=staged[:])

@@ -26,7 +26,7 @@ CHUNK = 256
 CHUNKS = M_OUT // CHUNK
 BLOCKS = N_OUT // P
 PER_BANK = BANK // CHUNK
-PER_STORE = 4
+BANKS_A_CHUNK = BLOCKS // PER_BANK
 
 
 def tile_list_pipeline_stage_transfer_kernel(
@@ -59,9 +59,9 @@ def tile_list_pipeline_stage_transfer_kernel(
         w2c = [keep.tile([P, H], U32, name="w2c%d" % a, align_bytes=64) for a in range(PASSES)]
         w2s = [keep.tile([P, H], U8, name="w2s%d" % a, align_bytes=64) for a in range(PASSES)]
         bias = keep.tile([P, PACK], F32, name="bias", align_bytes=64)
-        wg_first = keep.tile([P, S], F32, name="wg_first", align_bytes=64)
-        wg_rest = keep.tile([P, PACK - 1, S], F32, name="wg_rest", tag="late", align_bytes=64)
-        pages = [keep.tile([P, T2], F32, name="page%d" % t, align_bytes=64) for t in range(2)]
+        wg_first = keep.tile([P, 1, S], F32, name="wg_first", align_bytes=64)
+        wg_second = keep.tile([P, 1, S], F32, name="wg_second", align_bytes=64)
+        pages = [keep.tile([P, T2], F32, name="page%d" % t, align_bytes=64) for t in range(PACK - 1)]
         skip_sb = keep.tile([P, PACK, M_OUT], F32, name="skip_sb", align_bytes=64)
         w3c = keep.tile([P, N_OUT], U32, name="w3c", align_bytes=64)
         w3s = keep.tile([P, N_OUT], U8, name="w3s", align_bytes=64)
@@ -77,6 +77,9 @@ def tile_list_pipeline_stage_transfer_kernel(
         def load_w2(a):
             rows = w2[a * P * PACK : (a + 1) * P * PACK, :]
             nc.sync.dma_start(out=w2_raw[a][:], in_=rows.rearrange("(p j) c -> p j c", j=PACK))
+
+        def gather_words(a, lo, hi):
+            nc.vector.tensor_copy(out=v[a][:, lo:hi], in_=tab[a][:].indirect(idx[:, lo // 16 : hi // 16]))
 
         wgs_rows = wgs.rearrange("(m t) j -> m t j", t=PACK)
 
@@ -96,14 +99,19 @@ def tile_list_pipeline_stage_transfer_kernel(
                 in_=w1_scales[:, 4 * q : 4 * q + 4, :].rearrange("a r c -> r a c").bitcast(I32),
             )
         load_tab(1)
-        load_w2(2)
-        load_tab(2)
-        nc.sync.dma_start(out=bias[:], in_=b2.rearrange("(p t) -> p t", t=PACK))
-        for q in range(QUADS):
-            nc.sync.dma_start(out=wg_first[32 * q : 32 * q + 32, :], in_=wgs_rows[:, 0, :])
         nc.sync.dma_start(idx2[:], offs2)
-        for q in range(QUADS):
-            nc.sync.dma_start(out=wg_rest[32 * q : 32 * q + 32, :, :], in_=wgs_rows[:, 1:PACK, :])
+        load_w2(2)
+        gather_words(0, 0, S)
+        nc.vector.tensor_copy(out=v_s[0][:], in_=tab_s[:].indirect(idx[:]))
+        load_tab(2)
+        for a in range(1, PASSES):
+            nc.sync.dma_start(out=v_s[a][0:112, :].bitcast(I32), in_=v_s[0][4 * a : 4 * a + 112, :].bitcast(I32))
+        nc.sync.dma_start(out=bias[:], in_=b2.rearrange("(p t) -> p t", t=PACK))
+        wg_rest = keep.tile([P, 2, S], F32, name="wg_rest", tag="tab0", align_bytes=64)
+        wg = [wg_first[:, 0, :], wg_second[:, 0, :], wg_rest[:, 0, :], wg_rest[:, 1, :]]
+        for tile, lo, hi in ((wg_first, 0, 1), (wg_second, 1, 2), (wg_rest, 2, PACK)):
+            for q in (0, 2, 1, 3):
+                nc.sync.dma_start(out=tile[32 * q : 32 * q + 32, :, :], in_=wgs_rows[:, lo:hi, :])
         nc.sync.dma_start(idx3[:], offs3)
         nc.sync.dma_start(out=skip_sb[:], in_=skip.rearrange("(p t) m -> p t m", t=PACK))
         nc.vector.memset(w3s[:].bitcast(I32), 0)
@@ -122,16 +130,9 @@ def tile_list_pipeline_stage_transfer_kernel(
         def quantize_w2(a):
             nc.vector.quantize_mx(out=w2c[a][:].bitcast(FP8X4), scales=w2s[a][:], in_=w2_bf[a])
 
-        def gather_words(a, lo, hi):
-            nc.vector.tensor_copy(out=v[a][:, lo:hi], in_=tab[a][:].indirect(idx[:, lo // 16 : hi // 16]))
-
         for a in range(PASSES):
             cast_w2(a)
 
-        nc.vector.tensor_copy(out=v_s[0][:], in_=tab_s[:].indirect(idx[:]))
-        for a in range(1, PASSES):
-            nc.gpsimd.dma_start(out=v_s[a][0:112, :].bitcast(I32), in_=v_s[0][4 * a : 4 * a + 112, :].bitcast(I32))
-        gather_words(0, 0, S)
         nc.vector.tensor_copy(
             out=w1c[:].bitcast(U16).rearrange("p a (t m) -> p a t m", t=PACK),
             in_=w1_raw[:].bitcast(U16).rearrange("p a (m t) -> p a t m", t=PACK),
@@ -147,15 +148,10 @@ def tile_list_pipeline_stage_transfer_kernel(
         quantize_w2(2)
         gather_words(2, BANK, S)
 
-        for t in range(2):
+        for t in range(PACK - 1):
             nc.vector.memset(pages[t][:], 0.0)
-        for t, tenant in ((2, "w2_bf_rest"), (3, "tab2")):
-            page = keep.tile([P, T2], F32, name="page%d" % t, tag=tenant, align_bytes=64)
-            nc.gpsimd.memset(page[:], 0.0)
-            pages.append(page)
 
         units = [(t, half) for t in range(PACK) for half in range(HALVES)]
-        h_of = {}
 
         def make_h(t, half):
             cols = slice(half * BANK, (half + 1) * BANK)
@@ -168,7 +164,7 @@ def tile_list_pipeline_stage_transfer_kernel(
                     lhsT=w2c[a][:, rows].bitcast(FP8X4),
                     lhsT_scale=w2s[a][:, rows],
                     rhs=v[a][:, cols].bitcast(FP8X4),
-                    rhs_scale=v_s[a][:, cols],
+                    rhs_scale=v_s[0][4 * a : P, cols],
                     start=(a == 0),
                     stop=(a == PASSES - 1),
                 )
@@ -181,51 +177,61 @@ def tile_list_pipeline_stage_transfer_kernel(
                     start=(a == 0),
                     stop=(a == PASSES - 1),
                 )
-            gel = ring.tile([P, BANK], F32, name="gel")
-            nc.scalar.activation(out=gel[:], in_=acc_b[:], func=ACT.Gelu_apprx_tanh, bias=bias[:, t : t + 1])
-            h = ring.tile([P, BANK], F32, name="h")
-            nc.vector.tensor_tensor(out=h[:], in0=acc_a[:], in1=gel[:], op=ALU.add)
-            h_of[(t, half)] = h
-
-        def place_h(t, half):
-            cols = slice(half * BANK, (half + 1) * BANK)
-            weight = wg_first[:, cols] if t == 0 else wg_rest[:, t - 1, cols]
-            slots = idx2[:, half * BANK // 16 : (half + 1) * BANK // 16]
-            nc.vector.tensor_tensor(out=pages[t][:].indirect(slots), in0=h_of[(t, half)][:], in1=weight, op=ALU.mult)
-
-        make_h(*units[0])
-        for u in range(len(units)):
-            if u + 1 < len(units):
-                make_h(*units[u + 1])
-            place_h(*units[u])
+            return acc_a, acc_b
 
         span = PACK * CHUNK
-        work = keep.tile([P, CHUNKS * span + CHUNK + span], F32, name="work", tag="late", align_bytes=64)
-        out_rows = out.rearrange("(b p) m -> p b m", p=P)
 
-        def x_of(c):
-            return work[:, c * span : (c + 1) * span]
-
-        def gate_of(c):
+        def gate_of(work, c):
             return work[:, (c + 1) * span + CHUNK : (c + 2) * span + CHUNK]
 
-        def pick(c, t):
+        def pick(work, c, t):
+            x = work[:, c * span : (c + 1) * span]
             slots = idx3[:, c * CHUNK // 16 : (c + 1) * CHUNK // 16]
-            nc.vector.tensor_copy(out=x_of(c)[:, t * CHUNK : (t + 1) * CHUNK], in_=pages[t][:].indirect(slots))
-            if t % 2 == 1:
-                pair = slice((t - 1) * CHUNK, (t + 1) * CHUNK)
-                nc.scalar.activation(out=gate_of(c)[:, pair], in_=x_of(c)[:, pair], func=ACT.Sigmoid)
+            nc.vector.tensor_copy(out=x[:, t * CHUNK : (t + 1) * CHUNK], in_=pages[t][:].indirect(slots))
+            if t >= PACK - 2:
+                part = slice(0, (PACK - 1) * CHUNK) if t == PACK - 2 else slice(t * CHUNK, span)
+                nc.scalar.activation(out=gate_of(work, c)[:, part], in_=x[:, part], func=ACT.Sigmoid)
 
-        for t in range(PACK):
-            pick(0, t)
+        for u, (t, half) in enumerate(units):
+            cols = slice(half * BANK, (half + 1) * BANK)
+            weight = wg[t][:, cols]
+            slots = idx2[:, half * BANK // 16 : (half + 1) * BANK // 16]
+            acc_a, acc_b = make_h(t, half)
+            gel = ring.tile([P, BANK], F32, name="gel")
+            nc.scalar.activation(out=gel[:], in_=acc_b[:], func=ACT.Gelu_apprx_tanh, bias=bias[:, t : t + 1])
+            h = keep.tile([P, BANK], F32, name="h", tag={0: "h_first", 3: "page3"}.get(u, "h"), align_bytes=64)
+            if u == len(units) - 2:
+                sent = keep.tile([P, BANK], F32, name="sent", tag="work", align_bytes=64)
+            else:
+                sent = ring.tile([P, BANK], F32, name="sent")
+            if u == 0:
+                nc.vector.tensor_tensor(out=h[:], in0=acc_a[:], in1=gel[:], op=ALU.add)
+                nc.vector.tensor_tensor(out=sent[:], in0=h[:], in1=weight, op=ALU.mult)
+            else:
+                lin = ring.tile([P, BANK], F32, name="lin")
+                nc.scalar.copy(out=lin[:], in_=acc_a[:])
+                nc.gpsimd.tensor_tensor(out=h[:], in0=lin[:], in1=gel[:], op=ALU.add)
+                nc.gpsimd.tensor_tensor(out=sent[:], in0=h[:], in1=weight, op=ALU.mult)
+                if u == 3:
+                    page = keep.tile([P, T2], F32, name="page%d" % len(pages), align_bytes=64)
+                    nc.gpsimd.memset(page[:], 0.0)
+                    pages.append(page)
+            if u == len(units) - 1:
+                work = keep.tile([P, CHUNKS * span + CHUNK + span], F32, name="work", align_bytes=64)
+                for early in range(PACK - 1):
+                    pick(work, 0, early)
+            nc.vector.tensor_copy(out=pages[t][:].indirect(slots), in_=sent[:])
+
+        out_rows = out.rearrange("(b p) m -> p b m", p=P)
+        pick(work, 0, PACK - 1)
         for c in range(CHUNKS):
             cols = slice(c * CHUNK, (c + 1) * CHUNK)
             if c + 1 < CHUNKS:
-                pick(c + 1, 0)
+                pick(work, c + 1, 0)
             z = ring.tile([P, span], BF16, name="z", align_bytes=64)
             nc.vector.tensor_tensor(
                 out=z[:].rearrange("p (n i t) -> p n t i", i=2, t=PACK),
-                in0=gate_of(c).rearrange("p (t n i) -> p n t i", t=PACK, i=2),
+                in0=gate_of(work, c).rearrange("p (t n i) -> p n t i", t=PACK, i=2),
                 in1=skip_sb[:, :, cols].rearrange("p t (n i) -> p n t i", i=2),
                 op=ALU.mult,
             )
@@ -234,26 +240,29 @@ def tile_list_pipeline_stage_transfer_kernel(
             nc.vector.quantize_mx(out=zc[:].bitcast(FP8X4), scales=zs[:], in_=z[:])
             if c + 1 < CHUNKS:
                 for t in range(1, PACK):
-                    pick(c + 1, t)
-            for s in range(BLOCKS // PER_STORE):
-                staged = stage.tile([P, PER_STORE, CHUNK], F32, name="staged")
-                for k in range(PER_STORE // PER_BANK):
-                    acc = psum.tile([P, PER_BANK, CHUNK], F32, name="acc", tag="bank%d" % ((4 + (c * BLOCKS + s * PER_STORE) // PER_BANK + k) % 8))
-                    for e in range(PER_BANK):
-                        b = s * PER_STORE + k * PER_BANK + e
-                        nc.tensor.matmul_mx(
-                            out=acc[:, e, :],
-                            lhsT=w3c[:, b * P : (b + 1) * P].bitcast(FP8X4),
-                            lhsT_scale=w3s[:, b * P : (b + 1) * P],
-                            rhs=zc[:].bitcast(FP8X4),
-                            rhs_scale=zs[:],
-                            start=True,
-                            stop=True,
-                        )
-                    target = staged[:, k * PER_BANK : (k + 1) * PER_BANK, :]
-                    on_vector = k == 1 and (c == CHUNKS - 1 or s == BLOCKS // PER_STORE - 1)
-                    if on_vector:
-                        nc.vector.tensor_copy(out=target, in_=acc[:])
-                    else:
-                        nc.scalar.copy(out=target, in_=acc[:])
-                nc.sync.dma_start(out=out_rows[:, s * PER_STORE : (s + 1) * PER_STORE, cols], in_=staged[:])
+                    pick(work, c + 1, t)
+            banks_a_store = 1 if c == CHUNKS - 1 else 2
+            for n in range(BANKS_A_CHUNK):
+                k = n % banks_a_store
+                if k == 0:
+                    staged = stage.tile([P, banks_a_store * PER_BANK, CHUNK], F32, name="staged")
+                acc = psum.tile([P, PER_BANK, CHUNK], F32, name="acc", tag="bank%d" % ((4 + c * BANKS_A_CHUNK + n) % 8))
+                for e in range(PER_BANK):
+                    b = n * PER_BANK + e
+                    nc.tensor.matmul_mx(
+                        out=acc[:, e, :],
+                        lhsT=w3c[:, b * P : (b + 1) * P].bitcast(FP8X4),
+                        lhsT_scale=w3s[:, b * P : (b + 1) * P],
+                        rhs=zc[:].bitcast(FP8X4),
+                        rhs_scale=zs[:],
+                        start=True,
+                        stop=True,
+                    )
+                target = staged[:, k * PER_BANK : (k + 1) * PER_BANK, :]
+                if (n % 2 == 0) if c == CHUNKS - 1 else (n == 2):
+                    nc.vector.tensor_copy(out=target, in_=acc[:])
+                else:
+                    nc.scalar.copy(out=target, in_=acc[:])
+                if k == banks_a_store - 1:
+                    blocks = slice((n - k) * PER_BANK, (n + 1) * PER_BANK)
+                    nc.sync.dma_start(out=out_rows[:, blocks, cols], in_=staged[:])

@@ -223,46 +223,62 @@ def tile_list_pipeline_stage_transfer_kernel(
             nc.vector.tensor_copy(out=pages[t][:].indirect(slots), in_=sent[:])
 
         out_rows = out.rearrange("(b p) m -> p b m", p=P)
+        spent = ["tab1", "tab2", "w2_raw0", "w2_raw1", "w2_raw2", "w2_bf_rest"]
         pick(work, 0, PACK - 1)
         for c in range(CHUNKS):
             cols = slice(c * CHUNK, (c + 1) * CHUNK)
             if c + 1 < CHUNKS:
                 pick(work, c + 1, 0)
-            z = ring.tile([P, span], BF16, name="z", align_bytes=64)
-            nc.vector.tensor_tensor(
-                out=z[:].rearrange("p (n i t) -> p n t i", i=2, t=PACK),
-                in0=gate_of(work, c).rearrange("p (t n i) -> p n t i", t=PACK, i=2),
-                in1=skip_sb[:, :, cols].rearrange("p t (n i) -> p n t i", i=2),
-                op=ALU.mult,
-            )
-            zc = ring.tile([P, CHUNK], U32, name="zc", align_bytes=64)
-            zs = ring.tile([P, CHUNK], U8, name="zs", align_bytes=64)
-            nc.vector.quantize_mx(out=zc[:].bitcast(FP8X4), scales=zs[:], in_=z[:])
-            if c + 1 < CHUNKS:
+            last = c == CHUNKS - 1
+            width = CHUNK // 2 if last else CHUNK
+            operands = []
+            for lo in range(0, CHUNK, width):
+                z = ring.tile([P, PACK * width], BF16, name="z", align_bytes=64)
+                pairs = slice(lo // 2, (lo + width) // 2)
+                nc.vector.tensor_tensor(
+                    out=z[:].rearrange("p (n i t) -> p n t i", i=2, t=PACK),
+                    in0=gate_of(work, c).rearrange("p (t n i) -> p n t i", t=PACK, i=2)[:, pairs],
+                    in1=skip_sb[:, :, cols].rearrange("p t (n i) -> p n t i", i=2)[:, pairs],
+                    op=ALU.mult,
+                )
+                zc = ring.tile([P, width], U32, name="zc", align_bytes=64)
+                zs = ring.tile([P, width], U8, name="zs", align_bytes=64)
+                nc.vector.quantize_mx(out=zc[:].bitcast(FP8X4), scales=zs[:], in_=z[:])
+                operands.append((lo, zc, zs))
+            if not last:
                 for t in range(1, PACK):
                     pick(work, c + 1, t)
-            banks_a_store = 1 if c == CHUNKS - 1 else 2
-            for n in range(BANKS_A_CHUNK):
-                k = n % banks_a_store
-                if k == 0:
-                    staged = stage.tile([P, banks_a_store * PER_BANK, CHUNK], F32, name="staged")
-                acc = psum.tile([P, PER_BANK, CHUNK], F32, name="acc", tag="bank%d" % ((4 + c * BANKS_A_CHUNK + n) % 8))
-                for e in range(PER_BANK):
-                    b = n * PER_BANK + e
-                    nc.tensor.matmul_mx(
-                        out=acc[:, e, :],
-                        lhsT=w3c[:, b * P : (b + 1) * P].bitcast(FP8X4),
-                        lhsT_scale=w3s[:, b * P : (b + 1) * P],
-                        rhs=zc[:].bitcast(FP8X4),
-                        rhs_scale=zs[:],
-                        start=True,
-                        stop=True,
-                    )
-                target = staged[:, k * PER_BANK : (k + 1) * PER_BANK, :]
-                if (n % 2 == 0) if c == CHUNKS - 1 else (n == 2):
-                    nc.vector.tensor_copy(out=target, in_=acc[:])
-                else:
-                    nc.scalar.copy(out=target, in_=acc[:])
-                if k == banks_a_store - 1:
-                    blocks = slice((n - k) * PER_BANK, (n + 1) * PER_BANK)
-                    nc.sync.dma_start(out=out_rows[:, blocks, cols], in_=staged[:])
+            per_bank = BANK // width
+            banks_a_store = 1 if last else 2
+            n = 0
+            for lo, zc, zs in operands:
+                for first in range(0, BLOCKS, per_bank):
+                    k = n % banks_a_store
+                    if k == 0:
+                        if last:
+                            staged = keep.tile([P, per_bank, width], F32, name="staged", tag=spent[n], align_bytes=64)
+                        else:
+                            staged = stage.tile([P, banks_a_store * per_bank, width], F32, name="staged")
+                    acc = psum.tile([P, per_bank, width], F32, name="acc", tag="bank%d" % ((4 + c * BANKS_A_CHUNK + n) % 8))
+                    for e in range(per_bank):
+                        b = first + e
+                        nc.tensor.matmul_mx(
+                            out=acc[:, e, :],
+                            lhsT=w3c[:, b * P : (b + 1) * P].bitcast(FP8X4),
+                            lhsT_scale=w3s[:, b * P : (b + 1) * P],
+                            rhs=zc[:].bitcast(FP8X4),
+                            rhs_scale=zs[:],
+                            start=True,
+                            stop=True,
+                        )
+                    target = staged[:, k * per_bank : (k + 1) * per_bank, :]
+                    if (n in (2, 3, 5)) if last else (n == 0):
+                        nc.vector.tensor_copy(out=target, in_=acc[:])
+                    else:
+                        nc.scalar.copy(out=target, in_=acc[:])
+                    if k == banks_a_store - 1:
+                        blocks = slice(first - k * per_bank, first + per_bank)
+                        nc.sync.dma_start(
+                            out=out_rows[:, blocks, c * CHUNK + lo : c * CHUNK + lo + width], in_=staged[:]
+                        )
+                    n = n + 1

@@ -36,40 +36,47 @@ def tile_list_pipeline_stage_transfer_kernel(
     with ExitStack() as ctx:
         lists = ctx.enter_context(tc.tile_pool(name="lists", bufs=1))
         keep = ctx.enter_context(tc.tile_pool(name="keep", bufs=1))
+        pair = ctx.enter_context(tc.tile_pool(name="pair", bufs=2))
         ring = ctx.enter_context(tc.tile_pool(name="ring", bufs=3))
-        stage = ctx.enter_context(tc.tile_pool(name="stage", bufs=6))
+        stage = ctx.enter_context(tc.tile_pool(name="stage", bufs=8))
         psum = ctx.enter_context(tc.psum_pool(name="psum", bufs=1))
+
+        def held(shape, dtype, name, tag=None):
+            return keep.tile(shape, dtype, name=name, tag=tag or name, align_bytes=64)
 
         idx = lists.tile([P, S // 16], U16, name="idx")
         idx2 = lists.tile([P, S // 16], U16, name="idx2")
         idx3 = lists.tile([P, M_OUT // 16], U16, name="idx3")
 
-        tab = [keep.tile([P, T], U32, name="tab%d" % a, align_bytes=64) for a in range(PASSES)]
-        tab_s = keep.tile([P, T], U8, name="tab_s", align_bytes=64)
-        v = [keep.tile([P, S], U32, name="v%d" % a, align_bytes=64) for a in range(PASSES)]
-        v_s = [keep.tile([P, S], U8, name="v_s%d" % a, align_bytes=64) for a in range(PASSES)]
-        w1_raw = keep.tile([P, PASSES, 2 * H], U8, name="w1_raw", align_bytes=64)
-        w1_raw_s = keep.tile([P, PASSES, H], U8, name="w1_raw_s", align_bytes=64)
-        w1c = keep.tile([P, PASSES, 2 * H], U8, name="w1c", align_bytes=64)
-        w1s = keep.tile([P, PASSES, H], U8, name="w1s", align_bytes=64)
-        w2_raw = [keep.tile([P, PACK, H], F32, name="w2_raw%d" % a, align_bytes=64) for a in range(PASSES)]
-        w2_bf_first = keep.tile([P, H * PACK], BF16, name="w2_bf_first", align_bytes=64)
-        w2_bf_rest = keep.tile([P, PASSES - 1, H * PACK], BF16, name="w2_bf_rest", align_bytes=64)
-        w2_bf = [w2_bf_first[:]] + [w2_bf_rest[:, a - 1, :] for a in range(1, PASSES)]
-        w2c = [keep.tile([P, H], U32, name="w2c%d" % a, align_bytes=64) for a in range(PASSES)]
-        w2s = [keep.tile([P, H], U8, name="w2s%d" % a, align_bytes=64) for a in range(PASSES)]
-        bias = keep.tile([P, PACK], F32, name="bias", align_bytes=64)
-        wg_first = keep.tile([P, 1, S], F32, name="wg_first", align_bytes=64)
-        wg_second = keep.tile([P, 1, S], F32, name="wg_second", align_bytes=64)
-        pages = [keep.tile([P, T2], F32, name="page%d" % t, align_bytes=64) for t in range(PACK - 1)]
-        skip_sb = keep.tile([P, PACK, M_OUT], F32, name="skip_sb", align_bytes=64)
-        w3c = keep.tile([P, N_OUT], U32, name="w3c", align_bytes=64)
-        w3s = keep.tile([P, N_OUT], U8, name="w3s", align_bytes=64)
+        tab = [held([P, T], U32, "tab%d" % a) for a in range(PASSES)]
+        tab_s = held([P, T], U8, "tab_s")
+        v_s = held([P, S], U8, "v_s")
+        v_s_down = held([P, (PASSES - 1) * S], U8, "v_s_down")
+        w1_raw = held([P, PASSES, 2 * H], U8, "w1_raw")
+        w1_raw_s = held([P, PASSES, H], U8, "w1_raw_s")
+        w1c = held([P, PASSES, 2 * H], U8, "w1c")
+        w1s = held([P, PASSES, H], U8, "w1s")
+        w2_raw = [held([P, PACK, H], F32, "w2_raw%d" % a) for a in range(PASSES)]
+        bias = held([P, PACK], F32, "bias")
+        wg_a = held([P, 1, CHUNK], F32, "wg_a")
+        wg_b = held([P, 1, S - CHUNK], F32, "wg_b")
+        wg_second = held([P, 1, S], F32, "wg_second")
+        wg_rest = held([P, 2, S], F32, "wg_rest")
+        skip_sb = held([P, PACK, M_OUT], F32, "skip_sb")
+        w3c = held([P, N_OUT], U32, "w3c")
+        span = PACK * CHUNK
+        work = held([P, (CHUNKS + 1) * span + BANK], F32, "work")
+        warm_in = held([P, 1], F32, "warm_in")
+        warm_out = held([P, 1], F32, "warm_out")
+
+        nc.gpsimd.memset(warm_in[:], 0.0)
+        nc.scalar.activation(out=warm_out[:], in_=warm_in[:], func=ACT.Gelu_apprx_tanh)
 
         nc.vector.memset(tab_s[:].bitcast(I32), 0)
         nc.vector.memset(w1_raw_s[:].bitcast(I32), 0)
-        for a in range(1, PASSES):
-            nc.vector.memset(v_s[a][:].bitcast(I32), 0)
+        nc.vector.memset(v_s_down[:].bitcast(I32), 0)
+        pages = [held([P, T2], F32, "page0")]
+        nc.vector.memset(pages[0][:], 0.0)
 
         def load_tab(a):
             nc.sync.dma_start(out=tab[a][:].bitcast(I32), in_=tab_words[a].rearrange("p t i -> p (t i)").bitcast(I32))
@@ -78,207 +85,282 @@ def tile_list_pipeline_stage_transfer_kernel(
             rows = w2[a * P * PACK : (a + 1) * P * PACK, :]
             nc.sync.dma_start(out=w2_raw[a][:], in_=rows.rearrange("(p j) c -> p j c", j=PACK))
 
-        def gather_words(a, lo, hi):
-            nc.vector.tensor_copy(out=v[a][:, lo:hi], in_=tab[a][:].indirect(idx[:, lo // 16 : hi // 16]))
+        def gather_words(a, lo, hi, tag=None):
+            words = held([P, hi - lo], U32, "v%d_%d" % (a, lo), tag)
+            nc.vector.tensor_copy(out=words[:], in_=tab[a][:].indirect(idx[:, lo // 16 : hi // 16]))
+            return [words[:, c - lo : c - lo + BANK] for c in range(lo, hi, BANK)]
+
+        w2q = {}
+
+        def cast_w2(copy, a, lo, hi, tag=None):
+            grouped = held([P, (hi - lo) * P * PACK], BF16, "w2_bf%d_%d" % (a, lo), tag)
+            copy(
+                out=grouped[:].rearrange("p (t m j) -> p m t j", m=P, j=PACK),
+                in_=w2_raw[a][:].rearrange("p j (m t) -> p m t j", t=PACK)[:, :, lo:hi, :],
+            )
+            return grouped
+
+        def quantize_w2(grouped, a, lo, hi):
+            codes = held([P, (hi - lo) * P], U32, "w2c%d_%d" % (a, lo))
+            scales = held([P, (hi - lo) * P], U8, "w2s%d_%d" % (a, lo))
+            nc.vector.quantize_mx(out=codes[:].bitcast(FP8X4), scales=scales[:], in_=grouped[:])
+            for t in range(lo, hi):
+                cols = slice((t - lo) * P, (t - lo + 1) * P)
+                w2q[(a, t)] = (codes[:, cols], scales[:, cols])
 
         wgs_rows = wgs.rearrange("(m t) j -> m t j", t=PACK)
 
         nc.sync.dma_start(idx[:], offs)
-        load_tab(0)
         nc.sync.dma_start(out=w1_raw[:].bitcast(I32), in_=w1_words.rearrange("a p c -> p a c").bitcast(I32))
+        load_tab(0)
         for q in range(QUADS):
             nc.sync.dma_start(
                 out=tab_s[32 * q : 32 * q + 4 * PASSES, :].bitcast(I32),
                 in_=tab_scales[:, 4 * q : 4 * q + 4, :].bitcast(I32),
             )
         load_w2(0)
-        load_w2(1)
         for q in range(QUADS):
             nc.sync.dma_start(
                 out=w1_raw_s[32 * q : 32 * q + 4, :, :].bitcast(I32),
                 in_=w1_scales[:, 4 * q : 4 * q + 4, :].rearrange("a r c -> r a c").bitcast(I32),
             )
         load_tab(1)
+        load_w2(1)
+        load_tab(2)
+
+        nc.vector.tensor_copy(
+            out=w1c[:].bitcast(U16).rearrange("p a (t m) -> p t a m", t=PACK),
+            in_=w1_raw[:].bitcast(U16).rearrange("p a (m t) -> p t a m", t=PACK),
+        )
+        v = [gather_words(0, 0, S)]
+        nc.vector.tensor_copy(out=v_s[:], in_=tab_s[:].indirect(idx[:]))
+        nc.vector.tensor_copy(
+            out=w1s[:].rearrange("p a (t m) -> p t a m", t=PACK),
+            in_=w1_raw_s[:].rearrange("p a (m t) -> p t a m", t=PACK),
+        )
+        for a in range(1, PASSES):
+            nc.sync.dma_start(
+                out=v_s_down[0:112, (a - 1) * S : a * S].bitcast(I32), in_=v_s[4 * a : 4 * a + 112, :].bitcast(I32)
+            )
+        nc.sync.dma_start(out=bias[:], in_=b2.rearrange("(p t) -> p t", t=PACK))
         nc.sync.dma_start(idx2[:], offs2)
         load_w2(2)
-        gather_words(0, 0, S)
-        nc.vector.tensor_copy(out=v_s[0][:], in_=tab_s[:].indirect(idx[:]))
-        load_tab(2)
-        for a in range(1, PASSES):
-            nc.sync.dma_start(out=v_s[a][0:112, :].bitcast(I32), in_=v_s[0][4 * a : 4 * a + 112, :].bitcast(I32))
-        nc.sync.dma_start(out=bias[:], in_=b2.rearrange("(p t) -> p t", t=PACK))
-        wg_rest = keep.tile([P, 2, S], F32, name="wg_rest", tag="tab0", align_bytes=64)
-        wg = [wg_first[:, 0, :], wg_second[:, 0, :], wg_rest[:, 0, :], wg_rest[:, 1, :]]
-        for tile, lo, hi in ((wg_first, 0, 1), (wg_second, 1, 2), (wg_rest, 2, PACK)):
+        for tile, lo, hi, c0, c1 in (
+            (wg_a, 0, 1, 0, CHUNK),
+            (wg_b, 0, 1, CHUNK, S),
+            (wg_second, 1, 2, 0, S),
+            (wg_rest, 2, PACK, 0, S),
+        ):
             for q in (0, 2, 1, 3):
-                nc.sync.dma_start(out=tile[32 * q : 32 * q + 32, :, :], in_=wgs_rows[:, lo:hi, :])
+                nc.sync.dma_start(out=tile[32 * q : 32 * q + 32, :, :], in_=wgs_rows[:, lo:hi, c0:c1])
         nc.sync.dma_start(idx3[:], offs3)
         nc.sync.dma_start(out=skip_sb[:], in_=skip.rearrange("(p t) m -> p t m", t=PACK))
-        nc.vector.memset(w3s[:].bitcast(I32), 0)
         nc.sync.dma_start(out=w3c[:].bitcast(I32), in_=w3_words[0].rearrange("p c i -> p (c i)").bitcast(I32))
+
+        for t, spent in ((1, "w1_raw"), (2, "w1_raw_s"), (3, "tab0")):
+            pages.append(held([P, T2], F32, "page%d" % t, spent))
+            step = T2 if t == 1 else BANK
+            for lo in range(0, T2, step):
+                nc.gpsimd.memset(pages[t][:, lo : lo + step], 0.0)
+        w3s = held([P, N_OUT], U8, "w3s", "tab1")
+        nc.gpsimd.memset(w3s[:].bitcast(I32), 0)
         for q in range(QUADS):
             nc.sync.dma_start(
                 out=w3s[32 * q : 32 * q + 4, :].bitcast(I32), in_=w3_scales[0, 4 * q : 4 * q + 4, :].bitcast(I32)
             )
 
-        def cast_w2(a):
-            nc.scalar.copy(
-                out=w2_bf[a].rearrange("p (t m j) -> p m t j", t=PACK, j=PACK),
-                in_=w2_raw[a][:].rearrange("p j (m t) -> p m t j", t=PACK),
-            )
-
-        def quantize_w2(a):
-            nc.vector.quantize_mx(out=w2c[a][:].bitcast(FP8X4), scales=w2s[a][:], in_=w2_bf[a])
-
-        for a in range(PASSES):
-            cast_w2(a)
-
-        nc.vector.tensor_copy(
-            out=w1c[:].bitcast(U16).rearrange("p a (t m) -> p a t m", t=PACK),
-            in_=w1_raw[:].bitcast(U16).rearrange("p a (m t) -> p a t m", t=PACK),
-        )
-        nc.vector.tensor_copy(
-            out=w1s[:].rearrange("p a (t m) -> p a t m", t=PACK),
-            in_=w1_raw_s[:].rearrange("p a (m t) -> p a t m", t=PACK),
-        )
-        quantize_w2(0)
-        gather_words(1, 0, S)
-        quantize_w2(1)
-        gather_words(2, 0, BANK)
-        quantize_w2(2)
-        gather_words(2, BANK, S)
-
-        for t in range(PACK - 1):
-            nc.vector.memset(pages[t][:], 0.0)
+        grouped0 = cast_w2(nc.scalar.copy, 0, 0, PACK)
+        grouped1 = cast_w2(nc.scalar.copy, 1, 0, PACK)
+        v.append(gather_words(1, 0, S, "tab_s"))
+        quantize_w2(grouped0, 0, 0, PACK)
+        v.append(gather_words(2, 0, BANK))
+        quantize_w2(grouped1, 1, 0, PACK)
+        quantize_w2(cast_w2(nc.vector.tensor_copy, 2, 0, 1), 2, 0, 1)
+        v[2].extend(gather_words(2, BANK, S, "w2_bf2_0"))
+        grouped2 = cast_w2(nc.scalar.copy, 2, 1, 2)
 
         units = [(t, half) for t in range(PACK) for half in range(HALVES)]
 
-        def make_h(t, half):
+        def make_h(u):
+            t, half = units[u]
             cols = slice(half * BANK, (half + 1) * BANK)
             rows = slice(t * P, (t + 1) * P)
-            acc_b = psum.tile([P, BANK], F32, name="acc_b", tag="bank%d" % (2 * half))
-            acc_a = psum.tile([P, BANK], F32, name="acc_a", tag="bank%d" % (2 * half + 1))
+            acc_b = psum.tile([P, BANK], F32, name="acc_b", tag="bank%d" % (2 * u % 8))
+            acc_a = psum.tile([P, BANK], F32, name="acc_a", tag="bank%d" % (2 * u % 8 + 1))
             for a in range(PASSES):
-                nc.tensor.matmul_mx(
-                    out=acc_b[:],
-                    lhsT=w2c[a][:, rows].bitcast(FP8X4),
-                    lhsT_scale=w2s[a][:, rows],
-                    rhs=v[a][:, cols].bitcast(FP8X4),
-                    rhs_scale=v_s[0][4 * a : P, cols],
-                    start=(a == 0),
-                    stop=(a == PASSES - 1),
-                )
+                plane = v_s[:, cols] if a == 0 else v_s_down[:, (a - 1) * S + half * BANK : (a - 1) * S + (half + 1) * BANK]
                 nc.tensor.matmul_mx(
                     out=acc_a[:],
                     lhsT=w1c[:, a, 2 * t * P : 2 * (t + 1) * P].bitcast(FP4X4),
                     lhsT_scale=w1s[:, a, rows],
-                    rhs=v[a][:, cols].bitcast(FP8X4),
-                    rhs_scale=v_s[a][:, cols],
+                    rhs=v[a][half].bitcast(FP8X4),
+                    rhs_scale=plane,
+                    start=(a == 0),
+                    stop=(a == PASSES - 1),
+                )
+                nc.tensor.matmul_mx(
+                    out=acc_b[:],
+                    lhsT=w2q[(a, t)][0].bitcast(FP8X4),
+                    lhsT_scale=w2q[(a, t)][1],
+                    rhs=v[a][half].bitcast(FP8X4),
+                    rhs_scale=v_s[4 * a : P, cols],
                     start=(a == 0),
                     stop=(a == PASSES - 1),
                 )
             return acc_a, acc_b
 
-        span = PACK * CHUNK
+        gates = [work[:, c * span : (c + 1) * span] for c in range(CHUNKS)]
+        first_x = work[:, CHUNKS * span : (CHUNKS + 1) * span]
+        last_sent = work[:, (CHUNKS + 1) * span :]
 
-        def gate_of(work, c):
-            return work[:, (c + 1) * span + CHUNK : (c + 2) * span + CHUNK]
+        def quarter(region, k, n=1):
+            return region[:, k * CHUNK : (k + n) * CHUNK]
 
-        def pick(work, c, t):
-            x = work[:, c * span : (c + 1) * span]
+        home = {(0, t): (first_x, t) for t in range(PACK)}
+        home[(1, 0)] = (last_sent, 0)
+        home[(2, 1)] = (last_sent, 0)
+        for k, piece in enumerate(((1, 1), (1, 2), (1, 3), (2, 0))):
+            home[piece] = (gates[0], k)
+        for k, piece in enumerate(((2, 2), (2, 3), (3, 0), (3, 1))):
+            home[piece] = (gates[1], k)
+        for k, piece in enumerate(((3, 2), (3, 3))):
+            home[piece] = (gates[2], k)
+
+        def pick(c, t):
             slots = idx3[:, c * CHUNK // 16 : (c + 1) * CHUNK // 16]
-            nc.vector.tensor_copy(out=x[:, t * CHUNK : (t + 1) * CHUNK], in_=pages[t][:].indirect(slots))
-            if t >= PACK - 2:
-                part = slice(0, (PACK - 1) * CHUNK) if t == PACK - 2 else slice(t * CHUNK, span)
-                nc.scalar.activation(out=gate_of(work, c)[:, part], in_=x[:, part], func=ACT.Sigmoid)
+            nc.vector.tensor_copy(out=quarter(*home[(c, t)]), in_=pages[t][:].indirect(slots))
 
-        for u, (t, half) in enumerate(units):
-            cols = slice(half * BANK, (half + 1) * BANK)
-            weight = wg[t][:, cols]
-            slots = idx2[:, half * BANK // 16 : (half + 1) * BANK // 16]
-            acc_a, acc_b = make_h(t, half)
-            gel = ring.tile([P, BANK], F32, name="gel")
-            nc.scalar.activation(out=gel[:], in_=acc_b[:], func=ACT.Gelu_apprx_tanh, bias=bias[:, t : t + 1])
-            h = keep.tile([P, BANK], F32, name="h", tag={0: "h_first", 3: "page3"}.get(u, "h"), align_bytes=64)
-            if u == len(units) - 2:
-                sent = keep.tile([P, BANK], F32, name="sent", tag="work", align_bytes=64)
+        def sigmoid(c, t, n=1):
+            region, k = home[(c, t)]
+            nc.scalar.activation(out=quarter(gates[c], t, n), in_=quarter(region, k, n), func=ACT.Sigmoid)
+
+        def scatter(t, lo, values):
+            width = values.shape[1]
+            nc.vector.tensor_copy(out=pages[t][:].indirect(idx2[:, lo // 16 : (lo + width) // 16]), in_=values)
+
+        def weigh_on_gpsimd(lin, gel, weight, sent):
+            h = held([P, lin.shape[1]], F32, "h")
+            nc.gpsimd.tensor_tensor(out=h[:], in0=lin, in1=gel, op=ALU.add)
+            nc.gpsimd.tensor_tensor(out=sent, in0=h[:], in1=weight, op=ALU.mult)
+
+        acc_a, acc_b = make_h(0)
+        lin = pair.tile([P, BANK], F32, name="lin")
+        nc.scalar.copy(out=lin[:, 0:CHUNK], in_=acc_a[:, CHUNK:BANK])
+        gel = held([P, BANK], F32, "gel_first")
+        for lo in (0, CHUNK):
+            nc.scalar.activation(
+                out=gel[:, lo : lo + CHUNK], in_=acc_b[:, lo : lo + CHUNK], func=ACT.Gelu_apprx_tanh, bias=bias[:, 0:1]
+            )
+        h_first = held([P, CHUNK], F32, "h_first")
+        sent = ring.tile([P, BANK], F32, name="sent")
+        nc.vector.tensor_tensor(out=h_first[:], in0=acc_a[:, 0:CHUNK], in1=gel[:, 0:CHUNK], op=ALU.add)
+        nc.vector.tensor_tensor(out=sent[:, 0:CHUNK], in0=h_first[:], in1=wg_a[:, 0, :], op=ALU.mult)
+        scatter(0, 0, sent[:, 0:CHUNK])
+        weigh_on_gpsimd(lin[:, 0:CHUNK], gel[:, CHUNK:BANK], wg_b[:, 0, 0:CHUNK], sent[:, CHUNK:BANK])
+        quantize_w2(grouped2, 2, 1, 2)
+        scatter(0, CHUNK, sent[:, CHUNK:BANK])
+
+        wg = [None, wg_second[:, 0, :], wg_rest[:, 0, :], wg_rest[:, 1, :]]
+        for u in range(1, len(units)):
+            t, half = units[u]
+            last = u == len(units) - 1
+            weight = wg_b[:, 0, BANK - CHUNK :] if t == 0 else wg[t][:, half * BANK : (half + 1) * BANK]
+            acc_a, acc_b = make_h(u)
+            lin = pair.tile([P, BANK], F32, name="lin")
+            nc.scalar.copy(out=lin[:], in_=acc_a[:])
+            if last:
+                gel = gates[0][:, 0:BANK]
+            elif u == 1:
+                gel = held([P, BANK], F32, "gel_second")[:]
             else:
-                sent = ring.tile([P, BANK], F32, name="sent")
-            if u == 0:
-                nc.vector.tensor_tensor(out=h[:], in0=acc_a[:], in1=gel[:], op=ALU.add)
-                nc.vector.tensor_tensor(out=sent[:], in0=h[:], in1=weight, op=ALU.mult)
-            else:
-                lin = ring.tile([P, BANK], F32, name="lin")
-                nc.scalar.copy(out=lin[:], in_=acc_a[:])
-                nc.gpsimd.tensor_tensor(out=h[:], in0=lin[:], in1=gel[:], op=ALU.add)
-                nc.gpsimd.tensor_tensor(out=sent[:], in0=h[:], in1=weight, op=ALU.mult)
-                if u == 3:
-                    page = keep.tile([P, T2], F32, name="page%d" % len(pages), align_bytes=64)
-                    nc.gpsimd.memset(page[:], 0.0)
-                    pages.append(page)
-            if u == len(units) - 1:
-                work = keep.tile([P, CHUNKS * span + CHUNK + span], F32, name="work", align_bytes=64)
+                gel = ring.tile([P, BANK], F32, name="gel")[:]
+            nc.scalar.activation(out=gel, in_=acc_b[:], func=ACT.Gelu_apprx_tanh, bias=bias[:, t : t + 1])
+            sent = last_sent if last else ring.tile([P, BANK], F32, name="sent")[:]
+            weigh_on_gpsimd(lin[:], gel, weight, sent)
+            if last:
                 for early in range(PACK - 1):
-                    pick(work, 0, early)
-            nc.vector.tensor_copy(out=pages[t][:].indirect(slots), in_=sent[:])
+                    pick(0, early)
+                sigmoid(0, 0, PACK - 1)
+            scatter(t, half * BANK, sent)
+            if u == 1:
+                quantize_w2(cast_w2(nc.scalar.copy, 2, 2, PACK, "gel_second"), 2, 2, PACK)
 
         out_rows = out.rearrange("(b p) m -> p b m", p=P)
-        spent = ["tab1", "tab2", "w2_raw0", "w2_raw1", "w2_raw2", "w2_bf_rest"]
-        pick(work, 0, PACK - 1)
-        for c in range(CHUNKS):
+
+        def make_z(c):
             cols = slice(c * CHUNK, (c + 1) * CHUNK)
-            if c + 1 < CHUNKS:
-                pick(work, c + 1, 0)
-            last = c == CHUNKS - 1
-            width = CHUNK // 2 if last else CHUNK
-            operands = []
-            for lo in range(0, CHUNK, width):
-                z = ring.tile([P, PACK * width], BF16, name="z", align_bytes=64)
-                pairs = slice(lo // 2, (lo + width) // 2)
-                nc.vector.tensor_tensor(
-                    out=z[:].rearrange("p (n i t) -> p n t i", i=2, t=PACK),
-                    in0=gate_of(work, c).rearrange("p (t n i) -> p n t i", t=PACK, i=2)[:, pairs],
-                    in1=skip_sb[:, :, cols].rearrange("p t (n i) -> p n t i", i=2)[:, pairs],
-                    op=ALU.mult,
+            z = ring.tile([P, span], BF16, name="z", align_bytes=64)
+            nc.vector.tensor_tensor(
+                out=z[:].rearrange("p (n i t) -> p n t i", i=2, t=PACK),
+                in0=gates[c].rearrange("p (t n i) -> p n t i", t=PACK, i=2),
+                in1=skip_sb[:, :, cols].rearrange("p t (n i) -> p n t i", i=2),
+                op=ALU.mult,
+            )
+            zc = ring.tile([P, CHUNK], U32, name="zc", align_bytes=64)
+            zs = ring.tile([P, CHUNK], U8, name="zs", align_bytes=64)
+            nc.vector.quantize_mx(out=zc[:].bitcast(FP8X4), scales=zs[:], in_=z[:])
+            return zc, zs
+
+        def send_bank(c, n, zq, copy):
+            zc, zs = zq
+            acc = psum.tile([P, PER_BANK, CHUNK], F32, name="acc", tag="bank%d" % ((c * BANKS_A_CHUNK + n) % 8))
+            for e in range(PER_BANK):
+                b = n * PER_BANK + e
+                nc.tensor.matmul_mx(
+                    out=acc[:, e, :],
+                    lhsT=w3c[:, b * P : (b + 1) * P].bitcast(FP8X4),
+                    lhsT_scale=w3s[:, b * P : (b + 1) * P],
+                    rhs=zc[:].bitcast(FP8X4),
+                    rhs_scale=zs[:],
+                    start=True,
+                    stop=True,
                 )
-                zc = ring.tile([P, width], U32, name="zc", align_bytes=64)
-                zs = ring.tile([P, width], U8, name="zs", align_bytes=64)
-                nc.vector.quantize_mx(out=zc[:].bitcast(FP8X4), scales=zs[:], in_=z[:])
-                operands.append((lo, zc, zs))
-            if not last:
-                for t in range(1, PACK):
-                    pick(work, c + 1, t)
-            per_bank = BANK // width
-            banks_a_store = 1 if last else 2
-            n = 0
-            for lo, zc, zs in operands:
-                for first in range(0, BLOCKS, per_bank):
-                    k = n % banks_a_store
-                    if k == 0:
-                        if last:
-                            staged = keep.tile([P, per_bank, width], F32, name="staged", tag=spent[n], align_bytes=64)
-                        else:
-                            staged = stage.tile([P, banks_a_store * per_bank, width], F32, name="staged")
-                    acc = psum.tile([P, per_bank, width], F32, name="acc", tag="bank%d" % ((4 + c * BANKS_A_CHUNK + n) % 8))
-                    for e in range(per_bank):
-                        b = first + e
-                        nc.tensor.matmul_mx(
-                            out=acc[:, e, :],
-                            lhsT=w3c[:, b * P : (b + 1) * P].bitcast(FP8X4),
-                            lhsT_scale=w3s[:, b * P : (b + 1) * P],
-                            rhs=zc[:].bitcast(FP8X4),
-                            rhs_scale=zs[:],
-                            start=True,
-                            stop=True,
-                        )
-                    target = staged[:, k * per_bank : (k + 1) * per_bank, :]
-                    if (n in (2, 3, 5)) if last else (n == 0):
-                        nc.vector.tensor_copy(out=target, in_=acc[:])
-                    else:
-                        nc.scalar.copy(out=target, in_=acc[:])
-                    if k == banks_a_store - 1:
-                        blocks = slice(first - k * per_bank, first + per_bank)
-                        nc.sync.dma_start(
-                            out=out_rows[:, blocks, c * CHUNK + lo : c * CHUNK + lo + width], in_=staged[:]
-                        )
-                    n = n + 1
+            staged = stage.tile([P, PER_BANK, CHUNK], F32, name="staged")
+            copy(out=staged[:], in_=acc[:])
+            nc.sync.dma_start(
+                out=out_rows[:, n * PER_BANK : (n + 1) * PER_BANK, c * CHUNK : (c + 1) * CHUNK], in_=staged[:]
+            )
+
+        on_scalar, on_vector = nc.scalar.copy, nc.vector.tensor_copy
+
+        pick(0, 3)
+        sigmoid(0, 3)
+        pick(1, 0)
+        sigmoid(1, 0)
+        zq = make_z(0)
+        for c, t in ((1, 1), (1, 2), (2, 0), (1, 3)):
+            pick(c, t)
+        send_bank(0, 0, zq, on_scalar)
+        send_bank(0, 1, zq, on_scalar)
+        sigmoid(1, 1, 3)
+        send_bank(0, 2, zq, on_scalar)
+        pick(2, 1)
+        next_zq = make_z(1)
+        send_bank(0, 3, zq, on_scalar)
+        sigmoid(2, 0)
+        sigmoid(2, 1)
+        send_bank(0, 4, zq, on_scalar)
+        send_bank(0, 5, zq, on_scalar)
+        zq = next_zq
+        for c, t in ((2, 2), (2, 3), (3, 0), (3, 1)):
+            pick(c, t)
+        send_bank(1, 0, zq, on_scalar)
+        sigmoid(2, 2, 2)
+        send_bank(1, 1, zq, on_scalar)
+        send_bank(1, 2, zq, on_scalar)
+        next_zq = make_z(2)
+        sigmoid(3, 0, 2)
+        for n in (3, 4, 5):
+            send_bank(1, n, zq, on_scalar)
+        zq = next_zq
+        pick(3, 2)
+        pick(3, 3)
+        send_bank(2, 0, zq, on_scalar)
+        sigmoid(3, 2, 2)
+        send_bank(2, 1, zq, on_scalar)
+        send_bank(2, 2, zq, on_scalar)
+        next_zq = make_z(3)
+        for n in (3, 4, 5):
+            send_bank(2, n, zq, on_vector if n == 5 else on_scalar)
+        for n in range(BANKS_A_CHUNK):
+            send_bank(3, n, next_zq, on_scalar if n == 4 else on_vector)

@@ -38,6 +38,7 @@ def tile_list_pipeline_stage_transfer_kernel(
         keep = ctx.enter_context(tc.tile_pool(name="keep", bufs=1))
         pair = ctx.enter_context(tc.tile_pool(name="pair", bufs=2))
         ring = ctx.enter_context(tc.tile_pool(name="ring", bufs=3))
+        shared = ctx.enter_context(tc.tile_pool(name="shared", bufs=1))
         stage = ctx.enter_context(tc.tile_pool(name="stage", bufs=8))
         psum = ctx.enter_context(tc.psum_pool(name="psum", bufs=1))
 
@@ -65,7 +66,6 @@ def tile_list_pipeline_stage_transfer_kernel(
         skip_sb = held([P, PACK, M_OUT], F32, "skip_sb")
         w3c = held([P, N_OUT], U32, "w3c")
         span = PACK * CHUNK
-        work = held([P, (CHUNKS + 1) * span + BANK], F32, "work")
         warm_in = held([P, 1], F32, "warm_in")
         warm_out = held([P, 1], F32, "warm_out")
 
@@ -209,30 +209,15 @@ def tile_list_pipeline_stage_transfer_kernel(
                 )
             return acc_a, acc_b
 
-        gates = [work[:, c * span : (c + 1) * span] for c in range(CHUNKS)]
-        first_x = work[:, CHUNKS * span : (CHUNKS + 1) * span]
-        last_sent = work[:, (CHUNKS + 1) * span :]
+        def placed(shape, dtype, name, offset):
+            return shared.tile(shape, dtype, name=name, offset=offset, align_bytes=64)
 
-        def quarter(region, k, n=1):
-            return region[:, k * CHUNK : (k + n) * CHUNK]
-
-        home = {(0, t): (first_x, t) for t in range(PACK)}
-        home[(1, 0)] = (last_sent, 0)
-        home[(2, 1)] = (last_sent, 0)
-        for k, piece in enumerate(((1, 1), (1, 2), (1, 3), (2, 0))):
-            home[piece] = (gates[0], k)
-        for k, piece in enumerate(((2, 2), (2, 3), (3, 0), (3, 1))):
-            home[piece] = (gates[1], k)
-        for k, piece in enumerate(((3, 2), (3, 3))):
-            home[piece] = (gates[2], k)
-
-        def pick(c, t):
+        def pick(c, t, target):
             slots = idx3[:, c * CHUNK // 16 : (c + 1) * CHUNK // 16]
-            nc.vector.tensor_copy(out=quarter(*home[(c, t)]), in_=pages[t][:].indirect(slots))
+            nc.vector.tensor_copy(out=target, in_=pages[t][:].indirect(slots))
 
-        def sigmoid(c, t, n=1):
-            region, k = home[(c, t)]
-            nc.scalar.activation(out=quarter(gates[c], t, n), in_=quarter(region, k, n), func=ACT.Sigmoid)
+        def sigmoid(gate, x):
+            nc.scalar.activation(out=gate, in_=x, func=ACT.Sigmoid)
 
         def scatter(t, lo, values):
             width = values.shape[1]
@@ -269,39 +254,43 @@ def tile_list_pipeline_stage_transfer_kernel(
             lin = pair.tile([P, BANK], F32, name="lin")
             nc.scalar.copy(out=lin[:], in_=acc_a[:])
             if last:
-                gel = gates[0][:, 0:BANK]
+                gel = held([P, BANK], F32, "gel_last")[:]
             elif u == 1:
                 gel = held([P, BANK], F32, "gel_second")[:]
             else:
                 gel = ring.tile([P, BANK], F32, name="gel")[:]
             nc.scalar.activation(out=gel, in_=acc_b[:], func=ACT.Gelu_apprx_tanh, bias=bias[:, t : t + 1])
-            sent = last_sent if last else ring.tile([P, BANK], F32, name="sent")[:]
+            sent = held([P, BANK], F32, "sent_last")[:] if last else ring.tile([P, BANK], F32, name="sent")[:]
             weigh_on_gpsimd(lin[:], gel, weight, sent)
             if last:
-                for early in range(PACK - 1):
-                    pick(0, early)
-                sigmoid(0, 0, PACK - 1)
+                early = PACK - 1
+                x_early = held([P, early, CHUNK], F32, "x_early")
+                for slot in range(early):
+                    pick(0, slot, x_early[:, slot, :])
+                gate_early = held([P, early, CHUNK], F32, "gate_early", "gel_last")
+                sigmoid(gate_early[:], x_early[:])
+                rows = [placed([P, PACK, CHUNK], BF16, "rows0", 512)]
+                nc.gpsimd.tensor_tensor(
+                    out=rows[0][:, 0:early, :], in0=gate_early[:], in1=skip_sb[:, 0:early, 0:CHUNK], op=ALU.mult
+                )
             scatter(t, half * BANK, sent)
             if u == 1:
                 quantize_w2(cast_w2(nc.scalar.copy, 2, 2, PACK, "gel_second"), 2, 2, PACK)
 
         out_rows = out.rearrange("(b p) m -> p b m", p=P)
 
-        def make_z(c):
-            cols = slice(c * CHUNK, (c + 1) * CHUNK)
-            z = ring.tile([P, span], BF16, name="z", align_bytes=64)
-            nc.vector.tensor_tensor(
-                out=z[:].rearrange("p (n i t) -> p n t i", i=2, t=PACK),
-                in0=gates[c].rearrange("p (t n i) -> p n t i", t=PACK, i=2),
-                in1=skip_sb[:, :, cols].rearrange("p t (n i) -> p n t i", i=2),
-                op=ALU.mult,
+        def make_z(c, z, zc=None, zs=None):
+            nc.vector.tensor_copy(
+                out=z[:].rearrange("p (n i t) -> p n t i", i=PACK, t=PACK),
+                in_=rows[c][:].rearrange("p t (n i) -> p n t i", i=PACK),
             )
-            zc = ring.tile([P, CHUNK], U32, name="zc", align_bytes=64)
-            zs = ring.tile([P, CHUNK], U8, name="zs", align_bytes=64)
+            if zc is None:
+                zc = ring.tile([P, CHUNK], U32, name="zc", align_bytes=64)
+                zs = ring.tile([P, CHUNK], U8, name="zs", align_bytes=64)
             nc.vector.quantize_mx(out=zc[:].bitcast(FP8X4), scales=zs[:], in_=z[:])
             return zc, zs
 
-        def send_bank(c, n, zq, copy):
+        def fill_bank(c, n, zq):
             zc, zs = zq
             acc = psum.tile([P, PER_BANK, CHUNK], F32, name="acc", tag="bank%d" % ((c * BANKS_A_CHUNK + n) % 8))
             for e in range(PER_BANK):
@@ -315,6 +304,12 @@ def tile_list_pipeline_stage_transfer_kernel(
                     start=True,
                     stop=True,
                 )
+            return acc
+
+        def send_bank(c, n, zq, copy):
+            empty_bank(c, n, fill_bank(c, n, zq), copy)
+
+        def empty_bank(c, n, acc, copy):
             staged = stage.tile([P, PER_BANK, CHUNK], F32, name="staged")
             copy(out=staged[:], in_=acc[:])
             nc.sync.dma_start(
@@ -323,44 +318,70 @@ def tile_list_pipeline_stage_transfer_kernel(
 
         on_scalar, on_vector = nc.scalar.copy, nc.vector.tensor_copy
 
-        pick(0, 3)
-        sigmoid(0, 3)
-        pick(1, 0)
-        sigmoid(1, 0)
-        zq = make_z(0)
-        for c, t in ((1, 1), (1, 2), (2, 0), (1, 3)):
-            pick(c, t)
-        send_bank(0, 0, zq, on_scalar)
-        send_bank(0, 1, zq, on_scalar)
-        sigmoid(1, 1, 3)
-        send_bank(0, 2, zq, on_scalar)
-        pick(2, 1)
-        next_zq = make_z(1)
-        send_bank(0, 3, zq, on_scalar)
-        sigmoid(2, 0)
-        sigmoid(2, 1)
-        send_bank(0, 4, zq, on_scalar)
-        send_bank(0, 5, zq, on_scalar)
-        zq = next_zq
-        for c, t in ((2, 2), (2, 3), (3, 0), (3, 1)):
-            pick(c, t)
-        send_bank(1, 0, zq, on_scalar)
-        sigmoid(2, 2, 2)
-        send_bank(1, 1, zq, on_scalar)
-        send_bank(1, 2, zq, on_scalar)
-        next_zq = make_z(2)
-        sigmoid(3, 0, 2)
-        for n in (3, 4, 5):
-            send_bank(1, n, zq, on_scalar)
-        zq = next_zq
-        pick(3, 2)
-        pick(3, 3)
-        send_bank(2, 0, zq, on_scalar)
-        sigmoid(3, 2, 2)
-        send_bank(2, 1, zq, on_scalar)
-        send_bank(2, 2, zq, on_scalar)
-        next_zq = make_z(3)
-        for n in (3, 4, 5):
-            send_bank(2, n, zq, on_vector if n == 5 else on_scalar)
-        for n in range(BANKS_A_CHUNK):
-            send_bank(3, n, next_zq, on_scalar if n == 4 else on_vector)
+        piece = 4 * CHUNK
+        x, gate = {}, {}
+
+        def fetch(c, t, slot):
+            x[(c, t)] = placed([P, CHUNK], F32, "x%d%d" % (c, t), slot * piece)[:]
+            pick(c, t, x[(c, t)])
+
+        def product(engine, c, lo, hi, gates):
+            engine.tensor_tensor(
+                out=rows[c][:, lo:hi, :], in0=gates, in1=skip_sb[:, lo:hi, c * CHUNK : (c + 1) * CHUNK], op=ALU.mult
+            )
+
+        def gated(c, t, slot, engine=nc.gpsimd):
+            gate = placed([P, 1, CHUNK], F32, "gate%d%d" % (c, t), slot * piece)
+            sigmoid(gate[:, 0, :], x[(c, t)])
+            product(engine, c, t, t + 1, gate[:])
+
+        rows.append(placed([P, PACK, CHUNK], BF16, "rows1", 6 * piece))
+        rows.append(held([P, PACK, CHUNK], BF16, "rows2"))
+        rows.append(held([P, PACK, CHUNK], BF16, "rows3"))
+        last_gates = held([P, PACK, CHUNK], F32, "last_gates", "w2_raw0")
+
+        fetch(0, 3, 11)
+        x[(1, 0)] = held([P, CHUNK], F32, "x10", "sent_last")[:]
+        pick(1, 0, x[(1, 0)])
+        gated(0, 3, 12, nc.vector)
+        gated(1, 0, 13)
+        zq0 = make_z(
+            0,
+            placed([P, span], BF16, "z0", 3 * piece + 512),
+            placed([P, CHUNK], U32, "zc0", 8 * piece + 512),
+            placed([P, CHUNK], U8, "zs0", 10 * piece),
+        )
+        for slot, (c, t) in enumerate(((1, 1), (1, 2), (1, 3), (2, 0), (2, 1), (2, 2))):
+            fetch(c, t, slot)
+        for n in range(4):
+            send_bank(0, n, zq0, on_scalar)
+        later = [fill_bank(0, n, zq0) for n in (4, 5)]
+        for t in range(1, PACK):
+            gated(1, t, 7 + t)
+        fetch(2, 3, 0)
+        fetch(3, 0, 1)
+        fetch(3, 1, 2)
+        zq1 = make_z(1, held([P, span], BF16, "z1"))
+        fetch(3, 2, 6)
+        fetch(3, 3, 7)
+        empty_bank(0, 4, later[0], on_scalar)
+        gated(2, 0, 8)
+        gated(2, 1, 9)
+        empty_bank(0, 5, later[1], on_scalar)
+        gated(2, 2, 10)
+        gated(2, 3, 8)
+        zq2 = make_z(2, held([P, span], BF16, "z2"))
+        sigmoid(last_gates[:, 0, :], x[(3, 0)])
+        sigmoid(last_gates[:, 1, :], x[(3, 1)])
+        send_bank(1, 0, zq1, on_scalar)
+        sigmoid(last_gates[:, 2, :], x[(3, 2)])
+        sigmoid(last_gates[:, 3, :], x[(3, 3)])
+        send_bank(1, 1, zq1, on_vector)
+        product(nc.vector, 3, 0, PACK, last_gates[:])
+        send_bank(1, 2, zq1, on_scalar)
+        zq3 = make_z(3, held([P, span], BF16, "z3"))
+        for n in range(3, BANKS_A_CHUNK):
+            send_bank(1, n, zq1, on_scalar)
+        for c, zq in ((2, zq2), (3, zq3)):
+            for n in range(BANKS_A_CHUNK):
+                send_bank(c, n, zq, on_scalar if n % 2 else on_vector)

@@ -59,9 +59,9 @@ def tile_list_pipeline_stage_transfer_kernel(
         w1s = held([P, PASSES, H], U8, "w1s")
         w2_raw = [held([P, PACK, H], F32, "w2_raw%d" % a) for a in range(PASSES)]
         bias = held([P, PACK], F32, "bias")
-        wg_a = held([P, 1, CHUNK], F32, "wg_a")
-        wg_b = held([P, 1, S - CHUNK], F32, "wg_b")
-        wg_second = held([P, 1, S], F32, "wg_second")
+        wg_a = held([P, 1, BANK], F32, "wg_a")
+        wg_b = held([P, 1, BANK], F32, "wg_b")
+        wg_c = held([P, 2, BANK], F32, "wg_c")
         wg_rest = held([P, 2, S], F32, "wg_rest")
         skip_sb = held([P, PACK, M_OUT], F32, "skip_sb")
         w3c = held([P, N_OUT], U32, "w3c")
@@ -146,9 +146,9 @@ def tile_list_pipeline_stage_transfer_kernel(
         nc.sync.dma_start(idx2[:], offs2)
         load_w2(2)
         for tile, lo, hi, c0, c1 in (
-            (wg_a, 0, 1, 0, CHUNK),
-            (wg_b, 0, 1, CHUNK, S),
-            (wg_second, 1, 2, 0, S),
+            (wg_a, 0, 1, 0, BANK),
+            (wg_b, 1, 2, 0, BANK),
+            (wg_c, 0, 2, BANK, S),
             (wg_rest, 2, PACK, 0, S),
         ):
             for q in (0, 2, 1, 3):
@@ -176,10 +176,10 @@ def tile_list_pipeline_stage_transfer_kernel(
         v.append(gather_words(2, 0, BANK))
         quantize_w2(grouped1, 1, 0, PACK)
         quantize_w2(cast_w2(nc.vector.tensor_copy, 2, 0, 1), 2, 0, 1)
+        quantize_w2(cast_w2(nc.scalar.copy, 2, 1, 2), 2, 1, 2)
         v[2].extend(gather_words(2, BANK, S, "w2_bf2_0"))
-        grouped2 = cast_w2(nc.scalar.copy, 2, 1, 2)
 
-        units = [(t, half) for t in range(PACK) for half in range(HALVES)]
+        units = [(0, 0), (1, 0), (0, 1), (2, 0), (1, 1), (2, 1), (3, 0), (3, 1)]
 
         def make_h(u):
             t, half = units[u]
@@ -208,6 +208,8 @@ def tile_list_pipeline_stage_transfer_kernel(
                     stop=(a == PASSES - 1),
                 )
             return acc_a, acc_b
+
+        piece = 4 * CHUNK
 
         def placed(shape, dtype, name, offset):
             return shared.tile(shape, dtype, name=name, offset=offset, align_bytes=64)
@@ -239,56 +241,59 @@ def tile_list_pipeline_stage_transfer_kernel(
         h_first = held([P, CHUNK], F32, "h_first")
         sent = ring.tile([P, BANK], F32, name="sent")
         nc.vector.tensor_tensor(out=h_first[:], in0=acc_a[:, 0:CHUNK], in1=gel[:, 0:CHUNK], op=ALU.add)
-        nc.vector.tensor_tensor(out=sent[:, 0:CHUNK], in0=h_first[:], in1=wg_a[:, 0, :], op=ALU.mult)
+        nc.vector.tensor_tensor(out=sent[:, 0:CHUNK], in0=h_first[:], in1=wg_a[:, 0, 0:CHUNK], op=ALU.mult)
         scatter(0, 0, sent[:, 0:CHUNK])
-        weigh_on_gpsimd(lin[:, 0:CHUNK], gel[:, CHUNK:BANK], wg_b[:, 0, 0:CHUNK], sent[:, CHUNK:BANK])
-        quantize_w2(grouped2, 2, 1, 2)
+        weigh_on_gpsimd(lin[:, 0:CHUNK], gel[:, CHUNK:BANK], wg_a[:, 0, CHUNK:BANK], sent[:, CHUNK:BANK])
         scatter(0, CHUNK, sent[:, CHUNK:BANK])
 
-        wg = [None, wg_second[:, 0, :], wg_rest[:, 0, :], wg_rest[:, 1, :]]
+        wg = {(1, 0): wg_b[:, 0, :], (0, 1): wg_c[:, 0, :], (1, 1): wg_c[:, 1, :]}
+        for t, half in [unit for unit in units if unit[0] >= 2]:
+            wg[(t, half)] = wg_rest[:, t - 2, half * BANK : (half + 1) * BANK]
         for u in range(1, len(units)):
             t, half = units[u]
             last = u == len(units) - 1
-            weight = wg_b[:, 0, BANK - CHUNK :] if t == 0 else wg[t][:, half * BANK : (half + 1) * BANK]
+            weight = wg[(t, half)]
             acc_a, acc_b = make_h(u)
             lin = pair.tile([P, BANK], F32, name="lin")
             nc.scalar.copy(out=lin[:], in_=acc_a[:])
             if last:
-                gel = held([P, BANK], F32, "gel_last")[:]
-            elif u == 1:
-                gel = held([P, BANK], F32, "gel_second")[:]
+                gel = placed([P, BANK], F32, "gel_last", 0)[:]
             else:
                 gel = ring.tile([P, BANK], F32, name="gel")[:]
             nc.scalar.activation(out=gel, in_=acc_b[:], func=ACT.Gelu_apprx_tanh, bias=bias[:, t : t + 1])
-            sent = held([P, BANK], F32, "sent_last")[:] if last else ring.tile([P, BANK], F32, name="sent")[:]
+            if last:
+                sent = held([P, BANK], F32, "sent_last")[:]
+            elif u == len(units) - 2:
+                sent = held([P, BANK], F32, "sent_before_last", "x_first")[:]
+            else:
+                sent = ring.tile([P, BANK], F32, name="sent")[:]
             weigh_on_gpsimd(lin[:], gel, weight, sent)
             if last:
                 early = PACK - 1
-                x_early = held([P, early, CHUNK], F32, "x_early")
+                x_first = held([P, PACK, CHUNK], F32, "x_first")
                 for slot in range(early):
-                    pick(0, slot, x_early[:, slot, :])
-                gate_early = held([P, early, CHUNK], F32, "gate_early", "gel_last")
-                sigmoid(gate_early[:], x_early[:])
-                rows = [placed([P, PACK, CHUNK], BF16, "rows0", 512)]
-                nc.gpsimd.tensor_tensor(
-                    out=rows[0][:, 0:early, :], in0=gate_early[:], in1=skip_sb[:, 0:early, 0:CHUNK], op=ALU.mult
-                )
+                    pick(0, slot, x_first[:, slot, :])
+                gates = [placed([P, PACK, CHUNK], F32, "gate0", 0)]
+                sigmoid(gates[0][:, 0, :], x_first[:, 0, :])
+                sigmoid(gates[0][:, 1:early, :], x_first[:, 1:early, :])
             scatter(t, half * BANK, sent)
             if u == 1:
-                quantize_w2(cast_w2(nc.scalar.copy, 2, 2, PACK, "gel_second"), 2, 2, PACK)
+                quantize_w2(cast_w2(nc.scalar.copy, 2, 2, PACK, "gel_first"), 2, 2, PACK)
 
         out_rows = out.rearrange("(b p) m -> p b m", p=P)
 
-        def make_z(c, z, zc=None, zs=None):
-            nc.vector.tensor_copy(
-                out=z[:].rearrange("p (n i t) -> p n t i", i=PACK, t=PACK),
-                in_=rows[c][:].rearrange("p t (n i) -> p n t i", i=PACK),
+        def make_z(c, z, zc, zs):
+            nc.vector.tensor_tensor(
+                out=z[:].rearrange("p (n i t) -> p n t i", i=2, t=PACK),
+                in0=gates[c][:].rearrange("p t (n i) -> p n t i", i=2),
+                in1=skip_sb[:, :, c * CHUNK : (c + 1) * CHUNK].rearrange("p t (n i) -> p n t i", i=2),
+                op=ALU.mult,
             )
-            if zc is None:
-                zc = ring.tile([P, CHUNK], U32, name="zc", align_bytes=64)
-                zs = ring.tile([P, CHUNK], U8, name="zs", align_bytes=64)
             nc.vector.quantize_mx(out=zc[:].bitcast(FP8X4), scales=zs[:], in_=z[:])
             return zc, zs
+
+        def operand(c):
+            return held([P, CHUNK], U32, "zc%d" % c), held([P, CHUNK], U8, "zs%d" % c)
 
         def fill_bank(c, n, zq):
             zc, zs = zq
@@ -318,70 +323,55 @@ def tile_list_pipeline_stage_transfer_kernel(
 
         on_scalar, on_vector = nc.scalar.copy, nc.vector.tensor_copy
 
-        piece = 4 * CHUNK
-        x, gate = {}, {}
+        x = {}
 
-        def fetch(c, t, slot):
-            x[(c, t)] = placed([P, CHUNK], F32, "x%d%d" % (c, t), slot * piece)[:]
-            pick(c, t, x[(c, t)])
+        def fetch(tile, keys):
+            for k, key in enumerate(keys):
+                x[key] = tile[:, k, :]
+                pick(*key, x[key])
 
-        def product(engine, c, lo, hi, gates):
-            engine.tensor_tensor(
-                out=rows[c][:, lo:hi, :], in0=gates, in1=skip_sb[:, lo:hi, c * CHUNK : (c + 1) * CHUNK], op=ALU.mult
-            )
+        def gate(c, t):
+            sigmoid(gates[c][:, t, :], x[(c, t)])
 
-        def gated(c, t, slot, engine=nc.gpsimd):
-            gate = placed([P, 1, CHUNK], F32, "gate%d%d" % (c, t), slot * piece)
-            sigmoid(gate[:, 0, :], x[(c, t)])
-            product(engine, c, t, t + 1, gate[:])
-
-        rows.append(placed([P, PACK, CHUNK], BF16, "rows1", 6 * piece))
-        rows.append(held([P, PACK, CHUNK], BF16, "rows2"))
-        rows.append(held([P, PACK, CHUNK], BF16, "rows3"))
-        last_gates = held([P, PACK, CHUNK], F32, "last_gates", "w2_raw0")
-
-        fetch(0, 3, 11)
-        x[(1, 0)] = held([P, CHUNK], F32, "x10", "sent_last")[:]
-        pick(1, 0, x[(1, 0)])
-        gated(0, 3, 12, nc.vector)
-        gated(1, 0, 13)
+        pick(0, 3, x_first[:, 3, :])
+        sigmoid(gates[0][:, 3, :], x_first[:, 3, :])
+        fetch(held([P, 1, CHUNK], F32, "x10", "sent_last"), [(1, 0)])
+        gates.append(placed([P, PACK, CHUNK], F32, "gate1", 8 * piece))
+        gate(1, 0)
         zq0 = make_z(
             0,
-            placed([P, span], BF16, "z0", 3 * piece + 512),
-            placed([P, CHUNK], U32, "zc0", 8 * piece + 512),
-            placed([P, CHUNK], U8, "zs0", 10 * piece),
+            placed([P, span], BF16, "z0", 4 * piece),
+            placed([P, CHUNK], U32, "zc0", 12 * piece),
+            held([P, CHUNK], U8, "zs0"),
         )
-        for slot, (c, t) in enumerate(((1, 1), (1, 2), (1, 3), (2, 0), (2, 1), (2, 2))):
-            fetch(c, t, slot)
-        for n in range(4):
-            send_bank(0, n, zq0, on_scalar)
-        later = [fill_bank(0, n, zq0) for n in (4, 5)]
+        fetch(placed([P, 3, CHUNK], F32, "x1", 4 * piece), [(1, 1), (1, 2), (1, 3)])
         for t in range(1, PACK):
-            gated(1, t, 7 + t)
-        fetch(2, 3, 0)
-        fetch(3, 0, 1)
-        fetch(3, 1, 2)
-        zq1 = make_z(1, held([P, span], BF16, "z1"))
-        fetch(3, 2, 6)
-        fetch(3, 3, 7)
-        empty_bank(0, 4, later[0], on_scalar)
-        gated(2, 0, 8)
-        gated(2, 1, 9)
-        empty_bank(0, 5, later[1], on_scalar)
-        gated(2, 2, 10)
-        gated(2, 3, 8)
-        zq2 = make_z(2, held([P, span], BF16, "z2"))
-        sigmoid(last_gates[:, 0, :], x[(3, 0)])
-        sigmoid(last_gates[:, 1, :], x[(3, 1)])
+            gate(1, t)
+        send_bank(0, 0, zq0, on_vector)
+        zq1 = make_z(1, placed([P, span], BF16, "z1", 18 * piece), *operand(1))
+        for n in range(1, BANKS_A_CHUNK):
+            send_bank(0, n, zq0, on_scalar)
+        fetch(placed([P, 6, CHUNK], F32, "x2", 12 * piece + 512), [divmod(k, PACK) for k in range(8, 14)])
+        gates.append(placed([P, PACK, CHUNK], F32, "gate2", 0))
+        gates.append(placed([P, PACK, CHUNK], F32, "gate3", 8 * piece))
         send_bank(1, 0, zq1, on_scalar)
-        sigmoid(last_gates[:, 2, :], x[(3, 2)])
-        sigmoid(last_gates[:, 3, :], x[(3, 3)])
-        send_bank(1, 1, zq1, on_vector)
-        product(nc.vector, 3, 0, PACK, last_gates[:])
+        gate(2, 0)
+        send_bank(1, 1, zq1, on_scalar)
+        for t in range(1, PACK):
+            gate(2, t)
+        zq2 = make_z(2, placed([P, span], BF16, "z2", 4 * piece), *operand(2))
+        fetch(placed([P, 2, CHUNK], F32, "x3", 4 * piece), [(3, 2), (3, 3)])
         send_bank(1, 2, zq1, on_scalar)
-        zq3 = make_z(3, held([P, span], BF16, "z3"))
-        for n in range(3, BANKS_A_CHUNK):
-            send_bank(1, n, zq1, on_scalar)
-        for c, zq in ((2, zq2), (3, zq3)):
-            for n in range(BANKS_A_CHUNK):
-                send_bank(c, n, zq, on_scalar if n % 2 else on_vector)
+        send_bank(1, 3, zq1, on_scalar)
+        gate(3, 0)
+        gate(3, 1)
+        send_bank(1, 4, zq1, on_scalar)
+        send_bank(1, 5, zq1, on_scalar)
+        gate(3, 2)
+        gate(3, 3)
+        send_bank(2, 0, zq2, on_vector)
+        zq3 = make_z(3, held([P, span], BF16, "z3"), *operand(3))
+        for n in range(1, BANKS_A_CHUNK):
+            send_bank(2, n, zq2, on_vector if n == 5 else on_scalar)
+        for n in range(BANKS_A_CHUNK):
+            send_bank(3, n, zq3, on_scalar if n % 2 else on_vector)

@@ -100,8 +100,8 @@ def tile_list_pipeline_stage_transfer_kernel(
             )
             return grouped
 
-        def quantize_w2(grouped, a, lo, hi):
-            codes = held([P, (hi - lo) * P], U32, "w2c%d_%d" % (a, lo))
+        def quantize_w2(grouped, a, lo, hi, tag=None):
+            codes = held([P, (hi - lo) * P], U32, "w2c%d_%d" % (a, lo), tag)
             scales = held([P, (hi - lo) * P], U8, "w2s%d_%d" % (a, lo))
             nc.vector.quantize_mx(out=codes[:].bitcast(FP8X4), scales=scales[:], in_=grouped[:])
             for t in range(lo, hi):
@@ -138,13 +138,13 @@ def tile_list_pipeline_stage_transfer_kernel(
             out=w1s[:].rearrange("p a (t m) -> p t a m", t=PACK),
             in_=w1_raw_s[:].rearrange("p a (m t) -> p t a m", t=PACK),
         )
+        load_w2(2)
         for a in range(1, PASSES):
             nc.sync.dma_start(
                 out=v_s_down[0:112, (a - 1) * S : a * S].bitcast(I32), in_=v_s[4 * a : 4 * a + 112, :].bitcast(I32)
             )
         nc.sync.dma_start(out=bias[:], in_=b2.rearrange("(p t) -> p t", t=PACK))
         nc.sync.dma_start(idx2[:], offs2)
-        load_w2(2)
         for tile, lo, hi, c0, c1 in (
             (wg_a, 0, 1, 0, BANK),
             (wg_b, 1, 2, 0, BANK),
@@ -239,7 +239,7 @@ def tile_list_pipeline_stage_transfer_kernel(
                 out=gel[:, lo : lo + CHUNK], in_=acc_b[:, lo : lo + CHUNK], func=ACT.Gelu_apprx_tanh, bias=bias[:, 0:1]
             )
         h_first = held([P, CHUNK], F32, "h_first")
-        sent = ring.tile([P, BANK], F32, name="sent")
+        sent = held([P, BANK], F32, "sent_first")
         nc.vector.tensor_tensor(out=h_first[:], in0=acc_a[:, 0:CHUNK], in1=gel[:, 0:CHUNK], op=ALU.add)
         nc.vector.tensor_tensor(out=sent[:, 0:CHUNK], in0=h_first[:], in1=wg_a[:, 0, 0:CHUNK], op=ALU.mult)
         scatter(0, 0, sent[:, 0:CHUNK])
@@ -268,6 +268,8 @@ def tile_list_pipeline_stage_transfer_kernel(
             else:
                 sent = ring.tile([P, BANK], F32, name="sent")[:]
             weigh_on_gpsimd(lin[:], gel, weight, sent)
+            if u == 1:
+                quantize_w2(cast_w2(nc.scalar.copy, 2, 2, PACK, "gel_first"), 2, 2, PACK, "sent_first")
             if last:
                 early = PACK - 1
                 x_first = held([P, PACK, CHUNK], F32, "x_first")
@@ -277,8 +279,6 @@ def tile_list_pipeline_stage_transfer_kernel(
                 sigmoid(gates[0][:, 0, :], x_first[:, 0, :])
                 sigmoid(gates[0][:, 1:early, :], x_first[:, 1:early, :])
             scatter(t, half * BANK, sent)
-            if u == 1:
-                quantize_w2(cast_w2(nc.scalar.copy, 2, 2, PACK, "gel_first"), 2, 2, PACK)
 
         out_rows = out.rearrange("(b p) m -> p b m", p=P)
 

@@ -1,6 +1,7 @@
 from contextlib import ExitStack
 
 import concourse.mybir as mybir
+from concourse.masks import make_identity
 
 K, T, S, H, T2, M_OUT, N_OUT = 1536, 2048, 1024, 512, 2048, 1024, 1536
 FLOPS = 2 * (2 * K * H * S + H * N_OUT * M_OUT)
@@ -20,13 +21,15 @@ P = 128
 PACK = 4
 PASSES = K // (P * PACK)
 QUADS = 4
+PAGES = H // P
 BANK = 512
-HALVES = S // BANK
 CHUNK = 256
 CHUNKS = M_OUT // CHUNK
+SIDES = CHUNK // P
 BLOCKS = N_OUT // P
 PER_BANK = BANK // CHUNK
 BANKS_A_CHUNK = BLOCKS // PER_BANK
+WIDE = H // 2
 
 
 def tile_list_pipeline_stage_transfer_kernel(
@@ -38,7 +41,6 @@ def tile_list_pipeline_stage_transfer_kernel(
         keep = ctx.enter_context(tc.tile_pool(name="keep", bufs=1))
         pair = ctx.enter_context(tc.tile_pool(name="pair", bufs=2))
         ring = ctx.enter_context(tc.tile_pool(name="ring", bufs=3))
-        shared = ctx.enter_context(tc.tile_pool(name="shared", bufs=1))
         stage = ctx.enter_context(tc.tile_pool(name="stage", bufs=8))
         psum = ctx.enter_context(tc.psum_pool(name="psum", bufs=1))
 
@@ -53,251 +55,257 @@ def tile_list_pipeline_stage_transfer_kernel(
         tab_s = held([P, T], U8, "tab_s")
         v_s = held([P, S], U8, "v_s")
         v_s_down = held([P, (PASSES - 1) * S], U8, "v_s_down")
-        w1_raw = held([P, PASSES, 2 * H], U8, "w1_raw")
-        w1_raw_s = held([P, PASSES, H], U8, "w1_raw_s")
         w1c = held([P, PASSES, 2 * H], U8, "w1c")
         w1s = held([P, PASSES, H], U8, "w1s")
-        w2_raw = [held([P, PACK, H], F32, "w2_raw%d" % a) for a in range(PASSES)]
-        bias = held([P, PACK], F32, "bias")
-        wg_a = held([P, 1, BANK], F32, "wg_a")
-        wg_b = held([P, 1, BANK], F32, "wg_b")
-        wg_c = held([P, 2, BANK], F32, "wg_c")
-        wg_rest = held([P, 2, S], F32, "wg_rest")
-        skip_sb = held([P, PACK, M_OUT], F32, "skip_sb")
+        bias = held([P, PAGES], F32, "bias")
+        wg = [held([P, BANK], F32, "wg%d" % half) for half in range(2)]
+        skips = [held([P, PACK, CHUNK], F32, "skip%d" % c) for c in range(CHUNKS)]
         w3c = held([P, N_OUT], U32, "w3c")
-        span = PACK * CHUNK
-        warm_in = held([P, 1], F32, "warm_in")
+        w3s = held([P, N_OUT], U8, "w3s")
+        ident = held([P, P], F32, "ident")
         warm_out = held([P, 1], F32, "warm_out")
 
-        nc.gpsimd.memset(warm_in[:], 0.0)
-        nc.scalar.activation(out=warm_out[:], in_=warm_in[:], func=ACT.Gelu_apprx_tanh)
-
         nc.vector.memset(tab_s[:].bitcast(I32), 0)
-        nc.vector.memset(w1_raw_s[:].bitcast(I32), 0)
+        nc.vector.memset(w1s[:].bitcast(I32), 0)
         nc.vector.memset(v_s_down[:].bitcast(I32), 0)
-        pages = [held([P, T2], F32, "page0")]
-        nc.vector.memset(pages[0][:], 0.0)
+        nc.vector.memset(w3s[:].bitcast(I32), 0)
+        make_identity(nc, ident[:])
+        nc.scalar.activation(out=warm_out[:], in_=ident[:, 0:1], func=ACT.Gelu_apprx_tanh)
+
+        pages = []
+
+        def clear_page(tag=None):
+            page = held([P, T2], F32, "page%d" % len(pages), tag)
+            for lo in range(0, T2, BANK):
+                nc.gpsimd.memset(page[:, lo : lo + BANK], 0.0)
+            pages.append(page)
+
+        for u in range(PAGES):
+            clear_page()
 
         def load_tab(a):
             nc.sync.dma_start(out=tab[a][:].bitcast(I32), in_=tab_words[a].rearrange("p t i -> p (t i)").bitcast(I32))
 
-        def load_w2(a):
-            rows = w2[a * P * PACK : (a + 1) * P * PACK, :]
-            nc.sync.dma_start(out=w2_raw[a][:], in_=rows.rearrange("(p j) c -> p j c", j=PACK))
+        def load_w2(a, lo, hi):
+            raw = held([P, PACK, (hi - lo) * P], F32, "w2_raw%d_%d" % (a, lo))
+            rows = w2[a * P * PACK : (a + 1) * P * PACK, lo * P : hi * P]
+            nc.sync.dma_start(out=raw[:], in_=rows.rearrange("(p j) c -> p j c", j=PACK))
+            return raw
+
+        def load_scales(queues, plane, rows, scales):
+            for q, queue in enumerate(queues):
+                queue(out=plane[32 * q : 32 * q + rows].bitcast(I32), in_=scales(4 * q, 4 * q + 4).bitcast(I32))
+
+        v = {}
 
         def gather_words(a, lo, hi, tag=None):
-            words = held([P, hi - lo], U32, "v%d_%d" % (a, lo), tag)
-            nc.vector.tensor_copy(out=words[:], in_=tab[a][:].indirect(idx[:, lo // 16 : hi // 16]))
-            return [words[:, c - lo : c - lo + BANK] for c in range(lo, hi, BANK)]
+            words = held([P, (hi - lo) * BANK], U32, "v%d_%d" % (a, lo), tag)
+            nc.vector.tensor_copy(out=words[:], in_=tab[a][:].indirect(idx[:, lo * BANK // 16 : hi * BANK // 16]))
+            for half in range(lo, hi):
+                v[(a, half)] = words[:, (half - lo) * BANK : (half - lo + 1) * BANK]
+
+        def cast_w2(raw, target):
+            nc.scalar.copy(
+                out=target.rearrange("p (c i j) -> p c j i", i=4, j=PACK),
+                in_=raw.rearrange("p j (c i) -> p c j i", i=4),
+            )
 
         w2q = {}
 
-        def cast_w2(copy, a, lo, hi, tag=None):
-            grouped = held([P, (hi - lo) * P * PACK], BF16, "w2_bf%d_%d" % (a, lo), tag)
-            copy(
-                out=grouped[:].rearrange("p (t m j) -> p m t j", m=P, j=PACK),
-                in_=w2_raw[a][:].rearrange("p j (m t) -> p m t j", t=PACK)[:, :, lo:hi, :],
-            )
-            return grouped
-
-        def quantize_w2(grouped, a, lo, hi, tag=None):
-            codes = held([P, (hi - lo) * P], U32, "w2c%d_%d" % (a, lo), tag)
-            scales = held([P, (hi - lo) * P], U8, "w2s%d_%d" % (a, lo))
+        def quantize_w2(grouped, keys, tag=None):
+            name = "%d_%d" % keys[0]
+            codes = held([P, len(keys) * P], U32, "w2c" + name, tag)
+            scales = held([P, len(keys) * P], U8, "w2s" + name)
             nc.vector.quantize_mx(out=codes[:].bitcast(FP8X4), scales=scales[:], in_=grouped[:])
-            for t in range(lo, hi):
-                cols = slice((t - lo) * P, (t - lo + 1) * P)
-                w2q[(a, t)] = (codes[:, cols], scales[:, cols])
+            for n, key in enumerate(keys):
+                w2q[key] = (codes[:, n * P : (n + 1) * P], scales[:, n * P : (n + 1) * P])
 
-        wgs_rows = wgs.rearrange("(m t) j -> m t j", t=PACK)
+        def prepare_w2(raws, keys, tag=None, codes_tag=None):
+            grouped = held([P, len(keys) * P * PACK], BF16, "w2_bf%d_%d" % keys[0], tag)
+            width = len(keys) * P * PACK // len(raws)
+            for n, raw in enumerate(raws):
+                cast_w2(raw, grouped[:, n * width : (n + 1) * width])
+            quantize_w2(grouped, keys, codes_tag)
 
         nc.sync.dma_start(idx[:], offs)
-        nc.sync.dma_start(out=w1_raw[:].bitcast(I32), in_=w1_words.rearrange("a p c -> p a c").bitcast(I32))
         load_tab(0)
-        for q in range(QUADS):
-            nc.sync.dma_start(
-                out=tab_s[32 * q : 32 * q + 4 * PASSES, :].bitcast(I32),
-                in_=tab_scales[:, 4 * q : 4 * q + 4, :].bitcast(I32),
-            )
-        load_w2(0)
-        for q in range(QUADS):
-            nc.sync.dma_start(
-                out=w1_raw_s[32 * q : 32 * q + 4, :, :].bitcast(I32),
-                in_=w1_scales[:, 4 * q : 4 * q + 4, :].rearrange("a r c -> r a c").bitcast(I32),
-            )
+        on_sync = nc.sync.dma_start
         load_tab(1)
-        load_w2(1)
+        load_scales(4 * [on_sync], tab_s, 4 * PASSES, lambda lo, hi: tab_scales[:, lo:hi, :])
         load_tab(2)
-
-        nc.vector.tensor_copy(
-            out=w1c[:].bitcast(U16).rearrange("p a (t m) -> p t a m", t=PACK),
-            in_=w1_raw[:].bitcast(U16).rearrange("p a (m t) -> p t a m", t=PACK),
-        )
-        v = [gather_words(0, 0, S)]
+        raw_first = [load_w2(0, 0, 2)]
+        raw_first.append(load_w2(1, 0, 2))
+        gather_words(0, 0, 2)
         nc.vector.tensor_copy(out=v_s[:], in_=tab_s[:].indirect(idx[:]))
-        nc.vector.tensor_copy(
-            out=w1s[:].rearrange("p a (t m) -> p t a m", t=PACK),
-            in_=w1_raw_s[:].rearrange("p a (m t) -> p t a m", t=PACK),
-        )
-        load_w2(2)
+        load_scales(4 * [on_sync], w1s, 4, lambda lo, hi: w1_scales[:, lo:hi, :].rearrange("a r c -> r a c"))
+        raw_first.append(load_w2(2, 0, 2))
+        nc.sync.dma_start(out=w1c[:].bitcast(I32), in_=w1_words.rearrange("a p c -> p a c").bitcast(I32))
         for a in range(1, PASSES):
             nc.sync.dma_start(
                 out=v_s_down[0:112, (a - 1) * S : a * S].bitcast(I32), in_=v_s[4 * a : 4 * a + 112, :].bitcast(I32)
             )
-        nc.sync.dma_start(out=bias[:], in_=b2.rearrange("(p t) -> p t", t=PACK))
+        with nc.allow_non_contiguous_dma(reason="one bias value a partition and page"):
+            nc.sync.dma_start(out=bias[:], in_=b2.rearrange("(u p) -> p u", p=P))
+        nc.sync.dma_start(out=wg[0][:], in_=wgs[:, 0:BANK])
         nc.sync.dma_start(idx2[:], offs2)
-        for tile, lo, hi, c0, c1 in (
-            (wg_a, 0, 1, 0, BANK),
-            (wg_b, 1, 2, 0, BANK),
-            (wg_c, 0, 2, BANK, S),
-            (wg_rest, 2, PACK, 0, S),
-        ):
-            for q in (0, 2, 1, 3):
-                nc.sync.dma_start(out=tile[32 * q : 32 * q + 32, :, :], in_=wgs_rows[:, lo:hi, c0:c1])
+        raw_second = [load_w2(a, 2, 4) for a in range(PASSES)]
+        nc.sync.dma_start(out=wg[1][:], in_=wgs[:, BANK:S])
         nc.sync.dma_start(idx3[:], offs3)
-        nc.sync.dma_start(out=skip_sb[:], in_=skip.rearrange("(p t) m -> p t m", t=PACK))
+        skip_rows = skip.rearrange("(p t) m -> p t m", t=PACK)
+        for c in range(CHUNKS):
+            nc.sync.dma_start(out=skips[c][:], in_=skip_rows[:, :, c * CHUNK : (c + 1) * CHUNK])
         nc.sync.dma_start(out=w3c[:].bitcast(I32), in_=w3_words[0].rearrange("p c i -> p (c i)").bitcast(I32))
+        load_scales(4 * [on_sync], w3s, 4, lambda lo, hi: w3_scales[0, lo:hi, :])
 
-        for t, spent in ((1, "w1_raw"), (2, "w1_raw_s"), (3, "tab0")):
-            pages.append(held([P, T2], F32, "page%d" % t, spent))
-            step = T2 if t == 1 else BANK
-            for lo in range(0, T2, step):
-                nc.gpsimd.memset(pages[t][:, lo : lo + step], 0.0)
-        w3s = held([P, N_OUT], U8, "w3s", "tab1")
-        nc.gpsimd.memset(w3s[:].bitcast(I32), 0)
-        for q in range(QUADS):
-            nc.sync.dma_start(
-                out=w3s[32 * q : 32 * q + 4, :].bitcast(I32), in_=w3_scales[0, 4 * q : 4 * q + 4, :].bitcast(I32)
-            )
+        gather_words(1, 0, 2, "tab_s")
+        prepare_w2([raw_first[0][:]], [(0, 0), (0, 1)])
+        gather_words(2, 0, 1, "w2_bf0_0")
+        prepare_w2([raw_first[1][:]], [(1, 0), (1, 1)])
+        prepare_w2([raw_first[2][:, :, 0:P]], [(2, 0)])
+        prepare_w2([raw_first[2][:, :, P : 2 * P]], [(2, 1)])
+        gather_words(2, 1, 2, "w2_bf2_0")
 
-        grouped0 = cast_w2(nc.scalar.copy, 0, 0, PACK)
-        grouped1 = cast_w2(nc.scalar.copy, 1, 0, PACK)
-        v.append(gather_words(1, 0, S, "tab_s"))
-        quantize_w2(grouped0, 0, 0, PACK)
-        v.append(gather_words(2, 0, BANK))
-        quantize_w2(grouped1, 1, 0, PACK)
-        quantize_w2(cast_w2(nc.vector.tensor_copy, 2, 0, 1), 2, 0, 1)
-        quantize_w2(cast_w2(nc.scalar.copy, 2, 1, 2), 2, 1, 2)
-        v[2].extend(gather_words(2, BANK, S, "w2_bf2_0"))
+        units = [(0, 0), (1, 0), (0, 1), (1, 1), (2, 0), (3, 0), (2, 1), (3, 1)]
 
-        units = [(0, 0), (1, 0), (0, 1), (2, 0), (1, 1), (2, 1), (3, 0), (3, 1)]
-
-        def make_h(u):
-            t, half = units[u]
+        def make_h(n):
+            u, half = units[n]
             cols = slice(half * BANK, (half + 1) * BANK)
-            rows = slice(t * P, (t + 1) * P)
-            acc_b = psum.tile([P, BANK], F32, name="acc_b", tag="bank%d" % (2 * u % 8))
-            acc_a = psum.tile([P, BANK], F32, name="acc_a", tag="bank%d" % (2 * u % 8 + 1))
+            acc_b = psum.tile([P, BANK], F32, name="acc_b", tag="bank%d" % (2 * n % 8))
+            acc_a = psum.tile([P, BANK], F32, name="acc_a", tag="bank%d" % (2 * n % 8 + 1))
+            for a in range(PASSES):
+                nc.tensor.matmul_mx(
+                    out=acc_b[:],
+                    lhsT=w2q[(a, u)][0].bitcast(FP8X4),
+                    lhsT_scale=w2q[(a, u)][1],
+                    rhs=v[(a, half)].bitcast(FP8X4),
+                    rhs_scale=v_s[4 * a : P, cols],
+                    start=(a == 0),
+                    stop=(a == PASSES - 1),
+                )
             for a in range(PASSES):
                 plane = v_s[:, cols] if a == 0 else v_s_down[:, (a - 1) * S + half * BANK : (a - 1) * S + (half + 1) * BANK]
                 nc.tensor.matmul_mx(
                     out=acc_a[:],
-                    lhsT=w1c[:, a, 2 * t * P : 2 * (t + 1) * P].bitcast(FP4X4),
-                    lhsT_scale=w1s[:, a, rows],
-                    rhs=v[a][half].bitcast(FP8X4),
+                    lhsT=w1c[:, a, 2 * u * P : 2 * (u + 1) * P].bitcast(FP4X4),
+                    lhsT_scale=w1s[:, a, u * P : (u + 1) * P],
+                    rhs=v[(a, half)].bitcast(FP8X4),
                     rhs_scale=plane,
-                    start=(a == 0),
-                    stop=(a == PASSES - 1),
-                )
-                nc.tensor.matmul_mx(
-                    out=acc_b[:],
-                    lhsT=w2q[(a, t)][0].bitcast(FP8X4),
-                    lhsT_scale=w2q[(a, t)][1],
-                    rhs=v[a][half].bitcast(FP8X4),
-                    rhs_scale=v_s[4 * a : P, cols],
                     start=(a == 0),
                     stop=(a == PASSES - 1),
                 )
             return acc_a, acc_b
 
-        piece = 4 * CHUNK
-
-        def placed(shape, dtype, name, offset):
-            return shared.tile(shape, dtype, name=name, offset=offset, align_bytes=64)
-
-        def pick(c, t, target):
-            slots = idx3[:, c * CHUNK // 16 : (c + 1) * CHUNK // 16]
-            nc.vector.tensor_copy(out=target, in_=pages[t][:].indirect(slots))
-
-        def sigmoid(gate, x):
-            nc.scalar.activation(out=gate, in_=x, func=ACT.Sigmoid)
-
-        def scatter(t, lo, values):
+        def scatter(u, lo, values):
             width = values.shape[1]
-            nc.vector.tensor_copy(out=pages[t][:].indirect(idx2[:, lo // 16 : (lo + width) // 16]), in_=values)
+            nc.vector.tensor_copy(out=pages[u][:].indirect(idx2[:, lo // 16 : (lo + width) // 16]), in_=values)
 
         def weigh_on_gpsimd(lin, gel, weight, sent):
             h = held([P, lin.shape[1]], F32, "h")
             nc.gpsimd.tensor_tensor(out=h[:], in0=lin, in1=gel, op=ALU.add)
             nc.gpsimd.tensor_tensor(out=sent, in0=h[:], in1=weight, op=ALU.mult)
 
-        acc_a, acc_b = make_h(0)
-        lin = pair.tile([P, BANK], F32, name="lin")
-        nc.scalar.copy(out=lin[:, 0:CHUNK], in_=acc_a[:, CHUNK:BANK])
-        gel = held([P, BANK], F32, "gel_first")
-        for lo in (0, CHUNK):
-            nc.scalar.activation(
-                out=gel[:, lo : lo + CHUNK], in_=acc_b[:, lo : lo + CHUNK], func=ACT.Gelu_apprx_tanh, bias=bias[:, 0:1]
-            )
-        h_first = held([P, CHUNK], F32, "h_first")
-        sent = held([P, BANK], F32, "sent_first")
-        nc.vector.tensor_tensor(out=h_first[:], in0=acc_a[:, 0:CHUNK], in1=gel[:, 0:CHUNK], op=ALU.add)
-        nc.vector.tensor_tensor(out=sent[:, 0:CHUNK], in0=h_first[:], in1=wg_a[:, 0, 0:CHUNK], op=ALU.mult)
-        scatter(0, 0, sent[:, 0:CHUNK])
-        weigh_on_gpsimd(lin[:, 0:CHUNK], gel[:, CHUNK:BANK], wg_a[:, 0, CHUNK:BANK], sent[:, CHUNK:BANK])
-        scatter(0, CHUNK, sent[:, CHUNK:BANK])
+        def pick(c, u, target):
+            slots = idx3[:, c * CHUNK // 16 : (c + 1) * CHUNK // 16]
+            nc.vector.tensor_copy(out=target, in_=pages[u][:].indirect(slots))
 
-        wg = {(1, 0): wg_b[:, 0, :], (0, 1): wg_c[:, 0, :], (1, 1): wg_c[:, 1, :]}
-        for t, half in [unit for unit in units if unit[0] >= 2]:
-            wg[(t, half)] = wg_rest[:, t - 2, half * BANK : (half + 1) * BANK]
-        for u in range(1, len(units)):
-            t, half = units[u]
-            last = u == len(units) - 1
-            weight = wg[(t, half)]
-            acc_a, acc_b = make_h(u)
+        turned = {}
+
+        def turn_in(c, u, x):
+            for side in range(SIDES):
+                if (c, side) not in turned:
+                    turned[(c, side)] = psum.tile([P, H], F32, name="turned", tag="bank%d" % (SIDES * (c % 2) + side))
+                nc.tensor.transpose(turned[(c, side)][:, u * P : (u + 1) * P], x[:, side * P : (side + 1) * P], ident[:])
+
+        def fetch(c, lo, hi, tag=None):
+            x = held([P, hi - lo, CHUNK], F32, "x%d_%d" % (c, lo), tag)
+            for u in range(lo, hi):
+                pick(c, u, x[:, u - lo, :])
+            return x
+
+        def fetch_and_turn(c, lo, hi, tag=None):
+            x = fetch(c, lo, hi, tag)
+            for u in range(lo, hi):
+                turn_in(c, u, x[:, u - lo, :])
+
+        def sigmoid(gate, c, side, lo, hi):
+            rows = P // PACK
+            nc.scalar.activation(
+                out=gate[:, :, lo * rows : hi * rows],
+                in_=turned[(c, side)][:, lo * P : hi * P].rearrange("m (q t) -> m t q", t=PACK),
+                func=ACT.Sigmoid,
+            )
+
+        acc_a, acc_b = make_h(0)
+        gel = held([P, BANK], F32, "gel_first")
+        h_first = held([P, BANK], F32, "h_first")
+        sent = held([P, BANK], F32, "sent_first")
+        pieces = [slice(lo, lo + CHUNK) for lo in (0, CHUNK)]
+        for cols in pieces:
+            nc.scalar.activation(out=gel[:, cols], in_=acc_b[:, cols], func=ACT.Gelu_apprx_tanh, bias=bias[:, 0:1])
+        for cols in pieces:
+            nc.vector.tensor_tensor(out=h_first[:, cols], in0=acc_a[:, cols], in1=gel[:, cols], op=ALU.add)
+        for cols in pieces:
+            nc.vector.tensor_tensor(out=sent[:, cols], in0=h_first[:, cols], in1=wg[0][:, cols], op=ALU.mult)
+        scatter(0, 0, sent[:])
+
+        gates = {}
+        for n in range(1, len(units)):
+            u, half = units[n]
+            last = n == len(units) - 1
+            acc_a, acc_b = make_h(n)
+            if last:
+                gel = held([P, BANK], F32, "gel_last")[:]
+            else:
+                gel = ring.tile([P, BANK], F32, name="gel")[:]
+            nc.scalar.activation(out=gel, in_=acc_b[:], func=ACT.Gelu_apprx_tanh, bias=bias[:, u : u + 1])
             lin = pair.tile([P, BANK], F32, name="lin")
             nc.scalar.copy(out=lin[:], in_=acc_a[:])
             if last:
-                gel = placed([P, BANK], F32, "gel_last", 0)[:]
-            else:
-                gel = ring.tile([P, BANK], F32, name="gel")[:]
-            nc.scalar.activation(out=gel, in_=acc_b[:], func=ACT.Gelu_apprx_tanh, bias=bias[:, t : t + 1])
-            if last:
                 sent = held([P, BANK], F32, "sent_last")[:]
-            elif u == len(units) - 2:
-                sent = held([P, BANK], F32, "sent_before_last", "x_first")[:]
+            elif n == len(units) - 2:
+                sent = held([P, BANK], F32, "sent_before_last")[:]
             else:
-                sent = ring.tile([P, BANK], F32, name="sent")[:]
-            weigh_on_gpsimd(lin[:], gel, weight, sent)
-            if u == 1:
-                quantize_w2(cast_w2(nc.scalar.copy, 2, 2, PACK, "gel_first"), 2, 2, PACK, "sent_first")
+                sent = pair.tile([P, BANK], F32, name="sent")[:]
+            weigh_on_gpsimd(lin[:], gel, wg[half][:], sent)
+            if n == 3:
+                late = [(a, u2) for u2 in (2, 3) for a in range(PASSES)]
+                parts = [raw_second[a][:, :, (u2 - 2) * P : (u2 - 1) * P] for a, u2 in late]
+                prepare_w2(parts[0:4], late[0:4], tag="gel_first")
+                prepare_w2(parts[4:6], late[4:6], tag="h_first")
             if last:
-                early = PACK - 1
-                x_first = held([P, PACK, CHUNK], F32, "x_first")
-                for slot in range(early):
-                    pick(0, slot, x_first[:, slot, :])
-                gates = [placed([P, PACK, CHUNK], F32, "gate0", 0)]
-                sigmoid(gates[0][:, 0, :], x_first[:, 0, :])
-                sigmoid(gates[0][:, 1:early, :], x_first[:, 1:early, :])
-            scatter(t, half * BANK, sent)
+                fetch_and_turn(0, 0, PAGES - 1, "sent_before_last")
+                gates[(0, 0)] = held([P, PACK, P], F32, "gate0_0", "gel_last")
+                gates[(0, 1)] = held([P, PACK, P], F32, "gate0_1")
+                for side in range(SIDES):
+                    sigmoid(gates[(0, side)], 0, side, 0, PAGES - 1)
+            scatter(u, half * BANK, sent)
 
         out_rows = out.rearrange("(b p) m -> p b m", p=P)
 
-        def make_z(c, z, zc, zs):
-            nc.vector.tensor_tensor(
-                out=z[:].rearrange("p (n i t) -> p n t i", i=2, t=PACK),
-                in0=gates[c][:].rearrange("p t (n i) -> p n t i", i=2),
-                in1=skip_sb[:, :, c * CHUNK : (c + 1) * CHUNK].rearrange("p t (n i) -> p n t i", i=2),
-                op=ALU.mult,
-            )
+        def turn_back(c, side):
+            back = psum.tile([P, PACK, P], F32, name="back", tag="bank%d" % (SIDES * (c % 2) + side))
+            for t in range(PACK):
+                nc.tensor.transpose(back[:, t, :], gates[(c, side)][:, t, :], ident[:])
+            return back
+
+        def make_z(c, backs):
+            z = held([P, CHUNK * PACK], BF16, "z%d" % c)
+            for side in range(SIDES):
+                nc.vector.tensor_tensor(
+                    out=z[:, side * BANK : (side + 1) * BANK].rearrange("p (n i t) -> p n t i", i=2, t=PACK),
+                    in0=backs[side][:].rearrange("p t (n i) -> p n t i", i=2),
+                    in1=skips[c][:, :, side * P : (side + 1) * P].rearrange("p t (n i) -> p n t i", i=2),
+                    op=ALU.mult,
+                )
+            zc = held([P, CHUNK], U32, "zc%d" % c)
+            zs = held([P, CHUNK], U8, "zs%d" % c)
             nc.vector.quantize_mx(out=zc[:].bitcast(FP8X4), scales=zs[:], in_=z[:])
             return zc, zs
 
-        def operand(c):
-            return held([P, CHUNK], U32, "zc%d" % c), held([P, CHUNK], U8, "zs%d" % c)
-
-        def fill_bank(c, n, zq):
+        def send_bank(c, n, zq, copy):
             zc, zs = zq
-            acc = psum.tile([P, PER_BANK, CHUNK], F32, name="acc", tag="bank%d" % ((c * BANKS_A_CHUNK + n) % 8))
+            bank = 4 + n if n < 4 else SIDES * (c % 2) + n - 4
+            acc = psum.tile([P, PER_BANK, CHUNK], F32, name="acc", tag="bank%d" % bank)
             for e in range(PER_BANK):
                 b = n * PER_BANK + e
                 nc.tensor.matmul_mx(
@@ -309,69 +317,53 @@ def tile_list_pipeline_stage_transfer_kernel(
                     start=True,
                     stop=True,
                 )
-            return acc
-
-        def send_bank(c, n, zq, copy):
-            empty_bank(c, n, fill_bank(c, n, zq), copy)
-
-        def empty_bank(c, n, acc, copy):
             staged = stage.tile([P, PER_BANK, CHUNK], F32, name="staged")
             copy(out=staged[:], in_=acc[:])
             nc.sync.dma_start(
                 out=out_rows[:, n * PER_BANK : (n + 1) * PER_BANK, c * CHUNK : (c + 1) * CHUNK], in_=staged[:]
             )
 
-        on_scalar, on_vector = nc.scalar.copy, nc.vector.tensor_copy
+        def gate_and_turn(c):
+            for side in range(SIDES):
+                gates[(c, side)] = pair.tile([P, PACK, P], F32, name="gate")
+                sigmoid(gates[(c, side)], c, side, 0, PAGES)
+            return [turn_back(c, side) for side in range(SIDES)]
 
-        x = {}
+        def send(c, lo, hi, zq, on_vector):
+            for n in range(lo, hi):
+                send_bank(c, n, zq, nc.vector.tensor_copy if n in on_vector else nc.scalar.copy)
 
-        def fetch(tile, keys):
-            for k, key in enumerate(keys):
-                x[key] = tile[:, k, :]
-                pick(*key, x[key])
+        def turn_all(c, parts):
+            for u in range(PAGES):
+                turn_in(c, u, parts[u])
 
-        def gate(c, t):
-            sigmoid(gates[c][:, t, :], x[(c, t)])
-
-        pick(0, 3, x_first[:, 3, :])
-        sigmoid(gates[0][:, 3, :], x_first[:, 3, :])
-        fetch(held([P, 1, CHUNK], F32, "x10", "sent_last"), [(1, 0)])
-        gates.append(placed([P, PACK, CHUNK], F32, "gate1", 8 * piece))
-        gate(1, 0)
-        zq0 = make_z(
-            0,
-            placed([P, span], BF16, "z0", 4 * piece),
-            placed([P, CHUNK], U32, "zc0", 12 * piece),
-            held([P, CHUNK], U8, "zs0"),
-        )
-        fetch(placed([P, 3, CHUNK], F32, "x1", 4 * piece), [(1, 1), (1, 2), (1, 3)])
-        for t in range(1, PACK):
-            gate(1, t)
-        send_bank(0, 0, zq0, on_vector)
-        zq1 = make_z(1, placed([P, span], BF16, "z1", 18 * piece), *operand(1))
-        for n in range(1, BANKS_A_CHUNK):
-            send_bank(0, n, zq0, on_scalar)
-        fetch(placed([P, 6, CHUNK], F32, "x2", 12 * piece + 512), [divmod(k, PACK) for k in range(8, 14)])
-        gates.append(placed([P, PACK, CHUNK], F32, "gate2", 0))
-        gates.append(placed([P, PACK, CHUNK], F32, "gate3", 8 * piece))
-        send_bank(1, 0, zq1, on_scalar)
-        gate(2, 0)
-        send_bank(1, 1, zq1, on_scalar)
-        for t in range(1, PACK):
-            gate(2, t)
-        zq2 = make_z(2, placed([P, span], BF16, "z2", 4 * piece), *operand(2))
-        fetch(placed([P, 2, CHUNK], F32, "x3", 4 * piece), [(3, 2), (3, 3)])
-        send_bank(1, 2, zq1, on_scalar)
-        send_bank(1, 3, zq1, on_scalar)
-        gate(3, 0)
-        gate(3, 1)
-        send_bank(1, 4, zq1, on_scalar)
-        send_bank(1, 5, zq1, on_scalar)
-        gate(3, 2)
-        gate(3, 3)
-        send_bank(2, 0, zq2, on_vector)
-        zq3 = make_z(3, held([P, span], BF16, "z3"), *operand(3))
-        for n in range(1, BANKS_A_CHUNK):
-            send_bank(2, n, zq2, on_vector if n == 5 else on_scalar)
-        for n in range(BANKS_A_CHUNK):
-            send_bank(3, n, zq3, on_scalar if n % 2 else on_vector)
+        x_last = fetch(0, PAGES - 1, PAGES)
+        for side in range(SIDES):
+            turned[(0, side)] = psum.tile([P, H], F32, name="turned", tag="bank%d" % (SIDES + side))
+        turn_in(0, PAGES - 1, x_last[:, 0, :])
+        for side in range(SIDES):
+            sigmoid(gates[(0, side)], 0, side, PAGES - 1, PAGES)
+        backs0 = [turn_back(0, side) for side in range(SIDES)]
+        fetch_and_turn(1, 0, PAGES, "sent_last")
+        zq0 = make_z(0, backs0)
+        backs1 = gate_and_turn(1)
+        x2 = [fetch(2, 0, 1, "skip0")[:, 0, :], fetch(2, 1, 2, "z0")[:, 0, :]]
+        zq1 = make_z(1, backs1)
+        x2.append(fetch(2, 2, 3, "skip1")[:, 0, :])
+        x = held([P, PAGES, CHUNK], F32, "x_late", "z1")
+        pick(2, 3, x[:, 3, :])
+        x2.append(x[:, 3, :])
+        send(0, 0, BANKS_A_CHUNK, zq0, ())
+        turn_all(2, x2)
+        backs2 = gate_and_turn(2)
+        send(1, 0, 1, zq1, (0,))
+        for u in range(3):
+            pick(3, u, x[:, u, :])
+        zq2 = make_z(2, backs2)
+        x3 = [x[:, u, :] for u in range(3)] + [fetch(3, 3, PAGES, "skip2")[:, 0, :]]
+        send(1, 1, BANKS_A_CHUNK, zq1, ())
+        turn_all(3, x3)
+        backs3 = gate_and_turn(3)
+        zq3 = make_z(3, backs3)
+        send(2, 0, BANKS_A_CHUNK, zq2, (0, 1, 2))
+        send(3, 0, BANKS_A_CHUNK, zq3, (0, 2, 4))

@@ -63,9 +63,11 @@ def tile_list_pipeline_stage_transfer_kernel(
         w3c = held([P, N_OUT], U32, "w3c")
         w3s = held([P, N_OUT], U8, "w3s")
         ident = held([P, P], F32, "ident")
+        bias_rows = held([P, P], F32, "bias_rows")
         warm_out = held([P, 1], F32, "warm_out")
 
         nc.vector.memset(tab_s[:].bitcast(I32), 0)
+        nc.vector.memset(bias_rows[:], 0.0)
         nc.vector.memset(w1s[:].bitcast(I32), 0)
         nc.vector.memset(v_s_down[:].bitcast(I32), 0)
         nc.vector.memset(w3s[:].bitcast(I32), 0)
@@ -112,40 +114,39 @@ def tile_list_pipeline_stage_transfer_kernel(
 
         w2q = {}
 
-        def quantize_w2(grouped, keys, tag=None):
+        def quantize_w2(grouped, keys, codes=None):
             name = "%d_%d" % keys[0]
-            codes = held([P, len(keys) * P], U32, "w2c" + name, tag)
+            if codes is None:
+                codes = held([P, len(keys) * P], U32, "w2c" + name)[:]
             scales = held([P, len(keys) * P], U8, "w2s" + name)
-            nc.vector.quantize_mx(out=codes[:].bitcast(FP8X4), scales=scales[:], in_=grouped[:])
+            nc.vector.quantize_mx(out=codes.bitcast(FP8X4), scales=scales[:], in_=grouped[:])
             for n, key in enumerate(keys):
                 w2q[key] = (codes[:, n * P : (n + 1) * P], scales[:, n * P : (n + 1) * P])
 
-        def prepare_w2(raws, keys, tag=None, codes_tag=None):
+        def prepare_w2(raws, keys, tag=None, codes=None):
             grouped = held([P, len(keys) * P * PACK], BF16, "w2_bf%d_%d" % keys[0], tag)
             width = len(keys) * P * PACK // len(raws)
             for n, raw in enumerate(raws):
                 cast_w2(raw, grouped[:, n * width : (n + 1) * width])
-            quantize_w2(grouped, keys, codes_tag)
+            quantize_w2(grouped, keys, codes)
 
         nc.sync.dma_start(idx[:], offs)
         load_tab(0)
         on_sync = nc.sync.dma_start
         load_tab(1)
         load_scales(4 * [on_sync], tab_s, 4 * PASSES, lambda lo, hi: tab_scales[:, lo:hi, :])
+        nc.sync.dma_start(out=bias_rows[0:PAGES, :], in_=b2.rearrange("(u p) -> u p", p=P))
         load_tab(2)
-        raw_first = [load_w2(0, 0, 2)]
-        raw_first.append(load_w2(1, 0, 2))
-        gather_words(0, 0, 2)
-        nc.vector.tensor_copy(out=v_s[:], in_=tab_s[:].indirect(idx[:]))
+        raw_first = [load_w2(0, 0, 2), load_w2(1, 0, 2)]
         load_scales(4 * [on_sync], w1s, 4, lambda lo, hi: w1_scales[:, lo:hi, :].rearrange("a r c -> r a c"))
         raw_first.append(load_w2(2, 0, 2))
         nc.sync.dma_start(out=w1c[:].bitcast(I32), in_=w1_words.rearrange("a p c -> p a c").bitcast(I32))
+        gather_words(0, 0, 2)
+        nc.vector.tensor_copy(out=v_s[:], in_=tab_s[:].indirect(idx[:]))
         for a in range(1, PASSES):
             nc.sync.dma_start(
                 out=v_s_down[0:112, (a - 1) * S : a * S].bitcast(I32), in_=v_s[4 * a : 4 * a + 112, :].bitcast(I32)
             )
-        with nc.allow_non_contiguous_dma(reason="one bias value a partition and page"):
-            nc.sync.dma_start(out=bias[:], in_=b2.rearrange("(u p) -> p u", p=P))
         nc.sync.dma_start(out=wg[0][:], in_=wgs[:, 0:BANK])
         nc.sync.dma_start(idx2[:], offs2)
         raw_second = [load_w2(a, 2, 4) for a in range(PASSES)]
@@ -157,21 +158,24 @@ def tile_list_pipeline_stage_transfer_kernel(
         nc.sync.dma_start(out=w3c[:].bitcast(I32), in_=w3_words[0].rearrange("p c i -> p (c i)").bitcast(I32))
         load_scales(4 * [on_sync], w3s, 4, lambda lo, hi: w3_scales[0, lo:hi, :])
 
+        bias_turned = psum.tile([P, P], F32, name="bias_turned", tag="bank7")
+        nc.tensor.transpose(bias_turned[:], bias_rows[:], ident[:])
+        nc.scalar.copy(out=bias[:], in_=bias_turned[:, 0:PAGES])
         gather_words(1, 0, 2, "tab_s")
         prepare_w2([raw_first[0][:]], [(0, 0), (0, 1)])
         gather_words(2, 0, 1, "w2_bf0_0")
-        prepare_w2([raw_first[1][:]], [(1, 0), (1, 1)])
+        prepare_w2([raw_first[1][:, :, 0:P]], [(1, 0)])
         prepare_w2([raw_first[2][:, :, 0:P]], [(2, 0)])
-        prepare_w2([raw_first[2][:, :, P : 2 * P]], [(2, 1)])
         gather_words(2, 1, 2, "w2_bf2_0")
+        prepare_w2([raw_first[a][:, :, P : 2 * P] for a in (1, 2)], [(1, 1), (2, 1)])
 
         units = [(0, 0), (1, 0), (0, 1), (1, 1), (2, 0), (3, 0), (2, 1), (3, 1)]
 
         def make_h(n):
             u, half = units[n]
             cols = slice(half * BANK, (half + 1) * BANK)
-            acc_b = psum.tile([P, BANK], F32, name="acc_b", tag="bank%d" % (2 * n % 8))
-            acc_a = psum.tile([P, BANK], F32, name="acc_a", tag="bank%d" % (2 * n % 8 + 1))
+            acc_b = psum.tile([P, BANK], F32, name="acc_b", tag="bank%d" % (2 * n % 4))
+            acc_a = psum.tile([P, BANK], F32, name="acc_a", tag="bank%d" % (2 * n % 4 + 1))
             for a in range(PASSES):
                 nc.tensor.matmul_mx(
                     out=acc_b[:],
@@ -209,11 +213,12 @@ def tile_list_pipeline_stage_transfer_kernel(
             nc.vector.tensor_copy(out=target, in_=pages[u][:].indirect(slots))
 
         turned = {}
+        turn_banks = (2, 0)
 
         def turn_in(c, u, x):
             for side in range(SIDES):
                 if (c, side) not in turned:
-                    turned[(c, side)] = psum.tile([P, H], F32, name="turned", tag="bank%d" % (SIDES * (c % 2) + side))
+                    turned[(c, side)] = psum.tile([P, H], F32, name="turned", tag="bank%d" % (turn_banks[c % 2] + side))
                 nc.tensor.transpose(turned[(c, side)][:, u * P : (u + 1) * P], x[:, side * P : (side + 1) * P], ident[:])
 
         def fetch(c, lo, hi, tag=None):
@@ -264,31 +269,39 @@ def tile_list_pipeline_stage_transfer_kernel(
                 sent = held([P, BANK], F32, "sent_last")[:]
             elif n == len(units) - 2:
                 sent = held([P, BANK], F32, "sent_before_last")[:]
+            elif n == 2:
+                sent = held([P, BANK], F32, "sent_third")[:]
             else:
                 sent = pair.tile([P, BANK], F32, name="sent")[:]
             weigh_on_gpsimd(lin[:], gel, wg[half][:], sent)
             if n == 3:
                 late = [(a, u2) for u2 in (2, 3) for a in range(PASSES)]
                 parts = [raw_second[a][:, :, (u2 - 2) * P : (u2 - 1) * P] for a, u2 in late]
-                prepare_w2(parts[0:4], late[0:4], tag="gel_first")
-                prepare_w2(parts[4:6], late[4:6], tag="h_first")
+                late_codes = held([P, len(late) * P], U32, "late_codes", "sent_third")
+                prepare_w2(parts[0:4], late[0:4], "gel_first", late_codes[:, 0 : 4 * P])
+                prepare_w2(parts[4:6], late[4:6], "h_first", late_codes[:, 4 * P : 6 * P])
             if last:
-                fetch_and_turn(0, 0, PAGES - 1, "sent_before_last")
+                for early in range(2):
+                    turn_in(0, early, x_early[:, early, :])
+                fetch_and_turn(0, 2, PAGES - 1, "sent_before_last")
                 gates[(0, 0)] = held([P, PACK, P], F32, "gate0_0", "gel_last")
                 gates[(0, 1)] = held([P, PACK, P], F32, "gate0_1")
                 for side in range(SIDES):
                     sigmoid(gates[(0, side)], 0, side, 0, PAGES - 1)
             scatter(u, half * BANK, sent)
+            if n == 3:
+                x_early = fetch(0, 0, 2)
+                x_next = fetch(1, 0, 2)
 
         out_rows = out.rearrange("(b p) m -> p b m", p=P)
 
         def turn_back(c, side):
-            back = psum.tile([P, PACK, P], F32, name="back", tag="bank%d" % (SIDES * (c % 2) + side))
+            back = psum.tile([P, PACK, P], F32, name="back", tag="bank%d" % (turn_banks[c % 2] + side))
             for t in range(PACK):
                 nc.tensor.transpose(back[:, t, :], gates[(c, side)][:, t, :], ident[:])
             return back
 
-        def make_z(c, backs):
+        def multiply(c, backs):
             z = held([P, CHUNK * PACK], BF16, "z%d" % c)
             for side in range(SIDES):
                 nc.vector.tensor_tensor(
@@ -297,14 +310,22 @@ def tile_list_pipeline_stage_transfer_kernel(
                     in1=skips[c][:, :, side * P : (side + 1) * P].rearrange("p t (n i) -> p n t i", i=2),
                     op=ALU.mult,
                 )
+            return z
+
+        def quantize_z(c, z):
             zc = held([P, CHUNK], U32, "zc%d" % c)
             zs = held([P, CHUNK], U8, "zs%d" % c)
             nc.vector.quantize_mx(out=zc[:].bitcast(FP8X4), scales=zs[:], in_=z[:])
             return zc, zs
 
+        def make_z(c, backs):
+            return quantize_z(c, multiply(c, backs))
+
+        out_banks = [(2, 3, 4, 5, 6, 7), (0, 1, 4, 5, 6, 7), (2, 3, 4, 5, 6, 7), (0, 1, 4, 5, 6, 7)]
+
         def send_bank(c, n, zq, copy):
             zc, zs = zq
-            bank = 4 + n if n < 4 else SIDES * (c % 2) + n - 4
+            bank = out_banks[c][n]
             acc = psum.tile([P, PER_BANK, CHUNK], F32, name="acc", tag="bank%d" % bank)
             for e in range(PER_BANK):
                 b = n * PER_BANK + e
@@ -339,31 +360,36 @@ def tile_list_pipeline_stage_transfer_kernel(
 
         x_last = fetch(0, PAGES - 1, PAGES)
         for side in range(SIDES):
-            turned[(0, side)] = psum.tile([P, H], F32, name="turned", tag="bank%d" % (SIDES + side))
+            turned[(0, side)] = psum.tile([P, H], F32, name="turned", tag="bank%d" % (turn_banks[1] + side))
         turn_in(0, PAGES - 1, x_last[:, 0, :])
         for side in range(SIDES):
             sigmoid(gates[(0, side)], 0, side, PAGES - 1, PAGES)
         backs0 = [turn_back(0, side) for side in range(SIDES)]
-        fetch_and_turn(1, 0, PAGES, "sent_last")
+        for u in range(2):
+            turn_in(1, u, x_next[:, u, :])
+        fetch_and_turn(1, 2, PAGES, "sent_last")
+        x2 = held([P, 2, CHUNK], F32, "x2_first", "x0_3")
+        pick(2, 0, x2[:, 0, :])
+        pick(2, 1, x2[:, 1, :])
         zq0 = make_z(0, backs0)
         backs1 = gate_and_turn(1)
-        x2 = [fetch(2, 0, 1, "skip0")[:, 0, :], fetch(2, 1, 2, "z0")[:, 0, :]]
-        zq1 = make_z(1, backs1)
-        x2.append(fetch(2, 2, 3, "skip1")[:, 0, :])
-        x = held([P, PAGES, CHUNK], F32, "x_late", "z1")
-        pick(2, 3, x[:, 3, :])
-        x2.append(x[:, 3, :])
-        send(0, 0, BANKS_A_CHUNK, zq0, ())
+        x2 = [x2[:, 0, :], x2[:, 1, :], fetch(2, 2, 3, "skip0")[:, 0, :], fetch(2, 3, 4, "z0")[:, 0, :]]
+        send(0, 0, 2, zq0, ())
         turn_all(2, x2)
         backs2 = gate_and_turn(2)
-        send(1, 0, 1, zq1, (0,))
-        for u in range(3):
-            pick(3, u, x[:, u, :])
+        z1 = multiply(1, backs1)
+        send(0, 2, BANKS_A_CHUNK, zq0, (2,))
+        x3 = [fetch(3, 0, 1, "skip1")[:, 0, :]]
+        zq1 = quantize_z(1, z1)
+        x = held([P, 3, CHUNK], F32, "x_late", "z1")
+        for u in range(1, PAGES):
+            pick(3, u, x[:, u - 1, :])
+            x3.append(x[:, u - 1, :])
         zq2 = make_z(2, backs2)
-        x3 = [x[:, u, :] for u in range(3)] + [fetch(3, 3, PAGES, "skip2")[:, 0, :]]
-        send(1, 1, BANKS_A_CHUNK, zq1, ())
+        send(1, 0, 2, zq1, ())
         turn_all(3, x3)
         backs3 = gate_and_turn(3)
         zq3 = make_z(3, backs3)
-        send(2, 0, BANKS_A_CHUNK, zq2, (0, 1, 2))
+        send(1, 2, BANKS_A_CHUNK, zq1, (3, 4, 5))
+        send(2, 0, BANKS_A_CHUNK, zq2, ())
         send(3, 0, BANKS_A_CHUNK, zq3, (0, 2, 4))

@@ -29,7 +29,7 @@ SIDES = CHUNK // P
 BLOCKS = N_OUT // P
 PER_BANK = BANK // CHUNK
 BANKS_A_CHUNK = BLOCKS // PER_BANK
-WIDE = H // 2
+WARM_PASSES = 5
 
 
 def tile_list_pipeline_stage_transfer_kernel(
@@ -283,11 +283,24 @@ def tile_list_pipeline_stage_transfer_kernel(
             if last:
                 for early in range(2):
                     turn_in(0, early, x_early[:, early, :])
-                fetch_and_turn(0, 2, PAGES - 1, "sent_before_last")
                 gates[(0, 0)] = held([P, PACK, P], F32, "gate0_0", "gel_last")
                 gates[(0, 1)] = held([P, PACK, P], F32, "gate0_1")
                 for side in range(SIDES):
-                    sigmoid(gates[(0, side)], 0, side, 0, PAGES - 1)
+                    sigmoid(gates[(0, side)], 0, side, 0, 2)
+                fetch_and_turn(0, 2, PAGES - 1, "sent_before_last")
+                for side in range(SIDES):
+                    sigmoid(gates[(0, side)], 0, side, 2, PAGES - 1)
+                warm_acc = psum.tile([P, BANK], F32, name="warm_acc", tag="bank%d" % turn_banks[0])
+                for repeat in range(WARM_PASSES):
+                    nc.tensor.matmul_mx(
+                        out=warm_acc[:],
+                        lhsT=w2q[(0, 0)][0].bitcast(FP8X4),
+                        lhsT_scale=w2q[(0, 0)][1],
+                        rhs=v[(0, 0)].bitcast(FP8X4),
+                        rhs_scale=v_s[:, 0:BANK],
+                        start=True,
+                        stop=True,
+                    )
             scatter(u, half * BANK, sent)
             if n == 3:
                 x_early = fetch(0, 0, 2)

@@ -213,7 +213,7 @@ def tile_list_pipeline_stage_transfer_kernel(
             nc.vector.tensor_copy(out=target, in_=pages[u][:].indirect(slots))
 
         turned = {}
-        turn_banks = (2, 0)
+        turn_banks = (0, 2)
 
         def turn_in(c, u, x):
             for side in range(SIDES):
@@ -263,7 +263,7 @@ def tile_list_pipeline_stage_transfer_kernel(
             else:
                 gel = ring.tile([P, BANK], F32, name="gel")[:]
             nc.scalar.activation(out=gel, in_=acc_b[:], func=ACT.Gelu_apprx_tanh, bias=bias[:, u : u + 1])
-            lin = pair.tile([P, BANK], F32, name="lin")
+            lin = held([P, BANK], F32, "lin_last") if last else pair.tile([P, BANK], F32, name="lin")
             nc.scalar.copy(out=lin[:], in_=acc_a[:])
             if last:
                 sent = held([P, BANK], F32, "sent_last")[:]
@@ -281,19 +281,31 @@ def tile_list_pipeline_stage_transfer_kernel(
                 prepare_w2(parts[0:4], late[0:4], "gel_first", late_codes[:, 0 : 4 * P])
                 prepare_w2(parts[4:6], late[4:6], "h_first", late_codes[:, 4 * P : 6 * P])
             if last:
+                for side in range(SIDES):
+                    turned[(0, side)] = psum.tile([P, H], F32, name="turned", tag="bank%d" % (turn_banks[1] + side))
                 for early in range(2):
                     turn_in(0, early, x_early[:, early, :])
                 gates[(0, 0)] = held([P, PACK, P], F32, "gate0_0", "gel_last")
                 gates[(0, 1)] = held([P, PACK, P], F32, "gate0_1")
                 for side in range(SIDES):
                     sigmoid(gates[(0, side)], 0, side, 0, 2)
+                for side, spent in enumerate(("lin_last", "h")):
+                    turned[(1, side)] = psum.tile([P, H], F32, name="turned", tag="bank%d" % (turn_banks[0] + side))
+                    gates[(1, side)] = held([P, PACK, P], F32, "gate1_%d" % side, spent)
+                for early in range(2):
+                    turn_in(1, early, x_next[:, early, :])
+                for side in range(SIDES):
+                    sigmoid(gates[(1, side)], 1, side, 0, 2)
                 fetch_and_turn(0, 2, PAGES - 1, "sent_before_last")
                 for side in range(SIDES):
                     sigmoid(gates[(0, side)], 0, side, 2, PAGES - 1)
-                warm_acc = psum.tile([P, BANK], F32, name="warm_acc", tag="bank%d" % turn_banks[0])
+                warm_acc = [
+                    psum.tile([P, BANK], F32, name="warm_acc", tag="bank%d" % (turn_banks[1] + side))
+                    for side in range(SIDES)
+                ]
                 for repeat in range(WARM_PASSES):
                     nc.tensor.matmul_mx(
-                        out=warm_acc[:],
+                        out=warm_acc[repeat % SIDES][:],
                         lhsT=w2q[(0, 0)][0].bitcast(FP8X4),
                         lhsT_scale=w2q[(0, 0)][1],
                         rhs=v[(0, 0)].bitcast(FP8X4),
@@ -334,7 +346,7 @@ def tile_list_pipeline_stage_transfer_kernel(
         def make_z(c, backs):
             return quantize_z(c, multiply(c, backs))
 
-        out_banks = [(2, 3, 4, 5, 6, 7), (0, 1, 4, 5, 6, 7), (2, 3, 4, 5, 6, 7), (0, 1, 4, 5, 6, 7)]
+        out_banks = [(0, 1, 4, 5, 6, 7), (2, 3, 4, 5, 6, 7), (0, 1, 4, 5, 6, 7), (2, 3, 4, 5, 6, 7)]
 
         def send_bank(c, n, zq, copy):
             zc, zs = zq
@@ -378,14 +390,16 @@ def tile_list_pipeline_stage_transfer_kernel(
         for side in range(SIDES):
             sigmoid(gates[(0, side)], 0, side, PAGES - 1, PAGES)
         backs0 = [turn_back(0, side) for side in range(SIDES)]
-        for u in range(2):
-            turn_in(1, u, x_next[:, u, :])
+        for side in range(SIDES):
+            turned[(1, side)] = psum.tile([P, H], F32, name="turned", tag="bank%d" % (turn_banks[1] + side))
         fetch_and_turn(1, 2, PAGES, "sent_last")
+        for side in range(SIDES):
+            sigmoid(gates[(1, side)], 1, side, 2, PAGES)
         x2 = held([P, 2, CHUNK], F32, "x2_first", "x0_3")
         pick(2, 0, x2[:, 0, :])
         pick(2, 1, x2[:, 1, :])
         zq0 = make_z(0, backs0)
-        backs1 = gate_and_turn(1)
+        backs1 = [turn_back(1, side) for side in range(SIDES)]
         x2 = [x2[:, 0, :], x2[:, 1, :], fetch(2, 2, 3, "skip0")[:, 0, :], fetch(2, 3, 4, "z0")[:, 0, :]]
         send(0, 0, 2, zq0, ())
         turn_all(2, x2)
@@ -404,5 +418,5 @@ def tile_list_pipeline_stage_transfer_kernel(
         backs3 = gate_and_turn(3)
         zq3 = make_z(3, backs3)
         send(1, 2, BANKS_A_CHUNK, zq1, (3, 4, 5))
-        send(2, 0, BANKS_A_CHUNK, zq2, ())
+        send(2, 0, BANKS_A_CHUNK, zq2, (5,))
         send(3, 0, BANKS_A_CHUNK, zq3, (0, 2, 4))

@@ -55,7 +55,7 @@ def tile_list_pipeline_stage_transfer_kernel(
         tab_s = held([P, T], U8, "tab_s")
         v_s = held([P, S], U8, "v_s")
         v_s_down = held([P, (PASSES - 1) * S], U8, "v_s_down")
-        w1c = held([P, PASSES, 2 * H], U8, "w1c")
+        w1c = [held([P, PASSES, H], U8, "w1c%d" % part) for part in range(2)]
         w1s = held([P, PASSES, H], U8, "w1s")
         bias = held([P, PAGES], F32, "bias")
         wg = [held([P, BANK], F32, "wg%d" % half) for half in range(2)]
@@ -93,6 +93,10 @@ def tile_list_pipeline_stage_transfer_kernel(
             rows = w2[a * P * PACK : (a + 1) * P * PACK, lo * P : hi * P]
             nc.sync.dma_start(out=raw[:], in_=rows.rearrange("(p j) c -> p j c", j=PACK))
             return raw
+
+        def load_w1(part):
+            words = w1_words.rearrange("a p c -> p a c")[:, :, part * H : (part + 1) * H]
+            nc.sync.dma_start(out=w1c[part][:].bitcast(I32), in_=words.bitcast(I32))
 
         def load_scales(queues, plane, rows, scales):
             for q, queue in enumerate(queues):
@@ -139,8 +143,8 @@ def tile_list_pipeline_stage_transfer_kernel(
         load_tab(2)
         raw_first = [load_w2(0, 0, 2), load_w2(1, 0, 2)]
         load_scales(4 * [on_sync], w1s, 4, lambda lo, hi: w1_scales[:, lo:hi, :].rearrange("a r c -> r a c"))
+        load_w1(0)
         raw_first.append(load_w2(2, 0, 2))
-        nc.sync.dma_start(out=w1c[:].bitcast(I32), in_=w1_words.rearrange("a p c -> p a c").bitcast(I32))
         gather_words(0, 0, 2)
         nc.vector.tensor_copy(out=v_s[:], in_=tab_s[:].indirect(idx[:]))
         for a in range(1, PASSES):
@@ -150,6 +154,7 @@ def tile_list_pipeline_stage_transfer_kernel(
         nc.sync.dma_start(out=wg[0][:], in_=wgs[:, 0:BANK])
         nc.sync.dma_start(idx2[:], offs2)
         raw_second = [load_w2(a, 2, 4) for a in range(PASSES)]
+        load_w1(1)
         nc.sync.dma_start(out=wg[1][:], in_=wgs[:, BANK:S])
         nc.sync.dma_start(idx3[:], offs3)
         skip_rows = skip.rearrange("(p t) m -> p t m", t=PACK)
@@ -162,12 +167,14 @@ def tile_list_pipeline_stage_transfer_kernel(
         nc.tensor.transpose(bias_turned[:], bias_rows[:], ident[:])
         nc.scalar.copy(out=bias[:], in_=bias_turned[:, 0:PAGES])
         gather_words(1, 0, 2, "tab_s")
-        prepare_w2([raw_first[0][:]], [(0, 0), (0, 1)])
+        prepare_w2([raw_first[0][:, :, 0:P]], [(0, 0)])
         gather_words(2, 0, 1, "w2_bf0_0")
         prepare_w2([raw_first[1][:, :, 0:P]], [(1, 0)])
         prepare_w2([raw_first[2][:, :, 0:P]], [(2, 0)])
         gather_words(2, 1, 2, "w2_bf2_0")
-        prepare_w2([raw_first[a][:, :, P : 2 * P] for a in (1, 2)], [(1, 1), (2, 1)])
+        second_codes = held([P, PASSES * P], U32, "second_codes", "tab2")
+        prepare_w2([raw_first[a][:, :, P : 2 * P] for a in (0, 1)], [(0, 1), (1, 1)], codes=second_codes[:, 0 : 2 * P])
+        prepare_w2([raw_first[2][:, :, P : 2 * P]], [(2, 1)], codes=second_codes[:, 2 * P : 3 * P])
 
         units = [(0, 0), (1, 0), (0, 1), (1, 1), (2, 0), (3, 0), (2, 1), (3, 1)]
 
@@ -190,7 +197,7 @@ def tile_list_pipeline_stage_transfer_kernel(
                 plane = v_s[:, cols] if a == 0 else v_s_down[:, (a - 1) * S + half * BANK : (a - 1) * S + (half + 1) * BANK]
                 nc.tensor.matmul_mx(
                     out=acc_a[:],
-                    lhsT=w1c[:, a, 2 * u * P : 2 * (u + 1) * P].bitcast(FP4X4),
+                    lhsT=w1c[u // 2][:, a, 2 * (u % 2) * P : 2 * (u % 2 + 1) * P].bitcast(FP4X4),
                     lhsT_scale=w1s[:, a, u * P : (u + 1) * P],
                     rhs=v[(a, half)].bitcast(FP8X4),
                     rhs_scale=plane,
@@ -243,15 +250,17 @@ def tile_list_pipeline_stage_transfer_kernel(
         acc_a, acc_b = make_h(0)
         gel = held([P, BANK], F32, "gel_first")
         h_first = held([P, BANK], F32, "h_first")
-        sent = held([P, BANK], F32, "sent_first")
+        sent = held([P, CHUNK], F32, "sent_first")
         pieces = [slice(lo, lo + CHUNK) for lo in (0, CHUNK)]
         for cols in pieces:
             nc.scalar.activation(out=gel[:, cols], in_=acc_b[:, cols], func=ACT.Gelu_apprx_tanh, bias=bias[:, 0:1])
         for cols in pieces:
             nc.vector.tensor_tensor(out=h_first[:, cols], in0=acc_a[:, cols], in1=gel[:, cols], op=ALU.add)
-        for cols in pieces:
-            nc.vector.tensor_tensor(out=sent[:, cols], in0=h_first[:, cols], in1=wg[0][:, cols], op=ALU.mult)
-        scatter(0, 0, sent[:])
+        nc.vector.tensor_tensor(
+            out=pages[0][:].indirect(idx2[:, 0 : CHUNK // 16]), in0=h_first[:, pieces[0]], in1=wg[0][:, pieces[0]], op=ALU.mult
+        )
+        nc.vector.tensor_tensor(out=sent[:], in0=h_first[:, pieces[1]], in1=wg[0][:, pieces[1]], op=ALU.mult)
+        scatter(0, CHUNK, sent[:])
 
         gates = {}
         for n in range(1, len(units)):
@@ -346,7 +355,7 @@ def tile_list_pipeline_stage_transfer_kernel(
         def make_z(c, backs):
             return quantize_z(c, multiply(c, backs))
 
-        out_banks = [(0, 1, 4, 5, 6, 7), (2, 3, 4, 5, 6, 7), (0, 1, 4, 5, 6, 7), (2, 3, 4, 5, 6, 7)]
+        out_banks = [(0, 1, 4, 5, 6, 7), (2, 3, 4, 5, 6, 7), (0, 1, 4, 5, 6, 7), (2, 3, 0, 1, 4, 5)]
 
         def send_bank(c, n, zq, copy):
             zc, zs = zq

@@ -64,7 +64,6 @@ def tile_list_pipeline_stage_transfer_kernel(
         w3s = held([P, N_OUT], U8, "w3s")
         ident = held([P, P], F32, "ident")
         bias_rows = held([P, P], F32, "bias_rows")
-        warm_out = held([P, 1], F32, "warm_out")
 
         nc.vector.memset(tab_s[:].bitcast(I32), 0)
         nc.vector.memset(bias_rows[:], 0.0)
@@ -72,7 +71,6 @@ def tile_list_pipeline_stage_transfer_kernel(
         nc.vector.memset(v_s_down[:].bitcast(I32), 0)
         nc.vector.memset(w3s[:].bitcast(I32), 0)
         make_identity(nc, ident[:])
-        nc.scalar.activation(out=warm_out[:], in_=ident[:, 0:1], func=ACT.Gelu_apprx_tanh)
 
         pages = []
 

@@ -29,7 +29,6 @@ SIDES = CHUNK // P
 BLOCKS = N_OUT // P
 PER_BANK = BANK // CHUNK
 BANKS_A_CHUNK = BLOCKS // PER_BANK
-WARM_PASSES = 5
 
 
 def tile_list_pipeline_stage_transfer_kernel(
@@ -306,20 +305,6 @@ def tile_list_pipeline_stage_transfer_kernel(
                 fetch_and_turn(0, 2, PAGES - 1, "sent_before_last")
                 for side in range(SIDES):
                     sigmoid(gates[(0, side)], 0, side, 2, PAGES - 1)
-                warm_acc = [
-                    psum.tile([P, BANK], F32, name="warm_acc", tag="bank%d" % (turn_banks[1] + side))
-                    for side in range(SIDES)
-                ]
-                for repeat in range(WARM_PASSES):
-                    nc.tensor.matmul_mx(
-                        out=warm_acc[repeat % SIDES][:],
-                        lhsT=w2q[(0, 0)][0].bitcast(FP8X4),
-                        lhsT_scale=w2q[(0, 0)][1],
-                        rhs=v[(0, 0)].bitcast(FP8X4),
-                        rhs_scale=v_s[:, 0:BANK],
-                        start=True,
-                        stop=True,
-                    )
             scatter(u, half * BANK, sent)
             if n == 3:
                 x_early = fetch(0, 0, 2)

@@ -58,7 +58,7 @@ def tile_list_pipeline_stage_transfer_kernel(
         w1s = held([P, PASSES, H], U8, "w1s")
         bias = held([P, PAGES], F32, "bias")
         wg = [held([P, BANK], F32, "wg%d" % half) for half in range(2)]
-        skips = [held([P, PACK, CHUNK], F32, "skip%d" % c) for c in range(CHUNKS)]
+        skips = [held([P, M_OUT], F32, "skip%d" % u) for u in range(PAGES)]
         w3c = held([P, N_OUT], U32, "w3c")
         w3s = held([P, N_OUT], U8, "w3s")
         ident = held([P, P], F32, "ident")
@@ -154,9 +154,8 @@ def tile_list_pipeline_stage_transfer_kernel(
         load_w1(1)
         nc.sync.dma_start(out=wg[1][:], in_=wgs[:, BANK:S])
         nc.sync.dma_start(idx3[:], offs3)
-        skip_rows = skip.rearrange("(p t) m -> p t m", t=PACK)
-        for c in range(CHUNKS):
-            nc.sync.dma_start(out=skips[c][:], in_=skip_rows[:, :, c * CHUNK : (c + 1) * CHUNK])
+        for u in range(PAGES):
+            nc.sync.dma_start(out=skips[u][:], in_=skip[u * P : (u + 1) * P, :])
         nc.sync.dma_start(out=w3c[:].bitcast(I32), in_=w3_words[0].rearrange("p c i -> p (c i)").bitcast(I32))
         load_scales(4 * [on_sync], w3s, 4, lambda lo, hi: w3_scales[0, lo:hi, :])
 
@@ -212,37 +211,55 @@ def tile_list_pipeline_stage_transfer_kernel(
             nc.gpsimd.tensor_tensor(out=h[:], in0=lin, in1=gel, op=ALU.add)
             nc.gpsimd.tensor_tensor(out=sent, in0=h[:], in1=weight, op=ALU.mult)
 
-        def pick(c, u, target):
-            slots = idx3[:, c * CHUNK // 16 : (c + 1) * CHUNK // 16]
-            nc.vector.tensor_copy(out=target, in_=pages[u][:].indirect(slots))
+        x = {}
 
-        turned = {}
+        def fetch(keys, tag=None):
+            room = held([P, len(keys), CHUNK], F32, "x%d_%d" % keys[0], tag)
+            for n, (c, u) in enumerate(keys):
+                slots = idx3[:, c * CHUNK // 16 : (c + 1) * CHUNK // 16]
+                nc.vector.tensor_copy(out=room[:, n, :], in_=pages[u][:].indirect(slots))
+                x[(c, u)] = room[:, n, :]
+
         turn_banks = (0, 2)
+        turned = {}
+        gates = {}
+        skip_t = {}
+        z_t = {}
 
-        def turn_in(c, u, x):
+        def by_pairs(rows):
+            return rows.rearrange("m (p h e) -> m h p e", h=2, e=2)
+
+        def turn_skip(c, side):
+            bank = psum.tile([P, H], F32, name="skip_turned", tag="bank%d" % (4 + (SIDES * c + side) % 4))
+            entries = slice(c * CHUNK + side * P, c * CHUNK + (side + 1) * P)
+            for u in range(PAGES):
+                nc.tensor.transpose(bank[:, u * P : (u + 1) * P], skips[u][:, entries], ident[:])
+            skip_t[(c, side)] = held([P, 2, H // 2], F32, "skip_t%d_%d" % (c, side))
+            nc.scalar.copy(out=skip_t[(c, side)][:].rearrange("m h (p e) -> m h p e", e=2), in_=by_pairs(bank[:]))
+
+        def gate(c, lo, hi, first_bank=None):
             for side in range(SIDES):
-                if (c, side) not in turned:
-                    turned[(c, side)] = psum.tile([P, H], F32, name="turned", tag="bank%d" % (turn_banks[c % 2] + side))
-                nc.tensor.transpose(turned[(c, side)][:, u * P : (u + 1) * P], x[:, side * P : (side + 1) * P], ident[:])
-
-        def fetch(c, lo, hi, tag=None):
-            x = held([P, hi - lo, CHUNK], F32, "x%d_%d" % (c, lo), tag)
+                if first_bank is not None:
+                    turned[(c, side)] = psum.tile([P, H], F32, name="turned", tag="bank%d" % (first_bank + side))
+                if lo == 0:
+                    gates[(c, side)] = pair.tile([P, 2, H // 2], F32, name="gate%d" % side)
+                    z_t[(c, side)] = pair.tile([P, 2, H // 2], BF16, name="z_t%d" % side, align_bytes=64)
             for u in range(lo, hi):
-                pick(c, u, x[:, u - lo, :])
-            return x
-
-        def fetch_and_turn(c, lo, hi, tag=None):
-            x = fetch(c, lo, hi, tag)
-            for u in range(lo, hi):
-                turn_in(c, u, x[:, u - lo, :])
-
-        def sigmoid(gate, c, side, lo, hi):
-            rows = P // PACK
-            nc.scalar.activation(
-                out=gate[:, :, lo * rows : hi * rows],
-                in_=turned[(c, side)][:, lo * P : hi * P].rearrange("m (q t) -> m t q", t=PACK),
-                func=ACT.Sigmoid,
-            )
+                for side in range(SIDES):
+                    nc.tensor.transpose(
+                        turned[(c, side)][:, u * P : (u + 1) * P], x[(c, u)][:, side * P : (side + 1) * P], ident[:]
+                    )
+            part = slice(lo * P // 2, hi * P // 2)
+            for side in range(SIDES):
+                nc.scalar.activation(
+                    out=gates[(c, side)][:, :, part].rearrange("m h (p e) -> m h p e", e=2),
+                    in_=by_pairs(turned[(c, side)][:, lo * P : hi * P]),
+                    func=ACT.Sigmoid,
+                )
+            for side in range(SIDES):
+                nc.gpsimd.tensor_tensor(
+                    out=z_t[(c, side)][:, :, part], in0=gates[(c, side)][:, :, part], in1=skip_t[(c, side)][:, :, part], op=ALU.mult
+                )
 
         acc_a, acc_b = make_h(0)
         gel = held([P, BANK], F32, "gel_first")
@@ -259,7 +276,6 @@ def tile_list_pipeline_stage_transfer_kernel(
         nc.vector.tensor_tensor(out=sent[:], in0=h_first[:, pieces[1]], in1=wg[0][:, pieces[1]], op=ALU.mult)
         scatter(0, CHUNK, sent[:])
 
-        gates = {}
         for n in range(1, len(units)):
             u, half = units[n]
             last = n == len(units) - 1
@@ -287,128 +303,89 @@ def tile_list_pipeline_stage_transfer_kernel(
                 prepare_w2(parts[0:4], late[0:4], "gel_first", late_codes[:, 0 : 4 * P])
                 prepare_w2(parts[4:6], late[4:6], "h_first", late_codes[:, 4 * P : 6 * P])
             if last:
-                for side in range(SIDES):
-                    turned[(0, side)] = psum.tile([P, H], F32, name="turned", tag="bank%d" % (turn_banks[1] + side))
-                for early in range(2):
-                    turn_in(0, early, x_early[:, early, :])
-                gates[(0, 0)] = held([P, PACK, P], F32, "gate0_0", "gel_last")
-                gates[(0, 1)] = held([P, PACK, P], F32, "gate0_1")
-                for side in range(SIDES):
-                    sigmoid(gates[(0, side)], 0, side, 0, 2)
-                for side, spent in enumerate(("lin_last", "h")):
-                    turned[(1, side)] = psum.tile([P, H], F32, name="turned", tag="bank%d" % (turn_banks[0] + side))
-                    gates[(1, side)] = held([P, PACK, P], F32, "gate1_%d" % side, spent)
-                for early in range(2):
-                    turn_in(1, early, x_next[:, early, :])
-                for side in range(SIDES):
-                    sigmoid(gates[(1, side)], 1, side, 0, 2)
-                fetch_and_turn(0, 2, PAGES - 1, "sent_before_last")
-                for side in range(SIDES):
-                    sigmoid(gates[(0, side)], 0, side, 2, PAGES - 1)
+                for c in range(CHUNKS):
+                    for side in range(SIDES):
+                        turn_skip(c, side)
+                gate(0, 0, 2, 2)
+                gate(1, 0, 2, 0)
+                fetch([(0, 2)], "sent_before_last")
+                gate(0, 2, 3)
             scatter(u, half * BANK, sent)
             if n == 3:
-                x_early = fetch(0, 0, 2)
-                x_next = fetch(1, 0, 2)
+                fetch([(0, 0), (0, 1)])
+                fetch([(1, 0), (1, 1)])
 
         out_rows = out.rearrange("(b p) m -> p b m", p=P)
+        zq = {}
 
-        def turn_back(c, side):
-            back = psum.tile([P, PACK, P], F32, name="back", tag="bank%d" % (turn_banks[c % 2] + side))
-            for t in range(PACK):
-                nc.tensor.transpose(back[:, t, :], gates[(c, side)][:, t, :], ident[:])
-            return back
-
-        def multiply(c, backs):
-            z = held([P, CHUNK * PACK], BF16, "z%d" % c)
+        def turn_back(c):
+            backs = []
             for side in range(SIDES):
-                nc.vector.tensor_tensor(
-                    out=z[:, side * BANK : (side + 1) * BANK].rearrange("p (n i t) -> p n t i", i=2, t=PACK),
-                    in0=backs[side][:].rearrange("p t (n i) -> p n t i", i=2),
-                    in1=skips[c][:, :, side * P : (side + 1) * P].rearrange("p t (n i) -> p n t i", i=2),
-                    op=ALU.mult,
-                )
-            return z
+                back = psum.tile([P, 2, P], F32, name="back", tag="bank%d" % (turn_banks[c % 2] + side))
+                backs.append(back)
+                words = z_t[(c, side)][:].rearrange("m h f -> m (h f)").bitcast(F32)
+                for h in range(2):
+                    nc.tensor.transpose(back[:, h, :], words[:, h * P : (h + 1) * P], ident[:])
+            return backs
 
-        def quantize_z(c, z):
+        def make_z(c, backs):
+            z = held([P, CHUNK * PACK], BF16, "z%d" % c)
+            words = z[:].bitcast(F32).rearrange("p (s m h) -> p s m h", s=SIDES, h=2)
+            for side in range(SIDES):
+                nc.vector.tensor_copy(out=words[:, side], in_=backs[side][:].rearrange("p h m -> p m h"))
             zc = held([P, CHUNK], U32, "zc%d" % c)
             zs = held([P, CHUNK], U8, "zs%d" % c)
             nc.vector.quantize_mx(out=zc[:].bitcast(FP8X4), scales=zs[:], in_=z[:])
-            return zc, zs
+            zq[c] = (zc, zs)
 
-        def make_z(c, backs):
-            return quantize_z(c, multiply(c, backs))
+        out_banks = [(4, 5, 6, 7, 4, 5), (6, 7, 4, 5, 6, 7), (0, 1, 4, 5, 6, 7), (2, 3, 0, 1, 4, 5)]
 
-        out_banks = [(0, 1, 4, 5, 6, 7), (2, 3, 4, 5, 6, 7), (0, 1, 4, 5, 6, 7), (2, 3, 0, 1, 4, 5)]
-
-        def send_bank(c, n, zq, copy):
-            zc, zs = zq
-            bank = out_banks[c][n]
-            acc = psum.tile([P, PER_BANK, CHUNK], F32, name="acc", tag="bank%d" % bank)
-            for e in range(PER_BANK):
-                b = n * PER_BANK + e
-                nc.tensor.matmul_mx(
-                    out=acc[:, e, :],
-                    lhsT=w3c[:, b * P : (b + 1) * P].bitcast(FP8X4),
-                    lhsT_scale=w3s[:, b * P : (b + 1) * P],
-                    rhs=zc[:].bitcast(FP8X4),
-                    rhs_scale=zs[:],
-                    start=True,
-                    stop=True,
-                )
-            staged = stage.tile([P, PER_BANK, CHUNK], F32, name="staged")
-            copy(out=staged[:], in_=acc[:])
-            nc.sync.dma_start(
-                out=out_rows[:, n * PER_BANK : (n + 1) * PER_BANK, c * CHUNK : (c + 1) * CHUNK], in_=staged[:]
-            )
-
-        def gate_and_turn(c):
-            for side in range(SIDES):
-                gates[(c, side)] = pair.tile([P, PACK, P], F32, name="gate")
-                sigmoid(gates[(c, side)], c, side, 0, PAGES)
-            return [turn_back(c, side) for side in range(SIDES)]
-
-        def send(c, lo, hi, zq, on_vector):
+        def send(c, lo, hi, on_vector=()):
+            zc, zs = zq[c]
             for n in range(lo, hi):
-                send_bank(c, n, zq, nc.vector.tensor_copy if n in on_vector else nc.scalar.copy)
+                bank = out_banks[c][n]
+                acc = psum.tile([P, PER_BANK, CHUNK], F32, name="acc", tag="bank%d" % bank)
+                for e in range(PER_BANK):
+                    b = n * PER_BANK + e
+                    nc.tensor.matmul_mx(
+                        out=acc[:, e, :],
+                        lhsT=w3c[:, b * P : (b + 1) * P].bitcast(FP8X4),
+                        lhsT_scale=w3s[:, b * P : (b + 1) * P],
+                        rhs=zc[:].bitcast(FP8X4),
+                        rhs_scale=zs[:],
+                        start=True,
+                        stop=True,
+                    )
+                staged = stage.tile([P, PER_BANK, CHUNK], F32, name="staged")
+                copy = nc.vector.tensor_copy if n in on_vector else nc.scalar.copy
+                copy(out=staged[:], in_=acc[:])
+                nc.sync.dma_start(
+                    out=out_rows[:, n * PER_BANK : (n + 1) * PER_BANK, c * CHUNK : (c + 1) * CHUNK], in_=staged[:]
+                )
 
-        def turn_all(c, parts):
-            for u in range(PAGES):
-                turn_in(c, u, parts[u])
-
-        x_last = fetch(0, PAGES - 1, PAGES)
-        for side in range(SIDES):
-            turned[(0, side)] = psum.tile([P, H], F32, name="turned", tag="bank%d" % (turn_banks[1] + side))
-        turn_in(0, PAGES - 1, x_last[:, 0, :])
-        for side in range(SIDES):
-            sigmoid(gates[(0, side)], 0, side, PAGES - 1, PAGES)
-        backs0 = [turn_back(0, side) for side in range(SIDES)]
-        for side in range(SIDES):
-            turned[(1, side)] = psum.tile([P, H], F32, name="turned", tag="bank%d" % (turn_banks[1] + side))
-        fetch_and_turn(1, 2, PAGES, "sent_last")
-        for side in range(SIDES):
-            sigmoid(gates[(1, side)], 1, side, 2, PAGES)
-        x2 = held([P, 2, CHUNK], F32, "x2_first", "x0_3")
-        pick(2, 0, x2[:, 0, :])
-        pick(2, 1, x2[:, 1, :])
-        zq0 = make_z(0, backs0)
-        backs1 = [turn_back(1, side) for side in range(SIDES)]
-        x2 = [x2[:, 0, :], x2[:, 1, :], fetch(2, 2, 3, "skip0")[:, 0, :], fetch(2, 3, 4, "z0")[:, 0, :]]
-        send(0, 0, 2, zq0, ())
-        turn_all(2, x2)
-        backs2 = gate_and_turn(2)
-        z1 = multiply(1, backs1)
-        send(0, 2, BANKS_A_CHUNK, zq0, (2,))
-        x3 = [fetch(3, 0, 1, "skip1")[:, 0, :]]
-        zq1 = quantize_z(1, z1)
-        x = held([P, 3, CHUNK], F32, "x_late", "z1")
-        for u in range(1, PAGES):
-            pick(3, u, x[:, u - 1, :])
-            x3.append(x[:, u - 1, :])
-        zq2 = make_z(2, backs2)
-        send(1, 0, 2, zq1, ())
-        turn_all(3, x3)
-        backs3 = gate_and_turn(3)
-        zq3 = make_z(3, backs3)
-        send(1, 2, BANKS_A_CHUNK, zq1, (3, 4, 5))
-        send(2, 0, BANKS_A_CHUNK, zq2, (5,))
-        send(3, 0, BANKS_A_CHUNK, zq3, (0, 2, 4))
+        fetch([(0, 3)])
+        fetch([(1, 2), (1, 3), (2, 0), (2, 1)], "sent_last")
+        gate(0, 3, 4)
+        back = turn_back(0)
+        gate(1, 2, 4, 2)
+        make_z(0, back)
+        fetch([(2, 2), (2, 3), (3, 0), (3, 1)], "z0")
+        gate(2, 0, 2, 0)
+        send(0, 0, 2)
+        back = turn_back(1)
+        gate(2, 2, 4)
+        send(0, 2, 4)
+        make_z(1, back)
+        fetch([(3, 2), (3, 3)], "z1")
+        send(0, 4, 6)
+        gate(3, 0, 2, 2)
+        send(1, 0, 2, (1,))
+        back = turn_back(2)
+        gate(3, 2, 4)
+        make_z(2, back)
+        send(1, 2, 6, (3, 5))
+        back = turn_back(3)
+        send(2, 0, 2, (1,))
+        make_z(3, back)
+        send(2, 2, 6, (3, 5))
+        send(3, 0, BANKS_A_CHUNK, (1, 3, 5))

@@ -73,14 +73,14 @@ def tile_list_pipeline_stage_transfer_kernel(
 
         pages = []
 
-        def clear_page(tag=None):
+        def clear_page(engine, piece, tag=None):
             page = held([P, T2], F32, "page%d" % len(pages), tag)
-            for lo in range(0, T2, BANK):
-                nc.gpsimd.memset(page[:, lo : lo + BANK], 0.0)
+            for lo in range(0, T2, piece):
+                engine.memset(page[:, lo : lo + piece], 0.0)
             pages.append(page)
 
-        for u in range(PAGES):
-            clear_page()
+        for u in range(2):
+            clear_page(nc.vector, T2)
 
         def load_tab(a):
             nc.sync.dma_start(out=tab[a][:].bitcast(I32), in_=tab_words[a].rearrange("p t i -> p (t i)").bitcast(I32))
@@ -171,6 +171,9 @@ def tile_list_pipeline_stage_transfer_kernel(
         second_codes = held([P, PASSES * P], U32, "second_codes", "tab2")
         prepare_w2([raw_first[a][:, :, P : 2 * P] for a in (0, 1)], [(0, 1), (1, 1)], codes=second_codes[:, 0 : 2 * P])
         prepare_w2([raw_first[2][:, :, P : 2 * P]], [(2, 1)], codes=second_codes[:, 2 * P : 3 * P])
+
+        clear_page(nc.gpsimd, BANK, "w2_bf0_1")
+        clear_page(nc.gpsimd, BANK, "w2_bf2_1")
 
         units = [(0, 0), (1, 0), (0, 1), (1, 1), (2, 0), (3, 0), (2, 1), (3, 1)]
 

@@ -173,7 +173,6 @@ def tile_list_pipeline_stage_transfer_kernel(
         prepare_w2([raw_first[2][:, :, P : 2 * P]], [(2, 1)], codes=second_codes[:, 2 * P : 3 * P])
 
         clear_page(nc.gpsimd, BANK, "w2_bf0_1")
-        clear_page(nc.gpsimd, BANK, "w2_bf2_1")
 
         units = [(0, 0), (1, 0), (0, 1), (1, 1), (2, 0), (3, 0), (2, 1), (3, 1)]
 
@@ -305,6 +304,7 @@ def tile_list_pipeline_stage_transfer_kernel(
                 late_codes = held([P, len(late) * P], U32, "late_codes", "sent_third")
                 prepare_w2(parts[0:4], late[0:4], "gel_first", late_codes[:, 0 : 4 * P])
                 prepare_w2(parts[4:6], late[4:6], "h_first", late_codes[:, 4 * P : 6 * P])
+                clear_page(nc.gpsimd, BANK, "h_first")
             if last:
                 for c in range(CHUNKS):
                     for side in range(SIDES):

@@ -266,17 +266,15 @@ def tile_list_pipeline_stage_transfer_kernel(
         acc_a, acc_b = make_h(0)
         gel = held([P, BANK], F32, "gel_first")
         h_first = held([P, BANK], F32, "h_first")
-        sent = held([P, CHUNK], F32, "sent_first")
+        sent = held([P, BANK], F32, "sent_first")
         pieces = [slice(lo, lo + CHUNK) for lo in (0, CHUNK)]
         for cols in pieces:
             nc.scalar.activation(out=gel[:, cols], in_=acc_b[:, cols], func=ACT.Gelu_apprx_tanh, bias=bias[:, 0:1])
         for cols in pieces:
             nc.vector.tensor_tensor(out=h_first[:, cols], in0=acc_a[:, cols], in1=gel[:, cols], op=ALU.add)
-        nc.vector.tensor_tensor(
-            out=pages[0][:].indirect(idx2[:, 0 : CHUNK // 16]), in0=h_first[:, pieces[0]], in1=wg[0][:, pieces[0]], op=ALU.mult
-        )
-        nc.vector.tensor_tensor(out=sent[:], in0=h_first[:, pieces[1]], in1=wg[0][:, pieces[1]], op=ALU.mult)
-        scatter(0, CHUNK, sent[:])
+        for cols in pieces:
+            nc.vector.tensor_tensor(out=sent[:, cols], in0=h_first[:, cols], in1=wg[0][:, cols], op=ALU.mult)
+        scatter(0, 0, sent[:])
 
         for n in range(1, len(units)):
             u, half = units[n]

@@ -162,6 +162,7 @@ def tile_list_pipeline_stage_transfer_kernel(
         bias_turned = psum.tile([P, P], F32, name="bias_turned", tag="bank7")
         nc.tensor.transpose(bias_turned[:], bias_rows[:], ident[:])
         nc.scalar.copy(out=bias[:], in_=bias_turned[:, 0:PAGES])
+        clear_page(nc.gpsimd, BANK, "bias_rows")
         gather_words(1, 0, 2, "tab_s")
         prepare_w2([raw_first[0][:, :, 0:P]], [(0, 0)])
         gather_words(2, 0, 1, "w2_bf0_0")
@@ -171,8 +172,6 @@ def tile_list_pipeline_stage_transfer_kernel(
         second_codes = held([P, PASSES * P], U32, "second_codes", "tab2")
         prepare_w2([raw_first[a][:, :, P : 2 * P] for a in (0, 1)], [(0, 1), (1, 1)], codes=second_codes[:, 0 : 2 * P])
         prepare_w2([raw_first[2][:, :, P : 2 * P]], [(2, 1)], codes=second_codes[:, 2 * P : 3 * P])
-
-        clear_page(nc.gpsimd, BANK, "w2_bf0_1")
 
         units = [(0, 0), (1, 0), (0, 1), (1, 1), (2, 0), (3, 0), (2, 1), (3, 1)]
 

@@ -135,12 +135,12 @@ def tile_list_pipeline_stage_transfer_kernel(
         load_tab(0)
         on_sync = nc.sync.dma_start
         load_tab(1)
-        load_scales(4 * [on_sync], tab_s, 4 * PASSES, lambda lo, hi: tab_scales[:, lo:hi, :])
         nc.sync.dma_start(out=bias_rows[0:PAGES, :], in_=b2.rearrange("(u p) -> u p", p=P))
-        load_tab(2)
+        load_scales(4 * [on_sync], tab_s, 4 * PASSES, lambda lo, hi: tab_scales[:, lo:hi, :])
         raw_first = [load_w2(0, 0, 2), load_w2(1, 0, 2)]
         load_scales(4 * [on_sync], w1s, 4, lambda lo, hi: w1_scales[:, lo:hi, :].rearrange("a r c -> r a c"))
         load_w1(0)
+        load_tab(2)
         raw_first.append(load_w2(2, 0, 2))
         gather_words(0, 0, 2)
         nc.vector.tensor_copy(out=v_s[:], in_=tab_s[:].indirect(idx[:]))

from contextlib import ExitStack

import concourse.mybir as mybir
from concourse.masks import make_identity

K, T, S, H, T2, M_OUT, N_OUT = 1536, 2048, 1024, 512, 2048, 1024, 1536
FLOPS = 2 * (2 * K * H * S + H * N_OUT * M_OUT)

F32 = mybir.dt.float32
BF16 = mybir.dt.bfloat16
I32 = mybir.dt.int32
U32 = mybir.dt.uint32
U16 = mybir.dt.uint16
U8 = mybir.dt.uint8
FP8X4 = mybir.dt.float8_e4m3fn_x4
FP4X4 = mybir.dt.float4_e2m1fn_x4
ACT = mybir.ActivationFunctionType
ALU = mybir.AluOpType

P = 128
PACK = 4
PASSES = K // (P * PACK)
QUADS = 4
PAGES = H // P
BANK = 512
CHUNK = 256
CHUNKS = M_OUT // CHUNK
SIDES = CHUNK // P
BLOCKS = N_OUT // P
PER_BANK = BANK // CHUNK
BANKS_A_CHUNK = BLOCKS // PER_BANK


def tile_list_pipeline_stage_transfer_kernel(
    tc, tab_words, tab_scales, offs, w1_words, w1_scales, w2, b2, wgs, offs2, offs3, skip, w3_words, w3_scales, out
):
    nc = tc.nc
    with ExitStack() as ctx:
        lists = ctx.enter_context(tc.tile_pool(name="lists", bufs=1))
        keep = ctx.enter_context(tc.tile_pool(name="keep", bufs=1))
        pair = ctx.enter_context(tc.tile_pool(name="pair", bufs=2))
        ring = ctx.enter_context(tc.tile_pool(name="ring", bufs=3))
        stage = ctx.enter_context(tc.tile_pool(name="stage", bufs=8))
        psum = ctx.enter_context(tc.psum_pool(name="psum", bufs=1))

        def held(shape, dtype, name, tag=None):
            return keep.tile(shape, dtype, name=name, tag=tag or name, align_bytes=64)

        idx = lists.tile([P, S // 16], U16, name="idx")
        idx2 = lists.tile([P, S // 16], U16, name="idx2")
        idx3 = lists.tile([P, M_OUT // 16], U16, name="idx3")

        tab = [held([P, T], U32, "tab%d" % a) for a in range(PASSES)]
        tab_s = held([P, T], U8, "tab_s")
        v_s = held([P, S], U8, "v_s")
        v_s_down = held([P, (PASSES - 1) * S], U8, "v_s_down")
        w1c = [held([P, PASSES, H], U8, "w1c%d" % part) for part in range(2)]
        w1s = held([P, PASSES, H], U8, "w1s")
        bias = held([P, PAGES], F32, "bias")
        wg = [held([P, BANK], F32, "wg%d" % half) for half in range(2)]
        skips = [held([P, M_OUT], F32, "skip%d" % u) for u in range(PAGES)]
        w3c = held([P, N_OUT], U32, "w3c")
        w3s = held([P, N_OUT], U8, "w3s")
        ident = held([P, P], F32, "ident")
        bias_rows = held([P, P], F32, "bias_rows")

        nc.vector.memset(tab_s[:].bitcast(I32), 0)
        nc.vector.memset(bias_rows[:], 0.0)
        nc.vector.memset(w1s[:].bitcast(I32), 0)
        nc.vector.memset(v_s_down[:].bitcast(I32), 0)
        nc.vector.memset(w3s[:].bitcast(I32), 0)
        make_identity(nc, ident[:])

        pages = []

        def clear_page(engine, piece, tag=None):
            page = held([P, T2], F32, "page%d" % len(pages), tag)
            for lo in range(0, T2, piece):
                engine.memset(page[:, lo : lo + piece], 0.0)
            pages.append(page)

        for u in range(2):
            clear_page(nc.vector, T2)

        def load_tab(a):
            nc.sync.dma_start(out=tab[a][:].bitcast(I32), in_=tab_words[a].rearrange("p t i -> p (t i)").bitcast(I32))

        def load_w2(a, lo, hi):
            raw = held([P, PACK, (hi - lo) * P], F32, "w2_raw%d_%d" % (a, lo))
            rows = w2[a * P * PACK : (a + 1) * P * PACK, lo * P : hi * P]
            nc.sync.dma_start(out=raw[:], in_=rows.rearrange("(p j) c -> p j c", j=PACK))
            return raw

        def load_w1(part):
            words = w1_words.rearrange("a p c -> p a c")[:, :, part * H : (part + 1) * H]
            nc.sync.dma_start(out=w1c[part][:].bitcast(I32), in_=words.bitcast(I32))

        def load_scales(queues, plane, rows, scales):
            for q, queue in enumerate(queues):
                queue(out=plane[32 * q : 32 * q + rows].bitcast(I32), in_=scales(4 * q, 4 * q + 4).bitcast(I32))

        v = {}

        def gather_words(a, lo, hi, tag=None):
            words = held([P, (hi - lo) * BANK], U32, "v%d_%d" % (a, lo), tag)
            nc.vector.tensor_copy(out=words[:], in_=tab[a][:].indirect(idx[:, lo * BANK // 16 : hi * BANK // 16]))
            for half in range(lo, hi):
                v[(a, half)] = words[:, (half - lo) * BANK : (half - lo + 1) * BANK]

        def cast_w2(raw, target):
            nc.scalar.copy(
                out=target.rearrange("p (c i j) -> p c j i", i=4, j=PACK),
                in_=raw.rearrange("p j (c i) -> p c j i", i=4),
            )

        w2q = {}

        def quantize_w2(grouped, keys, codes=None):
            name = "%d_%d" % keys[0]
            if codes is None:
                codes = held([P, len(keys) * P], U32, "w2c" + name)[:]
            scales = held([P, len(keys) * P], U8, "w2s" + name)
            nc.vector.quantize_mx(out=codes.bitcast(FP8X4), scales=scales[:], in_=grouped[:])
            for n, key in enumerate(keys):
                w2q[key] = (codes[:, n * P : (n + 1) * P], scales[:, n * P : (n + 1) * P])

        def prepare_w2(raws, keys, tag=None, codes=None):
            grouped = held([P, len(keys) * P * PACK], BF16, "w2_bf%d_%d" % keys[0], tag)
            width = len(keys) * P * PACK // len(raws)
            for n, raw in enumerate(raws):
                cast_w2(raw, grouped[:, n * width : (n + 1) * width])
            quantize_w2(grouped, keys, codes)

        nc.sync.dma_start(idx[:], offs)
        load_tab(0)
        on_sync = nc.sync.dma_start
        load_tab(1)
        nc.sync.dma_start(out=bias_rows[0:PAGES, :], in_=b2.rearrange("(u p) -> u p", p=P))
        load_scales(4 * [on_sync], tab_s, 4 * PASSES, lambda lo, hi: tab_scales[:, lo:hi, :])
        raw_first = [load_w2(0, 0, 2), load_w2(1, 0, 2)]
        load_scales(4 * [on_sync], w1s, 4, lambda lo, hi: w1_scales[:, lo:hi, :].rearrange("a r c -> r a c"))
        load_w1(0)
        load_tab(2)
        raw_first.append(load_w2(2, 0, 2))
        gather_words(0, 0, 2)
        nc.vector.tensor_copy(out=v_s[:], in_=tab_s[:].indirect(idx[:]))
        for a in range(1, PASSES):
            nc.sync.dma_start(
                out=v_s_down[0:112, (a - 1) * S : a * S].bitcast(I32), in_=v_s[4 * a : 4 * a + 112, :].bitcast(I32)
            )
        nc.sync.dma_start(out=wg[0][:], in_=wgs[:, 0:BANK])
        nc.sync.dma_start(idx2[:], offs2)
        raw_second = [load_w2(a, 2, 4) for a in range(PASSES)]
        load_w1(1)
        nc.sync.dma_start(out=wg[1][:], in_=wgs[:, BANK:S])
        nc.sync.dma_start(idx3[:], offs3)
        for u in range(PAGES):
            nc.sync.dma_start(out=skips[u][:], in_=skip[u * P : (u + 1) * P, :])
        nc.sync.dma_start(out=w3c[:].bitcast(I32), in_=w3_words[0].rearrange("p c i -> p (c i)").bitcast(I32))
        load_scales(4 * [on_sync], w3s, 4, lambda lo, hi: w3_scales[0, lo:hi, :])

        bias_turned = psum.tile([P, P], F32, name="bias_turned", tag="bank7")
        nc.tensor.transpose(bias_turned[:], bias_rows[:], ident[:])
        nc.scalar.copy(out=bias[:], in_=bias_turned[:, 0:PAGES])
        clear_page(nc.gpsimd, BANK, "bias_rows")
        gather_words(1, 0, 2, "tab_s")
        prepare_w2([raw_first[0][:, :, 0:P]], [(0, 0)])
        gather_words(2, 0, 1, "w2_bf0_0")
        prepare_w2([raw_first[1][:, :, 0:P]], [(1, 0)])
        prepare_w2([raw_first[2][:, :, 0:P]], [(2, 0)])
        gather_words(2, 1, 2, "w2_bf2_0")
        second_codes = held([P, PASSES * P], U32, "second_codes", "tab2")
        prepare_w2([raw_first[a][:, :, P : 2 * P] for a in (0, 1)], [(0, 1), (1, 1)], codes=second_codes[:, 0 : 2 * P])
        prepare_w2([raw_first[2][:, :, P : 2 * P]], [(2, 1)], codes=second_codes[:, 2 * P : 3 * P])

        units = [(0, 0), (1, 0), (0, 1), (1, 1), (2, 0), (3, 0), (2, 1), (3, 1)]

        def make_h(n):
            u, half = units[n]
            cols = slice(half * BANK, (half + 1) * BANK)
            acc_b = psum.tile([P, BANK], F32, name="acc_b", tag="bank%d" % (2 * n % 4))
            acc_a = psum.tile([P, BANK], F32, name="acc_a", tag="bank%d" % (2 * n % 4 + 1))
            for a in range(PASSES):
                nc.tensor.matmul_mx(
                    out=acc_b[:],
                    lhsT=w2q[(a, u)][0].bitcast(FP8X4),
                    lhsT_scale=w2q[(a, u)][1],
                    rhs=v[(a, half)].bitcast(FP8X4),
                    rhs_scale=v_s[4 * a : P, cols],
                    start=(a == 0),
                    stop=(a == PASSES - 1),
                )
            for a in range(PASSES):
                plane = v_s[:, cols] if a == 0 else v_s_down[:, (a - 1) * S + half * BANK : (a - 1) * S + (half + 1) * BANK]
                nc.tensor.matmul_mx(
                    out=acc_a[:],
                    lhsT=w1c[u // 2][:, a, 2 * (u % 2) * P : 2 * (u % 2 + 1) * P].bitcast(FP4X4),
                    lhsT_scale=w1s[:, a, u * P : (u + 1) * P],
                    rhs=v[(a, half)].bitcast(FP8X4),
                    rhs_scale=plane,
                    start=(a == 0),
                    stop=(a == PASSES - 1),
                )
            return acc_a, acc_b

        def scatter(u, lo, values):
            width = values.shape[1]
            nc.vector.tensor_copy(out=pages[u][:].indirect(idx2[:, lo // 16 : (lo + width) // 16]), in_=values)

        def weigh_on_gpsimd(lin, gel, weight, sent):
            h = held([P, lin.shape[1]], F32, "h")
            nc.gpsimd.tensor_tensor(out=h[:], in0=lin, in1=gel, op=ALU.add)
            nc.gpsimd.tensor_tensor(out=sent, in0=h[:], in1=weight, op=ALU.mult)

        x = {}

        def fetch(keys, tag=None):
            room = held([P, len(keys), CHUNK], F32, "x%d_%d" % keys[0], tag)
            for n, (c, u) in enumerate(keys):
                slots = idx3[:, c * CHUNK // 16 : (c + 1) * CHUNK // 16]
                nc.vector.tensor_copy(out=room[:, n, :], in_=pages[u][:].indirect(slots))
                x[(c, u)] = room[:, n, :]

        turn_banks = (0, 2)
        turned = {}
        gates = {}
        skip_t = {}
        z_t = {}

        def by_pairs(rows):
            return rows.rearrange("m (p h e) -> m h p e", h=2, e=2)

        def turn_skip(c, side):
            bank = psum.tile([P, H], F32, name="skip_turned", tag="bank%d" % (4 + (SIDES * c + side) % 4))
            entries = slice(c * CHUNK + side * P, c * CHUNK + (side + 1) * P)
            for u in range(PAGES):
                nc.tensor.transpose(bank[:, u * P : (u + 1) * P], skips[u][:, entries], ident[:])
            skip_t[(c, side)] = held([P, 2, H // 2], F32, "skip_t%d_%d" % (c, side))
            nc.scalar.copy(out=skip_t[(c, side)][:].rearrange("m h (p e) -> m h p e", e=2), in_=by_pairs(bank[:]))

        def gate(c, lo, hi, first_bank=None):
            for side in range(SIDES):
                if first_bank is not None:
                    turned[(c, side)] = psum.tile([P, H], F32, name="turned", tag="bank%d" % (first_bank + side))
                if lo == 0:
                    gates[(c, side)] = pair.tile([P, 2, H // 2], F32, name="gate%d" % side)
                    z_t[(c, side)] = pair.tile([P, 2, H // 2], BF16, name="z_t%d" % side, align_bytes=64)
            for u in range(lo, hi):
                for side in range(SIDES):
                    nc.tensor.transpose(
                        turned[(c, side)][:, u * P : (u + 1) * P], x[(c, u)][:, side * P : (side + 1) * P], ident[:]
                    )
            part = slice(lo * P // 2, hi * P // 2)
            for side in range(SIDES):
                nc.scalar.activation(
                    out=gates[(c, side)][:, :, part].rearrange("m h (p e) -> m h p e", e=2),
                    in_=by_pairs(turned[(c, side)][:, lo * P : hi * P]),
                    func=ACT.Sigmoid,
                )
            for side in range(SIDES):
                nc.gpsimd.tensor_tensor(
                    out=z_t[(c, side)][:, :, part], in0=gates[(c, side)][:, :, part], in1=skip_t[(c, side)][:, :, part], op=ALU.mult
                )

        acc_a, acc_b = make_h(0)
        gel = held([P, BANK], F32, "gel_first")
        h_first = held([P, BANK], F32, "h_first")
        sent = held([P, BANK], F32, "sent_first")
        pieces = [slice(lo, lo + CHUNK) for lo in (0, CHUNK)]
        for cols in pieces:
            nc.scalar.activation(out=gel[:, cols], in_=acc_b[:, cols], func=ACT.Gelu_apprx_tanh, bias=bias[:, 0:1])
        for cols in pieces:
            nc.vector.tensor_tensor(out=h_first[:, cols], in0=acc_a[:, cols], in1=gel[:, cols], op=ALU.add)
        for cols in pieces:
            nc.vector.tensor_tensor(out=sent[:, cols], in0=h_first[:, cols], in1=wg[0][:, cols], op=ALU.mult)
        scatter(0, 0, sent[:])

        for n in range(1, len(units)):
            u, half = units[n]
            last = n == len(units) - 1
            acc_a, acc_b = make_h(n)
            if last:
                gel = held([P, BANK], F32, "gel_last")[:]
            else:
                gel = ring.tile([P, BANK], F32, name="gel")[:]
            nc.scalar.activation(out=gel, in_=acc_b[:], func=ACT.Gelu_apprx_tanh, bias=bias[:, u : u + 1])
            lin = held([P, BANK], F32, "lin_last") if last else pair.tile([P, BANK], F32, name="lin")
            nc.scalar.copy(out=lin[:], in_=acc_a[:])
            if last:
                sent = held([P, BANK], F32, "sent_last")[:]
            elif n == len(units) - 2:
                sent = held([P, BANK], F32, "sent_before_last")[:]
            elif n == 2:
                sent = held([P, BANK], F32, "sent_third")[:]
            else:
                sent = pair.tile([P, BANK], F32, name="sent")[:]
            weigh_on_gpsimd(lin[:], gel, wg[half][:], sent)
            if n == 3:
                late = [(a, u2) for u2 in (2, 3) for a in range(PASSES)]
                parts = [raw_second[a][:, :, (u2 - 2) * P : (u2 - 1) * P] for a, u2 in late]
                late_codes = held([P, len(late) * P], U32, "late_codes", "sent_third")
                prepare_w2(parts[0:4], late[0:4], "gel_first", late_codes[:, 0 : 4 * P])
                prepare_w2(parts[4:6], late[4:6], "h_first", late_codes[:, 4 * P : 6 * P])
                clear_page(nc.gpsimd, BANK, "h_first")
            if last:
                for c in range(CHUNKS):
                    for side in range(SIDES):
                        turn_skip(c, side)
                gate(0, 0, 2, 2)
                gate(1, 0, 2, 0)
                fetch([(0, 2)], "sent_before_last")
                gate(0, 2, 3)
            scatter(u, half * BANK, sent)
            if n == 3:
                fetch([(0, 0), (0, 1)])
                fetch([(1, 0), (1, 1)])

        out_rows = out.rearrange("(b p) m -> p b m", p=P)
        zq = {}

        def turn_back(c):
            backs = []
            for side in range(SIDES):
                back = psum.tile([P, 2, P], F32, name="back", tag="bank%d" % (turn_banks[c % 2] + side))
                backs.append(back)
                words = z_t[(c, side)][:].rearrange("m h f -> m (h f)").bitcast(F32)
                for h in range(2):
                    nc.tensor.transpose(back[:, h, :], words[:, h * P : (h + 1) * P], ident[:])
            return backs

        def make_z(c, backs):
            z = held([P, CHUNK * PACK], BF16, "z%d" % c)
            words = z[:].bitcast(F32).rearrange("p (s m h) -> p s m h", s=SIDES, h=2)
            for side in range(SIDES):
                nc.vector.tensor_copy(out=words[:, side], in_=backs[side][:].rearrange("p h m -> p m h"))
            zc = held([P, CHUNK], U32, "zc%d" % c)
            zs = held([P, CHUNK], U8, "zs%d" % c)
            nc.vector.quantize_mx(out=zc[:].bitcast(FP8X4), scales=zs[:], in_=z[:])
            zq[c] = (zc, zs)

        out_banks = [(4, 5, 6, 7, 4, 5), (6, 7, 4, 5, 6, 7), (0, 1, 4, 5, 6, 7), (2, 3, 0, 1, 4, 5)]

        def send(c, lo, hi, on_vector=()):
            zc, zs = zq[c]
            for n in range(lo, hi):
                bank = out_banks[c][n]
                acc = psum.tile([P, PER_BANK, CHUNK], F32, name="acc", tag="bank%d" % bank)
                for e in range(PER_BANK):
                    b = n * PER_BANK + e
                    nc.tensor.matmul_mx(
                        out=acc[:, e, :],
                        lhsT=w3c[:, b * P : (b + 1) * P].bitcast(FP8X4),
                        lhsT_scale=w3s[:, b * P : (b + 1) * P],
                        rhs=zc[:].bitcast(FP8X4),
                        rhs_scale=zs[:],
                        start=True,
                        stop=True,
                    )
                staged = stage.tile([P, PER_BANK, CHUNK], F32, name="staged")
                copy = nc.vector.tensor_copy if n in on_vector else nc.scalar.copy
                copy(out=staged[:], in_=acc[:])
                nc.sync.dma_start(
                    out=out_rows[:, n * PER_BANK : (n + 1) * PER_BANK, c * CHUNK : (c + 1) * CHUNK], in_=staged[:]
                )

        fetch([(0, 3)])
        fetch([(1, 2), (1, 3), (2, 0), (2, 1)], "sent_last")
        gate(0, 3, 4)
        back = turn_back(0)
        gate(1, 2, 4, 2)
        make_z(0, back)
        fetch([(2, 2), (2, 3), (3, 0), (3, 1)], "z0")
        gate(2, 0, 2, 0)
        send(0, 0, 2)
        back = turn_back(1)
        gate(2, 2, 4)
        send(0, 2, 4)
        make_z(1, back)
        fetch([(3, 2), (3, 3)], "z1")
        send(0, 4, 6)
        gate(3, 0, 2, 2)
        send(1, 0, 2, (1,))
        back = turn_back(2)
        gate(3, 2, 4)
        make_z(2, back)
        send(1, 2, 6, (3, 5))
        back = turn_back(3)
        send(2, 0, 2, (1,))
        make_z(3, back)
        send(2, 2, 6, (3, 5))
        send(3, 0, BANKS_A_CHUNK, (1, 3, 5))
